import numpy as np
import ml_dtypes


def mxq(x, axis, fmt="e4m3"):
    dtype, down = {"e4m3": (ml_dtypes.float8_e4m3fn, 7), "e5m2": (ml_dtypes.float8_e5m2, 14)}[fmt]
    v = np.moveaxis(np.asarray(x, np.float32).astype(ml_dtypes.bfloat16).astype(np.float64), axis, -1)
    blocks = v.reshape(v.shape[:-1] + (-1, 32))
    amax = np.abs(blocks).max(-1, keepdims=True)
    byte = np.maximum(np.where(amax > 0, np.frexp(amax)[1] - 1 + 127, 0) - down, 1)
    scale = np.exp2(byte - 127.0)
    codes = (blocks / scale).astype(np.float32).astype(dtype).astype(np.float64)
    return np.moveaxis((codes * scale).reshape(v.shape), -1, axis)


WIDE = False


def mx_kscale(k):
    if not WIDE:
        return np.ones(k)
    levels = np.array([10, -10, 5, -5, 0])
    if k % 512:
        return np.exp2(np.random.permutation(np.resize(levels, k // 32))).repeat(32)
    a = np.empty((k // 512, 16))
    for p in range(k // 512):
        a[p, :8] = np.random.permutation(np.resize(levels, 8))
        for g in range(8):
            far = levels[np.abs(levels - a[p, g]) >= 10]
            a[p, g + 8] = far[np.random.randint(len(far))]
    return np.exp2(a.ravel()).repeat(32)


def f64(x):
    return np.asarray(x).astype(np.float64)


def striped(idx):
    return np.tile(idx.reshape(-1, 16).T, (8, 1)).astype(np.uint16)


def unstriped(offs):
    return offs[:16].T.reshape(-1).astype(np.int64)


E2M1 = np.array([0.0, 0.5, 1.0, 1.5, 2.0, 3.0, 4.0, 6.0, -0.0, -0.5, -1.0, -1.5, -2.0, -3.0, -4.0, -6.0])


def pack_weight(w, fmt):
    k, n = w.shape
    w = f64(np.asarray(w, np.float32).astype(ml_dtypes.bfloat16)).reshape(k // 32, 32, n)
    amax = np.abs(w).max(1)
    if fmt == "e4m3":
        byte = np.frexp(amax)[1] - 1 + 127 - 7
    else:
        mant, ex = np.frexp(amax / 6.0)
        byte = np.where(mant > 0.5, ex, ex - 1) + 127
    byte = np.clip(np.where(amax > 0, byte, 1), 1, 254)
    scaled = (w * np.exp2(127.0 - byte)[:, None, :]).reshape(k, n).astype(np.float32)
    by_word = np.ascontiguousarray(scaled.reshape(k // 512, 128, 4, n).transpose(0, 1, 3, 2))
    if fmt == "e4m3":
        words = by_word.astype(ml_dtypes.float8_e4m3fn).view(np.uint8)
    else:
        c = by_word.astype(ml_dtypes.float4_e2m1fn).view(np.uint8) & 0xF
        words = (c[..., 0::2] | (c[..., 1::2] << 4)).reshape(k // 512, 128, 2 * n)
    return np.ascontiguousarray(words), np.ascontiguousarray(byte.astype(np.uint8).reshape(k // 512, 16, n))


def unpack_weight(words, scales, fmt):
    g, _, n = scales.shape
    words = np.ascontiguousarray(words).reshape(g, 128, n, -1)
    if fmt == "e4m3":
        vals = words.view(ml_dtypes.float8_e4m3fn).astype(np.float64)
    else:
        nib = np.empty((g, 128, n, 4), np.uint8)
        nib[..., 0::2] = words & 0xF
        nib[..., 1::2] = words >> 4
        vals = E2M1[nib]
    vals = vals * np.repeat(np.exp2(scales.astype(np.float64) - 127.0), 8, axis=1)[..., None]
    return vals.transpose(0, 1, 3, 2).reshape(g * 512, n)


def planes(y):
    n, m = y.shape
    v = y.astype(np.float32).astype(ml_dtypes.bfloat16).astype(np.float64).reshape(n // 32, 32, m)
    top = np.abs(v).max(1)
    byte = np.clip(np.where(top > 0, np.frexp(top)[1] - 1 + 127 - 7, 1), 1, 254)
    codes = (v * np.exp2(127.0 - byte)[:, None, :]).reshape(n, m).astype(np.float32).astype(ml_dtypes.float8_e4m3fn).view(np.uint8)
    words = codes.reshape(n // 512, 128, 4, m).transpose(0, 1, 3, 2)
    return np.ascontiguousarray(words), np.ascontiguousarray(byte.astype(np.uint8).reshape(n // 512, 16, m))


def gelu(v):
    return 0.5 * v * (1.0 + np.tanh(np.sqrt(2.0 / np.pi) * (v + 0.044715 * v**3)))


K, T, E, C, H, N = 512, 768, 6, 256, 512, 512


def by_expert(wq, xq):
    return np.concatenate([wq[e].T @ xq[:, e * C:(e + 1) * C] for e in range(E)], axis=1)


def setup_inputs():
    n = np.random.standard_normal
    s = mx_kscale(K)
    u = mx_kscale(H)
    first = np.random.permutation(np.repeat(np.arange(E), T // E))
    second = (first + 1 + np.random.permutation(np.repeat(np.arange(E - 1), -(-T // (E - 1)))[:T])) % E
    while np.bincount(second, minlength=E).max() != T // E:
        load = np.bincount(second, minlength=E); hi, lo = int(load.argmax()), int(load.argmin())
        t = np.flatnonzero((second == hi) & (first != lo))[0]; second[t] = lo
    slot_token = np.empty(E * C, np.int64); pos = np.empty((2, T), np.int64); fill = np.zeros(E, np.int64)
    place = np.stack([np.random.permutation(C) for _ in range(E)])
    for r, deal in enumerate((first, second)):
        for t in np.random.permutation(T):
            e = deal[t]; j = e * C + place[e, fill[e]]; fill[e] += 1; slot_token[j] = t; pos[r, t] = j
    g = np.random.uniform(0.2, 0.8, T)
    partner = np.concatenate([np.random.permutation(T) for _ in range(-(-E * C // T))])[:E * C]
    x = pack_weight(n((K, T)) * s[:, None], "e4m3")
    return {
        "x_words": x[0],
        "x_scales": x[1],
        "w1": (n((E, K, H)) / np.sqrt(K) / s[None, :, None] * u).astype(np.float32),
        "wp": (n((E, K, H)) / np.sqrt(K) / s[None, :, None] * u).astype(np.float32),
        "w2": (n((E, H, N)) / np.sqrt(H) / u[None, :, None]).astype(np.float32),
        "gate": np.stack([np.tile(g, (128, 1)), np.tile(1.0 - g, (128, 1))]).astype(np.float32),
        "offs": striped(slot_token),
        "pos1": striped(pos[0]),
        "pos2": striped(pos[1]),
        "offs2": striped(partner),
    }


def reference(x_words, x_scales, w1, wp, w2, gate, offs, pos1, pos2, offs2):
    w1q = mxq(f64(w1), 1, "e4m3")
    wpq = mxq(f64(wp), 1, "e4m3")
    w2q = mxq(f64(w2), 1, "e4m3")
    idx, idx2 = unstriped(offs), unstriped(offs2)
    x = unpack_weight(x_words, x_scales, "e4m3")
    h = gelu(by_expert(w1q, x[:, idx]) + by_expert(wpq, x[:, idx2]))
    y = by_expert(w2q, mxq(h, 0, "e4m3"))
    out = sum(f64(gate[r, :1]) * y[:, unstriped(p)] for r, p in enumerate((pos1, pos2)))
    out_0 = out
    return (out_0,) + planes(out_0)

@@ -1,0 +1,223 @@
+from contextlib import ExitStack
+
+import concourse.mybir as mybir
+from concourse.masks import make_identity
+
+K, T, E, C, H, N = 512, 768, 6, 256, 512, 512
+S = E * C
+P = 128
+FLOPS = 2 * S * (2 * K * H + H * N)
+BYTES = 3 * E * K * H * 4 + K * T + K * T // 32 + 2 * T * 4 + 2 * (S + T) * 16 + N * T * 5 + N * T // 32
+
+F32 = mybir.dt.float32
+BF16 = mybir.dt.bfloat16
+I32 = mybir.dt.int32
+U32 = mybir.dt.uint32
+U16 = mybir.dt.uint16
+U8 = mybir.dt.uint8
+FP8X4 = mybir.dt.float8_e4m3fn_x4
+MULT = mybir.AluOpType.mult
+ADD = mybir.AluOpType.add
+GELU = mybir.ActivationFunctionType.Gelu_apprx_tanh
+
+LAG = 2
+CHUNKS = [256,256,128,128]
+PE_CHUNKS = 3
+VSHARE = [0,0,0,0,0,64,0,128,128,0,128,128,0,128,128,0,128,64]
+LATE = 5
+
+
+def tile_moe_duo_gelu_kernel(
+    tc, x_words, x_scales, w1, wp, w2, gate, offs, pos1, pos2, offs2, out_0, out_1, out_2
+):
+    nc = tc.nc
+    with ExitStack() as ctx:
+        lists = ctx.enter_context(tc.tile_pool(name="lists", bufs=1))
+        keep = ctx.enter_context(tc.tile_pool(name="keep", bufs=1))
+        rawp = ctx.enter_context(tc.tile_pool(name="rawp", bufs=8))
+        groupp = ctx.enter_context(tc.tile_pool(name="groupp", bufs=7))
+        stage = ctx.enter_context(tc.tile_pool(name="stage", bufs=4))
+        tail = ctx.enter_context(tc.tile_pool(name="tail", bufs=4))
+        psum = ctx.enter_context(tc.psum_pool(name="psum", bufs=4))
+
+        offs_sb = lists.tile([P, S // 16], U16, name="offs_sb")
+        offs2_sb = lists.tile([P, S // 16], U16, name="offs2_sb")
+        pos1_sb = lists.tile([P, T // 16], U16, name="pos1_sb")
+        pos2_sb = lists.tile([P, T // 16], U16, name="pos2_sb")
+        xw = keep.tile([P, T], I32, name="xw", align_bytes=64)
+        xs = keep.tile([P, T], U8, name="xs", align_bytes=64)
+        nc.vector.memset(xs[:].bitcast(I32), 0)
+        zero = keep.tile([P, 1], F32, name="zero")
+        nc.vector.memset(zero[:], 0.0)
+        bias0 = keep.tile([P, 1], F32, name="bias0")
+        nc.scalar.activation(bias0[:], zero[:], GELU, bias=zero[:])
+        ident = keep.tile([P, P], F32, name="ident")
+        make_identity(nc, ident[:])
+
+        nc.sync.dma_start(offs_sb[:], offs)
+        nc.sync.dma_start(xw[:], x_words[0].rearrange("p t d -> p (t d)").bitcast(I32))
+        nc.sync.dma_start(offs2_sb[:], offs2)
+
+        order = []
+        for e in range(E + LAG):
+            if e < E:
+                order.extend([("w1", e), ("wp", e)])
+            if e >= LAG:
+                order.append(("w2", e - LAG))
+        source = {"w1": w1, "wp": wp, "w2": w2}
+        raw = []
+        for n, (which, e) in enumerate(order):
+            if n == LATE:
+                raw.append(keep.tile([P, 4, H], F32, name="late", align_bytes=64))
+            else:
+                raw.append(rawp.tile([P, 4, H], F32, name="raw"))
+            nc.sync.dma_start(raw[n][:], source[which][e].rearrange("(p j) c -> p j c", j=4))
+            if n == 0:
+                for r in range(4):
+                    nc.sync.dma_start(xs[:].bitcast(I32)[r:P:32, :], x_scales[0].bitcast(I32)[r:16:4, :])
+            if n == 8:
+                nc.sync.dma_start(pos1_sb[:], pos1)
+                nc.sync.dma_start(pos2_sb[:], pos2)
+        gate_sb = rawp.tile([P, 2, T], F32, name="raw")
+        nc.sync.dma_start(gate_sb[:], gate.rearrange("r p t -> p r t"))
+
+        y = [keep.tile([P, S], F32, name="y%d" % t) for t in range(4)]
+        h_codes = keep.tile([P, S], U32, name="h_codes", align_bytes=64)
+        h_scales = keep.tile([P, S], U8, name="h_scales", align_bytes=64)
+        gathered = {}
+        for which in ("w1", "wp"):
+            gathered[which] = (keep.tile([P, S], U32, name="words_" + which, align_bytes=64), keep.tile([P, S], U8, name="scales_" + which, align_bytes=64))
+        for sort, table in enumerate((xw[:].bitcast(U32), xs[:])):
+            for first in range(0, S, 2 * C):
+                for which, lst in (("w1", offs_sb), ("wp", offs2_sb)):
+                    nc.vector.tensor_copy(gathered[which][sort][:, first : first + 2 * C], table.indirect(lst[:, first // 16 : (first + 2 * C) // 16]))
+
+        grouped = {}
+        quantised = {}
+        hidden = {}
+
+        def cast(n):
+            share = VSHARE[n]
+            grouped[n] = groupp.tile([P, 4 * H], BF16, name="grouped", align_bytes=64)
+            src = raw[n][:].rearrange("p j (m t) -> p m j t", t=4)
+            dst = grouped[n][:].rearrange("p (t m j) -> p m j t", t=4, j=4)
+            if share > 0:
+                nc.vector.tensor_copy(dst[:, :, :, : share // 32], src[:, :, :, : share // 32])
+            if share < P:
+                nc.scalar.copy(dst[:, :, :, share // 32 :], src[:, :, :, share // 32 :])
+
+        def quantise(n, codes):
+            scales = groupp.tile([P, H], U8, name="scales", align_bytes=64)
+            w = H // 2 if n == len(order) - 1 else H
+            for c0 in range(0, H, w):
+                nc.vector.quantize_mx(codes[:, c0 : c0 + w].bitcast(FP8X4), scales[:, c0 : c0 + w], grouped[n][:, 4 * c0 : 4 * (c0 + w)])
+            quantised[order[n]] = (codes, scales)
+
+        def first_layer(e):
+            hidden[e] = stage.tile([P, C, 4], BF16, name="hb", align_bytes=64)
+            for half in range(C // P):
+                here = slice(e * C + half * P, e * C + (half + 1) * P)
+                bank = psum.tile([P, 4, P], F32, name="bank_a")
+                for t in range(4):
+                    cols = slice(t * P, (t + 1) * P)
+                    for which in ("w1", "wp"):
+                        codes, scales = quantised[(which, e)]
+                        words, sc = gathered[which]
+                        nc.tensor.matmul_mx(bank[:, t, :], lhsT=codes[:, cols].bitcast(FP8X4), lhsT_scale=scales[:, cols],
+                                            rhs=words[:, here].bitcast(FP8X4), rhs_scale=sc[:, here],
+                                            start=(which == "w1"), stop=(which == "wp"))
+                nc.scalar.activation(hidden[e][:, half * P : (half + 1) * P, :], bank[:].rearrange("p t n -> p n t"), GELU, bias=bias0[:])
+
+        def quantise_hidden(e):
+            mine = slice(e * C, (e + 1) * C)
+            nc.vector.quantize_mx(h_codes[:, mine].bitcast(FP8X4), h_scales[:, mine], hidden[e][:].rearrange("p n t -> p (n t)"))
+
+        def second_layer(e):
+            codes, scales = quantised[("w2", e)]
+            mine = slice(e * C, (e + 1) * C)
+            for pair in range(2):
+                bank = psum.tile([P, 2, C], F32, name="bank_b")
+                for i in range(2):
+                    cols = slice((2 * pair + i) * P, (2 * pair + i + 1) * P)
+                    nc.tensor.matmul_mx(bank[:, i, :], lhsT=codes[:, cols].bitcast(FP8X4), lhsT_scale=scales[:, cols],
+                                        rhs=h_codes[:, mine].bitcast(FP8X4), rhs_scale=h_scales[:, mine], start=True, stop=True)
+                for i in range(2):
+                    if (e, pair) == (4, 1):
+                        nc.vector.tensor_copy(y[2 * pair + i][:, mine], bank[:, i, :])
+                    else:
+                        nc.scalar.copy(y[2 * pair + i][:, mine], bank[:, i, :])
+
+        for n in range(LATE + 1):
+            cast(n)
+        first_codes = keep.tile([P, (LATE + 1) * H], U32, name="late", align_bytes=64)
+        for n in range(LATE + 1):
+            quantise(n, first_codes[:, n * H : (n + 1) * H])
+        early = [e for which, e in order[: LATE + 1] if which == "wp"]
+        for e in early:
+            first_layer(e)
+        for e in early:
+            quantise_hidden(e)
+        for which, e in order[: LATE + 1]:
+            if which == "w2":
+                second_layer(e)
+        for n in range(LATE + 1, len(order)):
+            which, e = order[n]
+            cast(n)
+            quantise(n, stage.tile([P, H], U32, name="codes", align_bytes=64)[:])
+            if which == "wp":
+                first_layer(e)
+                quantise_hidden(e)
+            if which == "w2":
+                second_layer(e)
+
+        out_rows = out_0.rearrange("(p t) n -> p t n", t=4)
+        out_words = out_1[0].rearrange("p n d -> p (n d)").bitcast(I32)
+        o_scales = keep.tile([P, T], U8, name="o_scales", align_bytes=64)
+        start = 0
+        for ci, width in enumerate(CHUNKS):
+            cols = slice(start, start + width)
+            lcols = slice(start // 16, (start + width) // 16)
+            o = tail.tile([P, 4, width], F32, name="o")
+            if ci == 0:
+                ob = keep.tile([P, width, 4], BF16, name="handoff", align_bytes=64)
+            else:
+                ob = tail.tile([P, width, 4], BF16, name="ob", align_bytes=64)
+            if ci == 2:
+                both = keep.tile([P, 2, 4, width], F32, name="handoff", align_bytes=64)
+            else:
+                both = rawp.tile([P, 2, 4, width], F32, name="raw")
+            prods = [both[:, r] for r in range(2)]
+            for t in range(4):
+                for r, lst in enumerate((pos1_sb, pos2_sb)):
+                    nc.vector.tensor_tensor(prods[r][:, t, :], y[t][:].indirect(lst[:, lcols]), gate_sb[:, r, cols], MULT)
+            if ci < PE_CHUNKS:
+                for b0 in range(0, width, P):
+                    block = slice(b0, b0 + P)
+                    bank = psum.tile([P, 4, P], F32, name="bank_a")
+                    for t in range(4):
+                        for r in range(2):
+                            nc.tensor.matmul(bank[:, t, :], prods[r][:, t, block], ident[:], start=(r == 0), stop=(r == 1), is_transpose=True)
+                    turned = stage.tile([P, 4, P], F32, name="turned")
+                    nc.scalar.copy(turned[:], bank[:])
+                    back = psum.tile([P, 4, P], F32, name="bank_b")
+                    for t in range(4):
+                        nc.tensor.transpose(back[:, t, :], turned[:, t, :], ident[:])
+                    nc.scalar.copy(o[:, :, block], back[:])
+                    nc.scalar.copy(ob[:, block, :], back[:].rearrange("p t n -> p n t"))
+            else:
+                nc.vector.tensor_tensor(o[:], prods[0], prods[1], ADD)
+                src = o[:].rearrange("p t (c i) -> p c t i", i=4)
+                dst = ob[:].rearrange("p (c i) t -> p c t i", i=4)
+                if ci == len(CHUNKS) - 1:
+                    nc.vector.tensor_copy(dst, src)
+                else:
+                    nc.scalar.copy(dst, src)
+            nc.sync.dma_start(out_rows[:, :, cols], o[:])
+            o_codes = tail.tile([P, width], U32, name="o_codes", align_bytes=64)
+            for c0, c1 in [(0, 256), (256, 384)] if width == 384 else [(0, width)]:
+                nc.vector.quantize_mx(o_codes[:, c0:c1].bitcast(FP8X4), o_scales[:, start + c0 : start + c1], ob[:, c0:c1, :].rearrange("p n t -> p (n t)"))
+            nc.sync.dma_start(out_words[:, cols], o_codes[:].bitcast(I32))
+            start = start + width
+        for r in range(4):
+            eng = nc.scalar if r % 2 else nc.sync
+            eng.dma_start(out_2[0].bitcast(I32)[r:16:4, :], o_scales[:].bitcast(I32)[r:P:32, :])

@@ -21,10 +21,16 @@ ADD = mybir.AluOpType.add
 GELU = mybir.ActivationFunctionType.Gelu_apprx_tanh
 
 LAG = 2
-CHUNKS = [256,256,128,128]
-PE_CHUNKS = 3
-VSHARE = [0,0,0,0,0,64,0,128,128,0,128,128,0,128,128,0,128,64]
-LATE = 5
+CHUNKS = [384,256,128]
+PE_CHUNKS = 1
+VSHARE = [0,0,0,0,64,0,0,128,128,0,128,128,0,64,128,64,128,64]
+SLOTS = 11
+SLOT_BYTES = 4 * H * 4
+QUANT_AFTER = [4,4,4,4,None,6,7,8,None,11,11,None,None,14,None,None,None,None]
+GELU_AFTER = [6,6,None,10,15,15]
+HIDDEN_AFTER = [None,8,7,9,13,16]
+Y_ON_VECTOR = [[5,0]]
+PROD_SLOT = [8,1,10]
 
 
 def tile_moe_duo_gelu_kernel(
@@ -34,10 +40,11 @@ def tile_moe_duo_gelu_kernel(
     with ExitStack() as ctx:
         lists = ctx.enter_context(tc.tile_pool(name="lists", bufs=1))
         keep = ctx.enter_context(tc.tile_pool(name="keep", bufs=1))
-        rawp = ctx.enter_context(tc.tile_pool(name="rawp", bufs=8))
-        groupp = ctx.enter_context(tc.tile_pool(name="groupp", bufs=7))
-        stage = ctx.enter_context(tc.tile_pool(name="stage", bufs=4))
-        tail = ctx.enter_context(tc.tile_pool(name="tail", bufs=4))
+        arena = ctx.enter_context(tc.tile_pool(name="arena", bufs=1))
+        codep = ctx.enter_context(tc.tile_pool(name="codep", bufs=9))
+        groupp = ctx.enter_context(tc.tile_pool(name="groupp", bufs=8))
+        stage = ctx.enter_context(tc.tile_pool(name="stage", bufs=3))
+        tail = ctx.enter_context(tc.tile_pool(name="tail", bufs=1))
         psum = ctx.enter_context(tc.psum_pool(name="psum", bufs=4))
 
         offs_sb = lists.tile([P, S // 16], U16, name="offs_sb")
@@ -47,15 +54,15 @@ def tile_moe_duo_gelu_kernel(
         xw = keep.tile([P, T], I32, name="xw", align_bytes=64)
         xs = keep.tile([P, T], U8, name="xs", align_bytes=64)
         nc.vector.memset(xs[:].bitcast(I32), 0)
-        zero = keep.tile([P, 1], F32, name="zero")
-        nc.vector.memset(zero[:], 0.0)
+        zero = arena.tile([P, (SLOTS - 1) * 4 * H], F32, name="zero", align_bytes=64, offset=SLOT_BYTES)[:, 0:1]
+        nc.vector.memset(zero, 0.0)
         bias0 = keep.tile([P, 1], F32, name="bias0")
-        nc.scalar.activation(bias0[:], zero[:], GELU, bias=zero[:])
+        nc.scalar.activation(bias0[:], zero, GELU, bias=zero)
         ident = keep.tile([P, P], F32, name="ident")
         make_identity(nc, ident[:])
 
-        nc.sync.dma_start(offs_sb[:], offs)
         nc.sync.dma_start(xw[:], x_words[0].rearrange("p t d -> p (t d)").bitcast(I32))
+        nc.sync.dma_start(offs_sb[:], offs)
         nc.sync.dma_start(offs2_sb[:], offs2)
 
         order = []
@@ -65,25 +72,32 @@ def tile_moe_duo_gelu_kernel(
             if e >= LAG:
                 order.append(("w2", e - LAG))
         source = {"w1": w1, "wp": wp, "w2": w2}
-        raw = []
-        for n, (which, e) in enumerate(order):
-            if n == LATE:
-                raw.append(keep.tile([P, 4, H], F32, name="late", align_bytes=64))
-            else:
-                raw.append(rawp.tile([P, 4, H], F32, name="raw"))
+        raw = {}
+        used = {}
+
+        def load(n):
+            which, e = order[n]
+            raw[n] = arena.tile([P, 4, H], F32, name="raw%d" % n, align_bytes=64, offset=(n % SLOTS) * SLOT_BYTES)
             nc.sync.dma_start(raw[n][:], source[which][e].rearrange("(p j) c -> p j c", j=4))
+
+        def tenant(after, shape, dtype, size, name):
+            start = used.get(after, 0)
+            used[after] = start + size
+            assert used[after] <= SLOT_BYTES
+            return arena.tile(shape, dtype, name=name, align_bytes=64, offset=(after % SLOTS) * SLOT_BYTES + start)
+
+        for n in range(SLOTS):
+            load(n)
             if n == 0:
                 for r in range(4):
                     nc.sync.dma_start(xs[:].bitcast(I32)[r:P:32, :], x_scales[0].bitcast(I32)[r:16:4, :])
             if n == 8:
                 nc.sync.dma_start(pos1_sb[:], pos1)
                 nc.sync.dma_start(pos2_sb[:], pos2)
-        gate_sb = rawp.tile([P, 2, T], F32, name="raw")
-        nc.sync.dma_start(gate_sb[:], gate.rearrange("r p t -> p r t"))
 
         y = [keep.tile([P, S], F32, name="y%d" % t) for t in range(4)]
         h_codes = keep.tile([P, S], U32, name="h_codes", align_bytes=64)
-        h_scales = keep.tile([P, S], U8, name="h_scales", align_bytes=64)
+        h_scales = {}
         gathered = {}
         for which in ("w1", "wp"):
             gathered[which] = (keep.tile([P, S], U32, name="words_" + which, align_bytes=64), keep.tile([P, S], U8, name="scales_" + which, align_bytes=64))
@@ -106,15 +120,22 @@ def tile_moe_duo_gelu_kernel(
             if share < P:
                 nc.scalar.copy(dst[:, :, :, share // 32 :], src[:, :, :, share // 32 :])
 
-        def quantise(n, codes):
-            scales = groupp.tile([P, H], U8, name="scales", align_bytes=64)
-            w = H // 2 if n == len(order) - 1 else H
+        def quantise(n):
+            codes = codep.tile([P, H], U32, name="codes", align_bytes=64)
+            if QUANT_AFTER[n] is None:
+                scales = codep.tile([P, H], U8, name="scales", align_bytes=64)
+            else:
+                scales = tenant(QUANT_AFTER[n], [P, H], U8, H, "scales%d" % n)
+            w = H // 2 if order[n][0] == "w2" and (VSHARE[n] == 64 or n == len(order) - 1) else H
             for c0 in range(0, H, w):
                 nc.vector.quantize_mx(codes[:, c0 : c0 + w].bitcast(FP8X4), scales[:, c0 : c0 + w], grouped[n][:, 4 * c0 : 4 * (c0 + w)])
             quantised[order[n]] = (codes, scales)
 
         def first_layer(e):
-            hidden[e] = stage.tile([P, C, 4], BF16, name="hb", align_bytes=64)
+            if GELU_AFTER[e] is None:
+                hidden[e] = stage.tile([P, C, 4], BF16, name="hb", align_bytes=64)
+            else:
+                hidden[e] = tenant(GELU_AFTER[e], [P, C, 4], BF16, C * 4 * 2, "hb%d" % e)
             for half in range(C // P):
                 here = slice(e * C + half * P, e * C + (half + 1) * P)
                 bank = psum.tile([P, 4, P], F32, name="bank_a")
@@ -130,7 +151,11 @@ def tile_moe_duo_gelu_kernel(
 
         def quantise_hidden(e):
             mine = slice(e * C, (e + 1) * C)
-            nc.vector.quantize_mx(h_codes[:, mine].bitcast(FP8X4), h_scales[:, mine], hidden[e][:].rearrange("p n t -> p (n t)"))
+            if HIDDEN_AFTER[e] is None:
+                h_scales[e] = keep.tile([P, C], U8, name="h_scales%d" % e, align_bytes=64)
+            else:
+                h_scales[e] = tenant(HIDDEN_AFTER[e], [P, C], U8, C, "h_scales%d" % e)
+            nc.vector.quantize_mx(h_codes[:, mine].bitcast(FP8X4), h_scales[e][:], hidden[e][:].rearrange("p n t -> p (n t)"))
 
         def second_layer(e):
             codes, scales = quantised[("w2", e)]
@@ -140,35 +165,31 @@ def tile_moe_duo_gelu_kernel(
                 for i in range(2):
                     cols = slice((2 * pair + i) * P, (2 * pair + i + 1) * P)
                     nc.tensor.matmul_mx(bank[:, i, :], lhsT=codes[:, cols].bitcast(FP8X4), lhsT_scale=scales[:, cols],
-                                        rhs=h_codes[:, mine].bitcast(FP8X4), rhs_scale=h_scales[:, mine], start=True, stop=True)
+                                        rhs=h_codes[:, mine].bitcast(FP8X4), rhs_scale=h_scales[e][:], start=True, stop=True)
                 for i in range(2):
-                    if (e, pair) == (4, 1):
+                    if [e, pair] in Y_ON_VECTOR:
                         nc.vector.tensor_copy(y[2 * pair + i][:, mine], bank[:, i, :])
                     else:
                         nc.scalar.copy(y[2 * pair + i][:, mine], bank[:, i, :])
 
-        for n in range(LATE + 1):
-            cast(n)
-        first_codes = keep.tile([P, (LATE + 1) * H], U32, name="late", align_bytes=64)
-        for n in range(LATE + 1):
-            quantise(n, first_codes[:, n * H : (n + 1) * H])
-        early = [e for which, e in order[: LATE + 1] if which == "wp"]
-        for e in early:
-            first_layer(e)
-        for e in early:
-            quantise_hidden(e)
-        for which, e in order[: LATE + 1]:
-            if which == "w2":
-                second_layer(e)
-        for n in range(LATE + 1, len(order)):
-            which, e = order[n]
-            cast(n)
-            quantise(n, stage.tile([P, H], U32, name="codes", align_bytes=64)[:])
-            if which == "wp":
-                first_layer(e)
-                quantise_hidden(e)
-            if which == "w2":
-                second_layer(e)
+        events = []
+        quant_step = {}
+        for n, key in enumerate(order):
+            quant_step[key] = max(n, QUANT_AFTER[n] or 0)
+            events.append((n, 0, n))
+            events.append((quant_step[key], 1, n))
+        for e in range(E):
+            first = max(quant_step[("w1", e)], quant_step[("wp", e)], GELU_AFTER[e] or 0)
+            hid = max(first, HIDDEN_AFTER[e] or 0)
+            events.extend([(first, 2, e), (hid, 3, e), (max(hid, quant_step[("w2", e)]), 4, e)])
+        for step, kind, arg in sorted(events):
+            if kind == 0 and arg >= SLOTS:
+                load(arg)
+            [cast, quantise, first_layer, quantise_hidden, second_layer][kind](arg)
+        gate_sb = []
+        for h in range(2):
+            gate_sb.append(arena.tile([P, 2, T // 2], F32, name="gate%d" % h, align_bytes=64, offset=(len(order) % SLOTS) * SLOT_BYTES + h * T * 4))
+            nc.sync.dma_start(gate_sb[h][:], gate.rearrange("r p t -> p r t")[:, :, h * T // 2 : (h + 1) * T // 2])
 
         out_rows = out_0.rearrange("(p t) n -> p t n", t=4)
         out_words = out_1[0].rearrange("p n d -> p (n d)").bitcast(I32)
@@ -177,19 +198,13 @@ def tile_moe_duo_gelu_kernel(
         for ci, width in enumerate(CHUNKS):
             cols = slice(start, start + width)
             lcols = slice(start // 16, (start + width) // 16)
-            o = tail.tile([P, 4, width], F32, name="o")
-            if ci == 0:
-                ob = keep.tile([P, width, 4], BF16, name="handoff", align_bytes=64)
-            else:
-                ob = tail.tile([P, width, 4], BF16, name="ob", align_bytes=64)
-            if ci == 2:
-                both = keep.tile([P, 2, 4, width], F32, name="handoff", align_bytes=64)
-            else:
-                both = rawp.tile([P, 2, 4, width], F32, name="raw")
+            o = tail.tile([P, 4, width], F32, name="o%d" % ci)
+            ob = tail.tile([P, width, 4], BF16, name="ob%d" % ci, align_bytes=64)
+            both = arena.tile([P, 2, 4, width], F32, name="both%d" % ci, align_bytes=64, offset=PROD_SLOT[ci] * SLOT_BYTES)
             prods = [both[:, r] for r in range(2)]
             for t in range(4):
                 for r, lst in enumerate((pos1_sb, pos2_sb)):
-                    nc.vector.tensor_tensor(prods[r][:, t, :], y[t][:].indirect(lst[:, lcols]), gate_sb[:, r, cols], MULT)
+                    nc.vector.tensor_tensor(prods[r][:, t, :], y[t][:].indirect(lst[:, lcols]), gate_sb[start // (T // 2)][:, r, start % (T // 2) : start % (T // 2) + width], MULT)
             if ci < PE_CHUNKS:
                 for b0 in range(0, width, P):
                     block = slice(b0, b0 + P)
@@ -212,8 +227,8 @@ def tile_moe_duo_gelu_kernel(
                     nc.vector.tensor_copy(dst, src)
                 else:
                     nc.scalar.copy(dst, src)
-            nc.sync.dma_start(out_rows[:, :, cols], o[:])
-            o_codes = tail.tile([P, width], U32, name="o_codes", align_bytes=64)
+            (nc.scalar if ci < PE_CHUNKS else nc.sync).dma_start(out_rows[:, :, cols], o[:])
+            o_codes = tail.tile([P, width], U32, name="o_codes%d" % ci, align_bytes=64)
             for c0, c1 in [(0, 256), (256, 384)] if width == 384 else [(0, width)]:
                 nc.vector.quantize_mx(o_codes[:, c0:c1].bitcast(FP8X4), o_scales[:, start + c0 : start + c1], ob[:, c0:c1, :].rearrange("p n t -> p (n t)"))
             nc.sync.dma_start(out_words[:, cols], o_codes[:].bitcast(I32))

@@ -20,17 +20,17 @@ MULT = mybir.AluOpType.mult
 ADD = mybir.AluOpType.add
 GELU = mybir.ActivationFunctionType.Gelu_apprx_tanh
 
-LAG = 2
-CHUNKS = [384,256,128]
-PE_CHUNKS = 1
-VSHARE = [0,0,0,0,64,0,0,128,128,0,128,128,0,64,128,64,128,64]
-SLOTS = 11
-SLOT_BYTES = 4 * H * 4
-QUANT_AFTER = [4,4,4,4,None,6,7,8,None,11,11,None,None,14,None,None,None,None]
-GELU_AFTER = [6,6,None,10,15,15]
-HIDDEN_AFTER = [None,8,7,9,13,16]
-Y_ON_VECTOR = [[5,0]]
-PROD_SLOT = [8,1,10]
+BLOCKS = N // P
+CHUNKS = T // P
+GROUP = 2 * P
+GROUPS = T // GROUP
+SLOTS = 10
+RAW_BYTES = 4 * H * 4
+SLOT_BYTES = RAW_BYTES + 1024
+PIECE_BYTES = 4 * P * 4
+BANK = 2048
+SCALAR_ALONE = 6
+ADDED_FIRST = 3
 
 
 def tile_moe_duo_gelu_kernel(
@@ -41,11 +41,8 @@ def tile_moe_duo_gelu_kernel(
         lists = ctx.enter_context(tc.tile_pool(name="lists", bufs=1))
         keep = ctx.enter_context(tc.tile_pool(name="keep", bufs=1))
         arena = ctx.enter_context(tc.tile_pool(name="arena", bufs=1))
-        codep = ctx.enter_context(tc.tile_pool(name="codep", bufs=9))
-        groupp = ctx.enter_context(tc.tile_pool(name="groupp", bufs=8))
-        stage = ctx.enter_context(tc.tile_pool(name="stage", bufs=3))
-        tail = ctx.enter_context(tc.tile_pool(name="tail", bufs=1))
-        psum = ctx.enter_context(tc.psum_pool(name="psum", bufs=4))
+        ring = ctx.enter_context(tc.tile_pool(name="ring", bufs=4))
+        psum = ctx.enter_context(tc.psum_pool(name="psum", bufs=1))
 
         offs_sb = lists.tile([P, S // 16], U16, name="offs_sb")
         offs2_sb = lists.tile([P, S // 16], U16, name="offs2_sb")
@@ -54,7 +51,7 @@ def tile_moe_duo_gelu_kernel(
         xw = keep.tile([P, T], I32, name="xw", align_bytes=64)
         xs = keep.tile([P, T], U8, name="xs", align_bytes=64)
         nc.vector.memset(xs[:].bitcast(I32), 0)
-        zero = arena.tile([P, (SLOTS - 1) * 4 * H], F32, name="zero", align_bytes=64, offset=SLOT_BYTES)[:, 0:1]
+        zero = arena.tile([P, (SLOTS - 1) * SLOT_BYTES // 4], F32, name="zero", align_bytes=64, offset=SLOT_BYTES)[:, 0:1]
         nc.vector.memset(zero, 0.0)
         bias0 = keep.tile([P, 1], F32, name="bias0")
         nc.scalar.activation(bias0[:], zero, GELU, bias=zero)
@@ -65,174 +62,258 @@ def tile_moe_duo_gelu_kernel(
         nc.sync.dma_start(offs_sb[:], offs)
         nc.sync.dma_start(offs2_sb[:], offs2)
 
-        order = []
-        for e in range(E + LAG):
-            if e < E:
-                order.extend([("w1", e), ("wp", e)])
-            if e >= LAG:
-                order.append(("w2", e - LAG))
-        source = {"w1": w1, "wp": wp, "w2": w2}
         raw = {}
-        used = {}
 
-        def load(n):
-            which, e = order[n]
-            raw[n] = arena.tile([P, 4, H], F32, name="raw%d" % n, align_bytes=64, offset=(n % SLOTS) * SLOT_BYTES)
-            nc.sync.dma_start(raw[n][:], source[which][e].rearrange("(p j) c -> p j c", j=4))
+        def slot(m):
+            return (m % SLOTS) * SLOT_BYTES
 
-        def tenant(after, shape, dtype, size, name):
-            start = used.get(after, 0)
-            used[after] = start + size
-            assert used[after] <= SLOT_BYTES
-            return arena.tile(shape, dtype, name=name, align_bytes=64, offset=(after % SLOTS) * SLOT_BYTES + start)
+        def load_first(m):
+            e, which = divmod(m, 2)
+            raw[m] = arena.tile([P, SLOT_BYTES // 4], F32, name="raw%d" % m, align_bytes=64, offset=slot(m))[:, : 4 * H].rearrange("p (j c) -> p j c", j=4)
+            nc.sync.dma_start(raw[m], (w1, wp)[which][e].rearrange("(p j) c -> p j c", j=4))
 
-        for n in range(SLOTS):
-            load(n)
-            if n == 0:
+        for m in range(SLOTS):
+            load_first(m)
+            if m == 0:
                 for r in range(4):
                     nc.sync.dma_start(xs[:].bitcast(I32)[r:P:32, :], x_scales[0].bitcast(I32)[r:16:4, :])
-            if n == 8:
-                nc.sync.dma_start(pos1_sb[:], pos1)
-                nc.sync.dma_start(pos2_sb[:], pos2)
 
-        y = [keep.tile([P, S], F32, name="y%d" % t) for t in range(4)]
-        h_codes = keep.tile([P, S], U32, name="h_codes", align_bytes=64)
-        h_scales = {}
+        def placed(shape, dtype, tag, name, at, bufs):
+            if at is None:
+                return ring.tile(shape, dtype, name=tag, align_bytes=64, bufs=bufs)
+            return arena.tile(shape, dtype, name=name, align_bytes=64, offset=at)
+
         gathered = {}
-        for which in ("w1", "wp"):
-            gathered[which] = (keep.tile([P, S], U32, name="words_" + which, align_bytes=64), keep.tile([P, S], U8, name="scales_" + which, align_bytes=64))
+        for which in range(2):
+            gathered[which] = (keep.tile([P, S], U32, name="words%d" % which, align_bytes=64), keep.tile([P, S], U8, name="bytes%d" % which, align_bytes=64))
         for sort, table in enumerate((xw[:].bitcast(U32), xs[:])):
             for first in range(0, S, 2 * C):
-                for which, lst in (("w1", offs_sb), ("wp", offs2_sb)):
+                for which, lst in enumerate((offs_sb, offs2_sb)):
                     nc.vector.tensor_copy(gathered[which][sort][:, first : first + 2 * C], table.indirect(lst[:, first // 16 : (first + 2 * C) // 16]))
 
         grouped = {}
         quantised = {}
         hidden = {}
+        h_codes = {}
+        h_scales = {}
 
-        def cast(n):
-            share = VSHARE[n]
-            grouped[n] = groupp.tile([P, 4 * H], BF16, name="grouped", align_bytes=64)
-            src = raw[n][:].rearrange("p j (m t) -> p m j t", t=4)
-            dst = grouped[n][:].rearrange("p (t m j) -> p m j t", t=4, j=4)
-            if share > 0:
-                nc.vector.tensor_copy(dst[:, :, :, : share // 32], src[:, :, :, : share // 32])
-            if share < P:
-                nc.scalar.copy(dst[:, :, :, share // 32 :], src[:, :, :, share // 32 :])
-
-        def quantise(n):
-            codes = codep.tile([P, H], U32, name="codes", align_bytes=64)
-            if QUANT_AFTER[n] is None:
-                scales = codep.tile([P, H], U8, name="scales", align_bytes=64)
+        def round_first(m):
+            grouped[m] = ring.tile([P, 4 * H], BF16, name="grouped", align_bytes=64, bufs=6)
+            src = raw[m].rearrange("p j (m t) -> p m j t", t=4)
+            dst = grouped[m][:].rearrange("p (t m j) -> p m j t", t=4, j=4)
+            if m < SCALAR_ALONE:
+                nc.scalar.copy(dst, src)
             else:
-                scales = tenant(QUANT_AFTER[n], [P, H], U8, H, "scales%d" % n)
-            w = H // 2 if order[n][0] == "w2" and (VSHARE[n] == 64 or n == len(order) - 1) else H
-            for c0 in range(0, H, w):
-                nc.vector.quantize_mx(codes[:, c0 : c0 + w].bitcast(FP8X4), scales[:, c0 : c0 + w], grouped[n][:, 4 * c0 : 4 * (c0 + w)])
-            quantised[order[n]] = (codes, scales)
+                hands = 4 if m % 2 == 0 else 2
+                if hands > 0:
+                    nc.vector.tensor_copy(dst[:, :, :, :hands], src[:, :, :, :hands])
+                if hands < 4:
+                    nc.scalar.copy(dst[:, :, :, hands:], src[:, :, :, hands:])
+            if m + SLOTS < 2 * E:
+                load_first(m + SLOTS)
 
-        def first_layer(e):
-            if GELU_AFTER[e] is None:
-                hidden[e] = stage.tile([P, C, 4], BF16, name="hb", align_bytes=64)
-            else:
-                hidden[e] = tenant(GELU_AFTER[e], [P, C, 4], BF16, C * 4 * 2, "hb%d" % e)
-            for half in range(C // P):
-                here = slice(e * C + half * P, e * C + (half + 1) * P)
-                bank = psum.tile([P, 4, P], F32, name="bank_a")
-                for t in range(4):
-                    cols = slice(t * P, (t + 1) * P)
-                    for which in ("w1", "wp"):
-                        codes, scales = quantised[(which, e)]
-                        words, sc = gathered[which]
-                        nc.tensor.matmul_mx(bank[:, t, :], lhsT=codes[:, cols].bitcast(FP8X4), lhsT_scale=scales[:, cols],
-                                            rhs=words[:, here].bitcast(FP8X4), rhs_scale=sc[:, here],
-                                            start=(which == "w1"), stop=(which == "wp"))
-                nc.scalar.activation(hidden[e][:, half * P : (half + 1) * P, :], bank[:].rearrange("p t n -> p n t"), GELU, bias=bias0[:])
+        def quantise_first(m, at):
+            codes = ring.tile([P, H], U32, name="codes", align_bytes=64, bufs=5)
+            scales = placed([P, H], U8, "scales", "scales%d" % m, at, 5)
+            step = H // 2 if m == 2 * E - 1 else H
+            for c0 in range(0, H, step):
+                nc.vector.quantize_mx(codes[:, c0 : c0 + step].bitcast(FP8X4), scales[:, c0 : c0 + step], grouped[m][:, 4 * c0 : 4 * (c0 + step)])
+            quantised[m] = (codes, scales)
 
-        def quantise_hidden(e):
-            mine = slice(e * C, (e + 1) * C)
-            if HIDDEN_AFTER[e] is None:
-                h_scales[e] = keep.tile([P, C], U8, name="h_scales%d" % e, align_bytes=64)
-            else:
-                h_scales[e] = tenant(HIDDEN_AFTER[e], [P, C], U8, C, "h_scales%d" % e)
-            nc.vector.quantize_mx(h_codes[:, mine].bitcast(FP8X4), h_scales[e][:], hidden[e][:].rearrange("p n t -> p (n t)"))
+        def first_layer(e, at):
+            hidden[e] = placed([P, C, 4], BF16, "hidden", "hidden%d" % e, at, 2)
+            banks = [psum.tile([P, 4, P], F32, name="bank_a%d_%d" % (e, half), offset=((2 * e + half) % 3) * BANK) for half in range(C // P)]
+            for hands in ([(0, 1), (2, 3)] if e == E - 1 else [(0, 1, 2, 3)]):
+                for half in range(C // P):
+                    here = slice(e * C + half * P, e * C + (half + 1) * P)
+                    for t in hands:
+                        cols = slice(t * P, (t + 1) * P)
+                        for which in range(2):
+                            codes, scales = quantised[2 * e + which]
+                            nc.tensor.matmul_mx(banks[half][:, t, :], lhsT=codes[:, cols].bitcast(FP8X4), lhsT_scale=scales[:, cols],
+                                                rhs=gathered[which][0][:, here].bitcast(FP8X4), rhs_scale=gathered[which][1][:, here],
+                                                start=(which == 0), stop=(which == 1))
+                    if hands[-1] == 3:
+                        nc.scalar.activation(hidden[e][:, half * P : (half + 1) * P, :], banks[half][:].rearrange("p t n -> p n t"), GELU, bias=bias0[:])
 
-        def second_layer(e):
-            codes, scales = quantised[("w2", e)]
-            mine = slice(e * C, (e + 1) * C)
-            for pair in range(2):
-                bank = psum.tile([P, 2, C], F32, name="bank_b")
-                for i in range(2):
-                    cols = slice((2 * pair + i) * P, (2 * pair + i + 1) * P)
-                    nc.tensor.matmul_mx(bank[:, i, :], lhsT=codes[:, cols].bitcast(FP8X4), lhsT_scale=scales[:, cols],
-                                        rhs=h_codes[:, mine].bitcast(FP8X4), rhs_scale=h_scales[e][:], start=True, stop=True)
-                for i in range(2):
-                    if [e, pair] in Y_ON_VECTOR:
-                        nc.vector.tensor_copy(y[2 * pair + i][:, mine], bank[:, i, :])
-                    else:
-                        nc.scalar.copy(y[2 * pair + i][:, mine], bank[:, i, :])
+        def quantise_hidden(e, at):
+            h_codes[e] = keep.tile([P, C], U32, name="h_codes%d" % e, align_bytes=64)
+            h_scales[e] = placed([P, C], U8, "h_scales", "h_scales%d" % e, at, 3)
+            nc.vector.quantize_mx(h_codes[e][:].bitcast(FP8X4), h_scales[e][:], hidden[e][:].rearrange("p n t -> p (n t)"))
 
-        events = []
-        quant_step = {}
-        for n, key in enumerate(order):
-            quant_step[key] = max(n, QUANT_AFTER[n] or 0)
-            events.append((n, 0, n))
-            events.append((quant_step[key], 1, n))
-        for e in range(E):
-            first = max(quant_step[("w1", e)], quant_step[("wp", e)], GELU_AFTER[e] or 0)
-            hid = max(first, HIDDEN_AFTER[e] or 0)
-            events.extend([(first, 2, e), (hid, 3, e), (max(hid, quant_step[("w2", e)]), 4, e)])
-        for step, kind, arg in sorted(events):
-            if kind == 0 and arg >= SLOTS:
-                load(arg)
-            [cast, quantise, first_layer, quantise_hidden, second_layer][kind](arg)
+        def behind(m, at):
+            return slot(m) + at if m < 2 * E else None
+
+        for m in range(SCALAR_ALONE):
+            round_first(m)
+        for m in range(SCALAR_ALONE - 1):
+            quantise_first(m, None)
+        for m in range(SCALAR_ALONE, 2 * E + 2):
+            if m < 2 * E:
+                round_first(m)
+            if m - 1 < 2 * E:
+                quantise_first(m - 1, behind(m, RAW_BYTES) if m % 2 == 0 else None)
+            if m == SCALAR_ALONE:
+                first_layer(0, behind(m - 1, 0))
+                first_layer(1, behind(m - 1, 2048))
+            if m % 2 == 1:
+                first_layer((m - 3) // 2, behind(m, 0) if True else None)
+            if m % 2 == 0 and True:
+                quantise_hidden((m - 6) // 2, behind(m, RAW_BYTES + 512))
+
+        raw2 = {}
+
+        def piece(n):
+            return (2 + n // 4) * SLOT_BYTES + n % 4 * PIECE_BYTES if n < BLOCKS * E else None
+
         gate_sb = []
-        for h in range(2):
-            gate_sb.append(arena.tile([P, 2, T // 2], F32, name="gate%d" % h, align_bytes=64, offset=(len(order) % SLOTS) * SLOT_BYTES + h * T * 4))
-            nc.sync.dma_start(gate_sb[h][:], gate.rearrange("r p t -> p r t")[:, :, h * T // 2 : (h + 1) * T // 2])
+        for b in range(BLOCKS):
+            for e in range(E):
+                raw2[(b, e)] = arena.tile([P, 4, P], F32, name="raw2_%d_%d" % (b, e), align_bytes=64, offset=piece(b * E + e))
+                nc.sync.dma_start(raw2[(b, e)][:], w2[e].rearrange("(p j) c -> p j c", j=4)[:, :, b * P : (b + 1) * P])
+            if b == 0:
+                nc.sync.dma_start(pos1_sb[:], pos1)
+                nc.sync.dma_start(pos2_sb[:], pos2)
+                for r in range(2):
+                    gate_sb.append(keep.tile([P, T], F32, name="gate%d" % r))
+                    nc.sync.dma_start(gate_sb[r][:], gate[r])
 
-        out_rows = out_0.rearrange("(p t) n -> p t n", t=4)
-        out_words = out_1[0].rearrange("p n d -> p (n d)").bitcast(I32)
-        o_scales = keep.tile([P, T], U8, name="o_scales", align_bytes=64)
-        start = 0
-        for ci, width in enumerate(CHUNKS):
-            cols = slice(start, start + width)
-            lcols = slice(start // 16, (start + width) // 16)
-            o = tail.tile([P, 4, width], F32, name="o%d" % ci)
-            ob = tail.tile([P, width, 4], BF16, name="ob%d" % ci, align_bytes=64)
-            both = arena.tile([P, 2, 4, width], F32, name="both%d" % ci, align_bytes=64, offset=PROD_SLOT[ci] * SLOT_BYTES)
-            prods = [both[:, r] for r in range(2)]
-            for t in range(4):
-                for r, lst in enumerate((pos1_sb, pos2_sb)):
-                    nc.vector.tensor_tensor(prods[r][:, t, :], y[t][:].indirect(lst[:, lcols]), gate_sb[start // (T // 2)][:, r, start % (T // 2) : start % (T // 2) + width], MULT)
-            if ci < PE_CHUNKS:
-                for b0 in range(0, width, P):
-                    block = slice(b0, b0 + P)
-                    bank = psum.tile([P, 4, P], F32, name="bank_a")
-                    for t in range(4):
-                        for r in range(2):
-                            nc.tensor.matmul(bank[:, t, :], prods[r][:, t, block], ident[:], start=(r == 0), stop=(r == 1), is_transpose=True)
-                    turned = stage.tile([P, 4, P], F32, name="turned")
-                    nc.scalar.copy(turned[:], bank[:])
-                    back = psum.tile([P, 4, P], F32, name="bank_b")
-                    for t in range(4):
-                        nc.tensor.transpose(back[:, t, :], turned[:, t, :], ident[:])
-                    nc.scalar.copy(o[:, :, block], back[:])
-                    nc.scalar.copy(ob[:, block, :], back[:].rearrange("p t n -> p n t"))
-            else:
-                nc.vector.tensor_tensor(o[:], prods[0], prods[1], ADD)
-                src = o[:].rearrange("p t (c i) -> p c t i", i=4)
-                dst = ob[:].rearrange("p (c i) t -> p c t i", i=4)
-                if ci == len(CHUNKS) - 1:
+        y = {}
+        grouped2 = {}
+        prods = {}
+        summed = {}
+
+        def round_second(b, experts, on_vector):
+            grouped2[(b, experts)] = ring.tile([P, len(experts), P, 4], BF16, name="grouped2", align_bytes=64)
+            for i, e in enumerate(experts):
+                src = raw2[(b, e)][:].rearrange("p j (c i) -> p c j i", i=4)
+                dst = grouped2[(b, experts)][:, i].rearrange("p (c i) j -> p c j i", i=4)
+                if e in on_vector:
                     nc.vector.tensor_copy(dst, src)
                 else:
                     nc.scalar.copy(dst, src)
-            (nc.scalar if ci < PE_CHUNKS else nc.sync).dma_start(out_rows[:, :, cols], o[:])
-            o_codes = tail.tile([P, width], U32, name="o_codes%d" % ci, align_bytes=64)
-            for c0, c1 in [(0, 256), (256, 384)] if width == 384 else [(0, width)]:
-                nc.vector.quantize_mx(o_codes[:, c0:c1].bitcast(FP8X4), o_scales[:, start + c0 : start + c1], ob[:, c0:c1, :].rearrange("p n t -> p (n t)"))
-            nc.sync.dma_start(out_words[:, cols], o_codes[:].bitcast(I32))
-            start = start + width
-        for r in range(4):
-            eng = nc.scalar if r % 2 else nc.sync
-            eng.dma_start(out_2[0].bitcast(I32)[r:16:4, :], o_scales[:].bitcast(I32)[r:P:32, :])
+
+        def second_layer(b, experts, at, bank_at):
+            if b not in y:
+                y[b] = ring.tile([P, S], F32, name="y", bufs=3)
+            count = len(experts)
+            codes = ring.tile([P, count * P], U32, name="codes2", align_bytes=64)
+            scales = placed([P, count * P], U8, "scales2", "scales2_%d_%d" % (b, experts[0]), at, 4)
+            nc.vector.quantize_mx(codes[:].bitcast(FP8X4), scales[:], grouped2[(b, experts)][:].rearrange("p e c j -> p (e c j)"))
+            bank = psum.tile([P, count, C], F32, name="bank_y%d_%d" % (b, experts[0]), offset=bank_at * BANK)
+            for i, e in enumerate(experts):
+                cols = slice(i * P, (i + 1) * P)
+                nc.tensor.matmul_mx(bank[:, i, :], lhsT=codes[:, cols].bitcast(FP8X4), lhsT_scale=scales[:, cols],
+                                    rhs=h_codes[e][:].bitcast(FP8X4), rhs_scale=h_scales[e][:], start=True, stop=True)
+            nc.scalar.copy(y[b][:, experts[0] * C : (experts[-1] + 1) * C], bank[:].rearrange("p e n -> p (e n)"))
+
+        def fetch(b, r, start, width, at):
+            prods[(b, r, start)] = placed([P, width], F32, "prods%d" % width, "prods_%d_%d" % (b, r), at, 6 if width < T else 3)
+            lst = (pos1_sb, pos2_sb)[r]
+            nc.vector.tensor_tensor(prods[(b, r, start)][:], y[b][:].indirect(lst[:, start // 16 : (start + width) // 16]), gate_sb[r][:, start : start + width], MULT)
+
+        def add(b, parts, at):
+            summed[b] = placed([P, T], F32, "summed", "summed%d" % b, at, 2)
+            for start, width in parts:
+                nc.vector.tensor_tensor(summed[b][:, start : start + width], prods[(b, 0, start)][:], prods[(b, 1, start)][:], ADD)
+            nc.sync.dma_start(out_0[b * P : (b + 1) * P, :], summed[b][:])
+
+        turned = {}
+        for h in range(2):
+            for g in range(GROUPS):
+                turned[(h, g)] = keep.tile([P, 2, 2, 64], F32, name="turned%d_%d" % (h, g), align_bytes=64)
+
+        def turn(g, bank, terms):
+            for a in range(2):
+                for r, term in enumerate(terms[a]):
+                    nc.tensor.matmul(bank[:, a, :], term, ident[:], start=(r == 0), stop=(r == len(terms[a]) - 1), is_transpose=True)
+
+        def chunk(tile, g, a):
+            return tile[:, a * T // 2 + g * P : a * T // 2 + (g + 1) * P]
+
+        def round_turned(b, g, bank):
+            h, low = divmod(b, 2)
+            dst = turned[(h, g)][:].bitcast(BF16)[:, :, :, 64 * low : 64 * (low + 1)].rearrange("t u a (p i) -> t u a p i", i=2)
+            nc.scalar.copy(dst, bank.rearrange("t a (p u i) -> t u a p i", u=2, i=2))
+
+        def turn_block(b, bank_at):
+            banks = psum.tile([P, 4, 2, P], F32, name="banks_t%d" % b, offset=bank_at * BANK)
+            tiles = [summed[b]] if b in summed else [prods[(b, 0, 0)], prods[(b, 1, 0)]]
+            for g in range(GROUPS):
+                turn(g, banks[:, g], [[chunk(tile, g, a) for tile in tiles] for a in range(2)])
+            for g in range(GROUPS):
+                round_turned(b, g, banks[:, g])
+
+        rounded = {}
+        o_codes = [keep.tile([P, T // 2], U32, name="o_codes%d" % h, align_bytes=64) for h in range(2)]
+        o_scales = keep.tile([P, 2, T // 2], U8, name="o_scales", align_bytes=64)
+        words_out = out_1[0].rearrange("p n d -> p (n d)").bitcast(I32)
+        scales_out = out_2[0].bitcast(I32).rearrange("(h q) (a t) -> q a h t", h=2, a=2)
+
+        def turn_back(h, groups, bank_at):
+            bank = psum.tile([P, len(groups), 2, P], F32, name="bank_w%d_%d" % (h, groups[0]), offset=bank_at * BANK)
+            for i, g in enumerate(groups):
+                for u in range(2):
+                    nc.tensor.transpose(bank[:, i, u, :], turned[(h, g)][:, u].rearrange("t a p -> t (a p)"), ident[:])
+            rounded[(h, groups)] = ring.tile([P, len(groups), P, 2], F32, name="rounded", align_bytes=64, bufs=5)
+            nc.scalar.copy(rounded[(h, groups)][:], bank[:].rearrange("p g u t -> p g t u"))
+
+        def hand_on(h, groups):
+            span = slice(groups[0] * P, (groups[-1] + 1) * P)
+            nc.vector.quantize_mx(o_codes[h][:, span].bitcast(FP8X4), o_scales[:, h, span], rounded[(h, groups)][:].rearrange("p g t u -> p (g t u)").bitcast(BF16))
+
+        def store_words(h):
+            for a in range(2):
+                nc.sync.dma_start(words_out[64 * h : 64 * (h + 1), a * T // 2 : (a + 1) * T // 2], o_codes[h][:].bitcast(I32)[64 * a : 64 * (a + 1), :])
+
+        round_second(0, (0, 1), (1,))
+        quantise_hidden(E - 2, None)
+        second_layer(0, (0, 1), None, 3)
+        round_second(0, (2, 3), (2, 3))
+        second_layer(0, (2, 3), None, 4)
+        round_second(0, (4,), (4,))
+        second_layer(0, (4,), None, 5)
+        quantise_hidden(E - 1, None)
+        round_second(0, (5,), (5,))
+        second_layer(0, (5,), None, 6)
+        for b in range(1, BLOCKS):
+            for i in range(E // 2):
+                round_second(b, (2 * i, 2 * i + 1), (0, 1) if b == 1 else ())
+                second_layer(b, (2 * i, 2 * i + 1), None, 3 + i)
+                fetch_at = (piece(b * E), piece(b * E + 2))
+                if i < 2:
+                    fetch(b - 1, i, 0, T, fetch_at[i])
+            if b - 1 < ADDED_FIRST:
+                add(b - 1, [(0, T)], piece(b * E + 4))
+
+        last = BLOCKS - 1
+        turn_block(0, 0)
+        turn_block(1, 6)
+        turn_back(0, (0, 1), 0)
+        turn_back(0, (2,), 1)
+        hand_on(0, (0, 1))
+        hand_on(0, (2,))
+        store_words(0)
+        turn_block(2, 6)
+        fetch(last, 0, 0, T, None)
+        for g in range(GROUPS):
+            for a in range(2):
+                fetch(last, 1, a * T // 2 + g * P, P, None)
+            bank = psum.tile([P, 2, P], F32, name="bank_t%d" % g, offset=(2, 3, 4)[g] * BANK)
+            turn(g, bank[:], [[chunk(prods[(last, 0, 0)], g, a), prods[(last, 1, a * T // 2 + g * P)][:]] for a in range(2)])
+            round_turned(last, g, bank[:])
+            turn_back(1, (g,), (5, 0, 1)[g])
+
+        for b in range(ADDED_FIRST, last):
+            add(b, [(0, T)], None)
+        summed[last] = ring.tile([P, T], F32, name="summed", align_bytes=64, bufs=2)
+        for start in range(0, T, P):
+            nc.vector.tensor_tensor(summed[last][:, start : start + P], prods[(last, 0, 0)][:, start : start + P], prods[(last, 1, start)][:], ADD)
+        nc.sync.dma_start(out_0[last * P : (last + 1) * P, :], summed[last][:])
+        for g in range(GROUPS):
+            hand_on(1, (g,))
+        store_words(1)
+        for q in range(4):
+            a, low = divmod(q, 2)
+            eng = nc.scalar if low else nc.sync
+            eng.dma_start(scales_out[4 * low : 4 * low + 4, a], o_scales[:].bitcast(I32)[32 * q : 32 * q + 4])

@@ -20,17 +20,14 @@ MULT = mybir.AluOpType.mult
 ADD = mybir.AluOpType.add
 GELU = mybir.ActivationFunctionType.Gelu_apprx_tanh
 
-BLOCKS = N // P
-CHUNKS = T // P
-GROUP = 2 * P
-GROUPS = T // GROUP
+CHUNKS = [(0, 256), (256, 256), (512, 256)]
+WHOLE = 3
 SLOTS = 10
 RAW_BYTES = 4 * H * 4
-SLOT_BYTES = RAW_BYTES + 1024
-PIECE_BYTES = 4 * P * 4
+PAD_BYTES = 1024
+SLOT_BYTES = RAW_BYTES + 2 * PAD_BYTES
 BANK = 2048
 SCALAR_ALONE = 6
-ADDED_FIRST = 3
 
 
 def tile_moe_duo_gelu_kernel(
@@ -67,13 +64,15 @@ def tile_moe_duo_gelu_kernel(
         def slot(m):
             return (m % SLOTS) * SLOT_BYTES
 
-        def load_first(m):
-            e, which = divmod(m, 2)
-            raw[m] = arena.tile([P, SLOT_BYTES // 4], F32, name="raw%d" % m, align_bytes=64, offset=slot(m))[:, : 4 * H].rearrange("p (j c) -> p j c", j=4)
-            nc.sync.dma_start(raw[m], (w1, wp)[which][e].rearrange("(p j) c -> p j c", j=4))
+        def load(m):
+            source = (w1, wp)[m % 2][m // 2] if m < 2 * E else w2[m - 2 * E]
+            lead = 0 if m < SLOTS else PAD_BYTES
+            tile = arena.tile([P, (RAW_BYTES + PAD_BYTES) // 4], F32, name="raw%d" % m, align_bytes=64, offset=slot(m) + PAD_BYTES - lead)
+            raw[m] = tile[:, lead // 4 : lead // 4 + 4 * H].rearrange("p (j c) -> p j c", j=4)
+            nc.sync.dma_start(raw[m], source.rearrange("(p j) c -> p j c", j=4))
 
         for m in range(SLOTS):
-            load_first(m)
+            load(m)
             if m == 0:
                 for r in range(4):
                     nc.sync.dma_start(xs[:].bitcast(I32)[r:P:32, :], x_scales[0].bitcast(I32)[r:16:4, :])
@@ -91,6 +90,7 @@ def tile_moe_duo_gelu_kernel(
                 for which, lst in enumerate((offs_sb, offs2_sb)):
                     nc.vector.tensor_copy(gathered[which][sort][:, first : first + 2 * C], table.indirect(lst[:, first // 16 : (first + 2 * C) // 16]))
 
+        gate_sb = [keep.tile([P, T], F32, name="gate%d" % r) for r in range(2)]
         grouped = {}
         quantised = {}
         hidden = {}
@@ -104,20 +104,27 @@ def tile_moe_duo_gelu_kernel(
             if m < SCALAR_ALONE:
                 nc.scalar.copy(dst, src)
             else:
-                hands = 4 if m % 2 == 0 else 2
+                hands = 2 if m in (11, 13, 17) else (0 if m in (7, 9) else 4)
                 if hands > 0:
                     nc.vector.tensor_copy(dst[:, :, :, :hands], src[:, :, :, :hands])
                 if hands < 4:
                     nc.scalar.copy(dst[:, :, :, hands:], src[:, :, :, hands:])
-            if m + SLOTS < 2 * E:
-                load_first(m + SLOTS)
+
+        def load_ahead(m):
+            if SLOTS <= m < 3 * E:
+                load(m)
+            if m == 3 * E - 1:
+                nc.sync.dma_start(pos1_sb[:], pos1)
+                nc.sync.dma_start(pos2_sb[:], pos2)
+                for r in range(2):
+                    nc.sync.dma_start(gate_sb[r][:], gate[r])
 
         def quantise_first(m, at):
             codes = ring.tile([P, H], U32, name="codes", align_bytes=64, bufs=5)
             scales = placed([P, H], U8, "scales", "scales%d" % m, at, 5)
-            step = H // 2 if m == 2 * E - 1 else H
-            for c0 in range(0, H, step):
-                nc.vector.quantize_mx(codes[:, c0 : c0 + step].bitcast(FP8X4), scales[:, c0 : c0 + step], grouped[m][:, 4 * c0 : 4 * (c0 + step)])
+            cuts = {2 * E - 1: (0, 2 * P, H), 3 * E - 1: (0, P, 2 * P, H)}.get(m, (0, H))
+            for c0, c1 in zip(cuts, cuts[1:]):
+                nc.vector.quantize_mx(codes[:, c0:c1].bitcast(FP8X4), scales[:, c0:c1], grouped[m][:, 4 * c0 : 4 * c1])
             quantised[m] = (codes, scales)
 
         def first_layer(e, at):
@@ -142,178 +149,97 @@ def tile_moe_duo_gelu_kernel(
             nc.vector.quantize_mx(h_codes[e][:].bitcast(FP8X4), h_scales[e][:], hidden[e][:].rearrange("p n t -> p (n t)"))
 
         def behind(m, at):
-            return slot(m) + at if m < 2 * E else None
+            if m >= 3 * E:
+                return None
+            return slot(m) + at + (PAD_BYTES + RAW_BYTES if m < SLOTS else 0)
+
+        y = [keep.tile([P, S], F32, name="y%d" % t) for t in range(4)]
+
+        def second_layer(e):
+            codes, scales = quantised[2 * E + e]
+            mine = slice(e * C, (e + 1) * C)
+            for t in range(4):
+                bank = psum.tile([P, C], F32, name="bank_y%d_%d" % (e, t), offset=(3 + (4 * e + t) % 5) * BANK)
+                cols = slice(t * P, (t + 1) * P)
+                nc.tensor.matmul_mx(bank[:], lhsT=codes[:, cols].bitcast(FP8X4), lhsT_scale=scales[:, cols],
+                                    rhs=h_codes[e][:].bitcast(FP8X4), rhs_scale=h_scales[e][:], start=True, stop=True)
+                nc.scalar.copy(y[t][:, mine], bank[:])
 
         for m in range(SCALAR_ALONE):
             round_first(m)
+            load_ahead(m + SLOTS - 2)
         for m in range(SCALAR_ALONE - 1):
             quantise_first(m, None)
-        for m in range(SCALAR_ALONE, 2 * E + 2):
-            if m < 2 * E:
+        for m in range(SCALAR_ALONE, 3 * E + 1):
+            if m < 3 * E:
                 round_first(m)
-            if m - 1 < 2 * E:
-                quantise_first(m - 1, behind(m, RAW_BYTES) if m % 2 == 0 else None)
+            quantise_first(m - 1, behind(m, 0) if m % 2 == 0 and m < 12 else None)
             if m == SCALAR_ALONE:
-                first_layer(0, behind(m - 1, 0))
-                first_layer(1, behind(m - 1, 2048))
-            if m % 2 == 1:
-                first_layer((m - 3) // 2, behind(m, 0) if True else None)
-            if m % 2 == 0 and True:
-                quantise_hidden((m - 6) // 2, behind(m, RAW_BYTES + 512))
+                first_layer(0, slot(m - 1) + PAD_BYTES)
+                first_layer(1, slot(m - 1) + PAD_BYTES + 2048)
+            if (m - 3) % 2 == 0 and 2 <= (m - 3) // 2 < E:
+                first_layer((m - 3) // 2, slot(m) + PAD_BYTES)
+            if (m - 6) % 2 == 0 and 0 <= (m - 6) // 2 < E:
+                quantise_hidden((m - 6) // 2, behind(m, 512))
+            load_ahead(m + SLOTS - 2)
+            if m > 2 * E:
+                second_layer(m - 1 - 2 * E)
 
-        raw2 = {}
-
-        def piece(n):
-            return (2 + n // 4) * SLOT_BYTES + n % 4 * PIECE_BYTES if n < BLOCKS * E else None
-
-        gate_sb = []
-        for b in range(BLOCKS):
-            for e in range(E):
-                raw2[(b, e)] = arena.tile([P, 4, P], F32, name="raw2_%d_%d" % (b, e), align_bytes=64, offset=piece(b * E + e))
-                nc.sync.dma_start(raw2[(b, e)][:], w2[e].rearrange("(p j) c -> p j c", j=4)[:, :, b * P : (b + 1) * P])
-            if b == 0:
-                nc.sync.dma_start(pos1_sb[:], pos1)
-                nc.sync.dma_start(pos2_sb[:], pos2)
-                for r in range(2):
-                    gate_sb.append(keep.tile([P, T], F32, name="gate%d" % r))
-                    nc.sync.dma_start(gate_sb[r][:], gate[r])
-
-        y = {}
-        grouped2 = {}
+        out_rows = out_0.rearrange("(p t) n -> p t n", t=4)
+        out_words = out_1[0].rearrange("p n d -> p (n d)").bitcast(I32)
+        o_scales = keep.tile([P, T], U8, name="o_scales", align_bytes=64)
+        summed = keep.tile([P, 4, T], F32, name="summed")
         prods = {}
-        summed = {}
 
-        def round_second(b, experts, on_vector):
-            grouped2[(b, experts)] = ring.tile([P, len(experts), P, 4], BF16, name="grouped2", align_bytes=64)
-            for i, e in enumerate(experts):
-                src = raw2[(b, e)][:].rearrange("p j (c i) -> p c j i", i=4)
-                dst = grouped2[(b, experts)][:, i].rearrange("p (c i) j -> p c j i", i=4)
-                if e in on_vector:
-                    nc.vector.tensor_copy(dst, src)
-                else:
-                    nc.scalar.copy(dst, src)
+        def fetch(t, start, width):
+            prods[(t, start)] = ring.tile([P, 2, width], F32, name="prods%d" % width, bufs=2)
+            for r, lst in enumerate((pos1_sb, pos2_sb)):
+                nc.vector.tensor_tensor(prods[(t, start)][:, r, :], y[t][:].indirect(lst[:, start // 16 : (start + width) // 16]), gate_sb[r][:, start : start + width], MULT)
 
-        def second_layer(b, experts, at, bank_at):
-            if b not in y:
-                y[b] = ring.tile([P, S], F32, name="y", bufs=3)
-            count = len(experts)
-            codes = ring.tile([P, count * P], U32, name="codes2", align_bytes=64)
-            scales = placed([P, count * P], U8, "scales2", "scales2_%d_%d" % (b, experts[0]), at, 4)
-            nc.vector.quantize_mx(codes[:].bitcast(FP8X4), scales[:], grouped2[(b, experts)][:].rearrange("p e c j -> p (e c j)"))
-            bank = psum.tile([P, count, C], F32, name="bank_y%d_%d" % (b, experts[0]), offset=bank_at * BANK)
-            for i, e in enumerate(experts):
-                cols = slice(i * P, (i + 1) * P)
-                nc.tensor.matmul_mx(bank[:, i, :], lhsT=codes[:, cols].bitcast(FP8X4), lhsT_scale=scales[:, cols],
-                                    rhs=h_codes[e][:].bitcast(FP8X4), rhs_scale=h_scales[e][:], start=True, stop=True)
-            nc.scalar.copy(y[b][:, experts[0] * C : (experts[-1] + 1) * C], bank[:].rearrange("p e n -> p (e n)"))
+        def add_by_turning(t, count):
+            there = [psum.tile([P, P], F32, name="there%d_%d" % (t, b), offset=b * BANK) for b in range(count)]
+            for r in range(2):
+                for b in range(count):
+                    nc.tensor.matmul(there[b][:], prods[(t, 0)][:, r, b * P : (b + 1) * P], ident[:], start=(r == 0), stop=(r == 1), is_transpose=True)
+            for first in range(0, count, 2):
+                back = psum.tile([P, 2, P], F32, name="back%d_%d" % (t, first), offset=(6 + first // 2 % 2) * BANK)
+                for b in range(2):
+                    turned = ring.tile([P, P], F32, name="turned", bufs=4)
+                    nc.scalar.copy(turned[:], there[first + b][:])
+                    nc.tensor.transpose(back[:, b, :], turned[:], ident[:])
+                nc.scalar.copy(summed[:, t, first * P : (first + 2) * P], back[:].rearrange("p b n -> p (b n)"))
 
-        def fetch(b, r, start, width, at):
-            prods[(b, r, start)] = placed([P, width], F32, "prods%d" % width, "prods_%d_%d" % (b, r), at, 6 if width < T else 3)
-            lst = (pos1_sb, pos2_sb)[r]
-            nc.vector.tensor_tensor(prods[(b, r, start)][:], y[b][:].indirect(lst[:, start // 16 : (start + width) // 16]), gate_sb[r][:, start : start + width], MULT)
+        def add(t, first, start, width):
+            cols = slice(start - first, start - first + width)
+            nc.vector.tensor_tensor(summed[:, t, start : start + width], prods[(t, first)][:, 0, cols], prods[(t, first)][:, 1, cols], ADD)
 
-        def add(b, parts, at):
-            summed[b] = placed([P, T], F32, "summed", "summed%d" % b, at, 2)
-            for start, width in parts:
-                nc.vector.tensor_tensor(summed[b][:, start : start + width], prods[(b, 0, start)][:], prods[(b, 1, start)][:], ADD)
-            nc.sync.dma_start(out_0[b * P : (b + 1) * P, :], summed[b][:])
+        def hand_on(start, width, on_vector):
+            rounded = keep.tile([P, width, 4], BF16, name="rounded%d" % start, align_bytes=64)
+            src = summed[:, :, start : start + width].rearrange("p t (c i) -> p c t i", i=4)
+            dst = rounded[:].rearrange("p (c i) t -> p c t i", i=4)
+            if on_vector:
+                nc.vector.tensor_copy(dst, src)
+            else:
+                nc.scalar.copy(dst, src)
+            o_codes = keep.tile([P, width], U32, name="o_codes%d" % start, align_bytes=64)
+            for c0 in range(0, width, 2 * P):
+                c1 = min(width, c0 + 2 * P)
+                nc.vector.quantize_mx(o_codes[:, c0:c1].bitcast(FP8X4), o_scales[:, start + c0 : start + c1], rounded[:, c0:c1, :].rearrange("p n t -> p (n t)"))
+            nc.sync.dma_start(out_words[:, start : start + width], o_codes[:].bitcast(I32))
 
-        turned = {}
-        for h in range(2):
-            for g in range(GROUPS):
-                turned[(h, g)] = keep.tile([P, 2, 2, 64], F32, name="turned%d_%d" % (h, g), align_bytes=64)
-
-        def turn(g, bank, terms):
-            for a in range(2):
-                for r, term in enumerate(terms[a]):
-                    nc.tensor.matmul(bank[:, a, :], term, ident[:], start=(r == 0), stop=(r == len(terms[a]) - 1), is_transpose=True)
-
-        def chunk(tile, g, a):
-            return tile[:, a * T // 2 + g * P : a * T // 2 + (g + 1) * P]
-
-        def round_turned(b, g, bank):
-            h, low = divmod(b, 2)
-            dst = turned[(h, g)][:].bitcast(BF16)[:, :, :, 64 * low : 64 * (low + 1)].rearrange("t u a (p i) -> t u a p i", i=2)
-            nc.scalar.copy(dst, bank.rearrange("t a (p u i) -> t u a p i", u=2, i=2))
-
-        def turn_block(b, bank_at):
-            banks = psum.tile([P, 4, 2, P], F32, name="banks_t%d" % b, offset=bank_at * BANK)
-            tiles = [summed[b]] if b in summed else [prods[(b, 0, 0)], prods[(b, 1, 0)]]
-            for g in range(GROUPS):
-                turn(g, banks[:, g], [[chunk(tile, g, a) for tile in tiles] for a in range(2)])
-            for g in range(GROUPS):
-                round_turned(b, g, banks[:, g])
-
-        rounded = {}
-        o_codes = [keep.tile([P, T // 2], U32, name="o_codes%d" % h, align_bytes=64) for h in range(2)]
-        o_scales = keep.tile([P, 2, T // 2], U8, name="o_scales", align_bytes=64)
-        words_out = out_1[0].rearrange("p n d -> p (n d)").bitcast(I32)
-        scales_out = out_2[0].bitcast(I32).rearrange("(h q) (a t) -> q a h t", h=2, a=2)
-
-        def turn_back(h, groups, bank_at):
-            bank = psum.tile([P, len(groups), 2, P], F32, name="bank_w%d_%d" % (h, groups[0]), offset=bank_at * BANK)
-            for i, g in enumerate(groups):
-                for u in range(2):
-                    nc.tensor.transpose(bank[:, i, u, :], turned[(h, g)][:, u].rearrange("t a p -> t (a p)"), ident[:])
-            rounded[(h, groups)] = ring.tile([P, len(groups), P, 2], F32, name="rounded", align_bytes=64, bufs=5)
-            nc.scalar.copy(rounded[(h, groups)][:], bank[:].rearrange("p g u t -> p g t u"))
-
-        def hand_on(h, groups):
-            span = slice(groups[0] * P, (groups[-1] + 1) * P)
-            nc.vector.quantize_mx(o_codes[h][:, span].bitcast(FP8X4), o_scales[:, h, span], rounded[(h, groups)][:].rearrange("p g t u -> p (g t u)").bitcast(BF16))
-
-        def store_words(h):
-            for a in range(2):
-                nc.sync.dma_start(words_out[64 * h : 64 * (h + 1), a * T // 2 : (a + 1) * T // 2], o_codes[h][:].bitcast(I32)[64 * a : 64 * (a + 1), :])
-
-        round_second(0, (0, 1), (1,))
-        quantise_hidden(E - 2, None)
-        second_layer(0, (0, 1), None, 3)
-        round_second(0, (2, 3), (2, 3))
-        second_layer(0, (2, 3), None, 4)
-        round_second(0, (4,), (4,))
-        second_layer(0, (4,), None, 5)
-        quantise_hidden(E - 1, None)
-        round_second(0, (5,), (5,))
-        second_layer(0, (5,), None, 6)
-        for b in range(1, BLOCKS):
-            for i in range(E // 2):
-                round_second(b, (2 * i, 2 * i + 1), (0, 1) if b == 1 else ())
-                second_layer(b, (2 * i, 2 * i + 1), None, 3 + i)
-                fetch_at = (piece(b * E), piece(b * E + 2))
-                if i < 2:
-                    fetch(b - 1, i, 0, T, fetch_at[i])
-            if b - 1 < ADDED_FIRST:
-                add(b - 1, [(0, T)], piece(b * E + 4))
-
-        last = BLOCKS - 1
-        turn_block(0, 0)
-        turn_block(1, 6)
-        turn_back(0, (0, 1), 0)
-        turn_back(0, (2,), 1)
-        hand_on(0, (0, 1))
-        hand_on(0, (2,))
-        store_words(0)
-        turn_block(2, 6)
-        fetch(last, 0, 0, T, None)
-        for g in range(GROUPS):
-            for a in range(2):
-                fetch(last, 1, a * T // 2 + g * P, P, None)
-            bank = psum.tile([P, 2, P], F32, name="bank_t%d" % g, offset=(2, 3, 4)[g] * BANK)
-            turn(g, bank[:], [[chunk(prods[(last, 0, 0)], g, a), prods[(last, 1, a * T // 2 + g * P)][:]] for a in range(2)])
-            round_turned(last, g, bank[:])
-            turn_back(1, (g,), (5, 0, 1)[g])
-
-        for b in range(ADDED_FIRST, last):
-            add(b, [(0, T)], None)
-        summed[last] = ring.tile([P, T], F32, name="summed", align_bytes=64, bufs=2)
-        for start in range(0, T, P):
-            nc.vector.tensor_tensor(summed[last][:, start : start + P], prods[(last, 0, 0)][:, start : start + P], prods[(last, 1, start)][:], ADD)
-        nc.sync.dma_start(out_0[last * P : (last + 1) * P, :], summed[last][:])
-        for g in range(GROUPS):
-            hand_on(1, (g,))
-        store_words(1)
-        for q in range(4):
-            a, low = divmod(q, 2)
-            eng = nc.scalar if low else nc.sync
-            eng.dma_start(scales_out[4 * low : 4 * low + 4, a], o_scales[:].bitcast(I32)[32 * q : 32 * q + 4])
+        for t in range(WHOLE):
+            fetch(t, 0, T)
+            turned_blocks = 6
+            add_by_turning(t, turned_blocks)
+            if turned_blocks * P < T:
+                add(t, 0, turned_blocks * P, T - turned_blocks * P)
+            nc.sync.dma_start(out_rows[:, t, :], summed[:, t, :])
+        for ci, (start, width) in enumerate(CHUNKS):
+            for t in range(WHOLE, 4):
+                fetch(t, start, width)
+                add(t, start, start, width)
+            (nc.sync).dma_start(out_rows[:, WHOLE:, start : start + width], summed[:, WHOLE:, start : start + width])
+            hand_on(start, width, ci == len(CHUNKS) - 1)
+        for r in range(4):
+            eng = nc.scalar if r % 2 else nc.sync
+            eng.dma_start(out_2[0].bitcast(I32)[r:16:4, :], o_scales[:].bitcast(I32)[r:P:32, :])

@@ -101,14 +101,11 @@ def tile_moe_duo_gelu_kernel(
             grouped[m] = ring.tile([P, 4 * H], BF16, name="grouped", align_bytes=64, bufs=6)
             src = raw[m].rearrange("p j (m t) -> p m j t", t=4)
             dst = grouped[m][:].rearrange("p (t m j) -> p m j t", t=4, j=4)
-            if m < SCALAR_ALONE:
-                nc.scalar.copy(dst, src)
-            else:
-                hands = 2 if m in (11, 13, 17) else (0 if m in (7, 9) else 4)
-                if hands > 0:
-                    nc.vector.tensor_copy(dst[:, :, :, :hands], src[:, :, :, :hands])
-                if hands < 4:
-                    nc.scalar.copy(dst[:, :, :, hands:], src[:, :, :, hands:])
+            hands = 0 if m < 6 or m == 9 else (2 if m % 2 else 4)
+            if hands > 0:
+                nc.vector.tensor_copy(dst[:, :, :, :hands], src[:, :, :, :hands])
+            if hands < 4:
+                nc.scalar.copy(dst[:, :, :, hands:], src[:, :, :, hands:])
 
         def load_ahead(m):
             if SLOTS <= m < 3 * E:
@@ -120,7 +117,7 @@ def tile_moe_duo_gelu_kernel(
                     nc.sync.dma_start(gate_sb[r][:], gate[r])
 
         def quantise_first(m, at):
-            codes = ring.tile([P, H], U32, name="codes", align_bytes=64, bufs=5)
+            codes = ring.tile([P, H], U32, name="codes", align_bytes=64, bufs=6)
             scales = placed([P, H], U8, "scales", "scales%d" % m, at, 5)
             cuts = {2 * E - 1: (0, 2 * P, H), 3 * E - 1: (0, P, 2 * P, H)}.get(m, (0, H))
             for c0, c1 in zip(cuts, cuts[1:]):
@@ -173,14 +170,18 @@ def tile_moe_duo_gelu_kernel(
         for m in range(SCALAR_ALONE, 3 * E + 1):
             if m < 3 * E:
                 round_first(m)
-            quantise_first(m - 1, behind(m, 0) if m % 2 == 0 and m < 12 else None)
+            for k in range(SCALAR_ALONE - 1, 3 * E):
+                if m == k + 1:
+                    quantise_first(k, behind(m, 0) if k % 2 == 1 and k < 11 else None)
             if m == SCALAR_ALONE:
                 first_layer(0, slot(m - 1) + PAD_BYTES)
                 first_layer(1, slot(m - 1) + PAD_BYTES + 2048)
-            if (m - 3) % 2 == 0 and 2 <= (m - 3) // 2 < E:
-                first_layer((m - 3) // 2, slot(m) + PAD_BYTES)
-            if (m - 6) % 2 == 0 and 0 <= (m - 6) // 2 < E:
-                quantise_hidden((m - 6) // 2, behind(m, 512))
+            for e in range(2, E):
+                if m == 2 * e + 3:
+                    first_layer(e, slot(m) + PAD_BYTES)
+            for e in range(E):
+                if m == 2 * e + 6:
+                    quantise_hidden(e, behind(m, 512))
             load_ahead(m + SLOTS - 2)
             if m > 2 * E:
                 second_layer(m - 1 - 2 * E)
@@ -191,10 +192,13 @@ def tile_moe_duo_gelu_kernel(
         summed = keep.tile([P, 4, T], F32, name="summed")
         prods = {}
 
-        def fetch(t, start, width):
+        def fetch(t, start, width, parts):
             prods[(t, start)] = ring.tile([P, 2, width], F32, name="prods%d" % width, bufs=2)
             for r, lst in enumerate((pos1_sb, pos2_sb)):
-                nc.vector.tensor_tensor(prods[(t, start)][:, r, :], y[t][:].indirect(lst[:, start // 16 : (start + width) // 16]), gate_sb[r][:, start : start + width], MULT)
+                step = width // parts if r == 1 else width
+                for c0 in range(0, width, step):
+                    cols = slice(start + c0, start + c0 + step)
+                    nc.vector.tensor_tensor(prods[(t, start)][:, r, c0 : c0 + step], y[t][:].indirect(lst[:, cols.start // 16 : cols.stop // 16]), gate_sb[r][:, cols], MULT)
 
         def add_by_turning(t, count):
             there = [psum.tile([P, P], F32, name="there%d_%d" % (t, b), offset=b * BANK) for b in range(count)]
@@ -213,33 +217,36 @@ def tile_moe_duo_gelu_kernel(
             cols = slice(start - first, start - first + width)
             nc.vector.tensor_tensor(summed[:, t, start : start + width], prods[(t, first)][:, 0, cols], prods[(t, first)][:, 1, cols], ADD)
 
-        def hand_on(start, width, on_vector):
+        def hand_on(start, width, parts):
             rounded = keep.tile([P, width, 4], BF16, name="rounded%d" % start, align_bytes=64)
-            src = summed[:, :, start : start + width].rearrange("p t (c i) -> p c t i", i=4)
-            dst = rounded[:].rearrange("p (c i) t -> p c t i", i=4)
-            if on_vector:
-                nc.vector.tensor_copy(dst, src)
-            else:
-                nc.scalar.copy(dst, src)
             o_codes = keep.tile([P, width], U32, name="o_codes%d" % start, align_bytes=64)
-            for c0 in range(0, width, 2 * P):
-                c1 = min(width, c0 + 2 * P)
-                nc.vector.quantize_mx(o_codes[:, c0:c1].bitcast(FP8X4), o_scales[:, start + c0 : start + c1], rounded[:, c0:c1, :].rearrange("p n t -> p (n t)"))
+            step = width // parts
+            for c0 in range(0, width, step):
+                src = summed[:, :, start + c0 : start + c0 + step].rearrange("p t (c i) -> p c t i", i=4)
+                dst = rounded[:, c0 : c0 + step, :].rearrange("p (c i) t -> p c t i", i=4)
+                if start + width == T:
+                    nc.vector.tensor_copy(dst, src)
+                else:
+                    nc.scalar.copy(dst, src)
+            for c0 in range(0, width, step):
+                nc.vector.quantize_mx(o_codes[:, c0 : c0 + step].bitcast(FP8X4), o_scales[:, start + c0 : start + c0 + step], rounded[:, c0 : c0 + step, :].rearrange("p n t -> p (n t)"))
             nc.sync.dma_start(out_words[:, start : start + width], o_codes[:].bitcast(I32))
 
         for t in range(WHOLE):
-            fetch(t, 0, T)
+            fetch(t, 0, T, 1)
             turned_blocks = 6
             add_by_turning(t, turned_blocks)
             if turned_blocks * P < T:
                 add(t, 0, turned_blocks * P, T - turned_blocks * P)
-            nc.sync.dma_start(out_rows[:, t, :], summed[:, t, :])
-        for ci, (start, width) in enumerate(CHUNKS):
-            for t in range(WHOLE, 4):
-                fetch(t, start, width)
-                add(t, start, start, width)
-            (nc.sync).dma_start(out_rows[:, WHOLE:, start : start + width], summed[:, WHOLE:, start : start + width])
-            hand_on(start, width, ci == len(CHUNKS) - 1)
+            if t < WHOLE - 1:
+                nc.sync.dma_start(out_rows[:, t, :], summed[:, t, :])
+        for start, width in CHUNKS:
+            parts = 2 if start + width == T else 1
+            fetch(WHOLE, start, width, parts)
+            for c0 in range(start, start + width, width // parts):
+                add(WHOLE, start, c0, width // parts)
+            nc.sync.dma_start(out_rows[:, WHOLE - 1 :, start : start + width], summed[:, WHOLE - 1 :, start : start + width])
+            hand_on(start, width, parts)
         for r in range(4):
             eng = nc.scalar if r % 2 else nc.sync
             eng.dma_start(out_2[0].bitcast(I32)[r:16:4, :], o_scales[:].bitcast(I32)[r:P:32, :])

@@ -20,14 +20,20 @@ MULT = mybir.AluOpType.mult
 ADD = mybir.AluOpType.add
 GELU = mybir.ActivationFunctionType.Gelu_apprx_tanh
 
-CHUNKS = [(0, 256), (256, 256), (512, 256)]
-WHOLE = 3
-SLOTS = 10
-RAW_BYTES = 4 * H * 4
-PAD_BYTES = 1024
-SLOT_BYTES = RAW_BYTES + 2 * PAD_BYTES
+HANDS = 4
+FIRST = 2 * E
+MATRICES = 3 * E
 BANK = 2048
-SCALAR_ALONE = 6
+
+ROOMS = 10
+MATRIX_BYTES = 4 * H * 4
+MARGIN_BYTES = 1024
+ROOM_BYTES = MATRIX_BYTES + 2 * MARGIN_BYTES
+
+SCALAR_ALONE = 7
+GELU_LAG = 3
+HIDDEN_LAG = 6
+CHUNK = 256
 
 
 def tile_moe_duo_gelu_kernel(
@@ -48,44 +54,42 @@ def tile_moe_duo_gelu_kernel(
         xw = keep.tile([P, T], I32, name="xw", align_bytes=64)
         xs = keep.tile([P, T], U8, name="xs", align_bytes=64)
         nc.vector.memset(xs[:].bitcast(I32), 0)
-        zero = arena.tile([P, (SLOTS - 1) * SLOT_BYTES // 4], F32, name="zero", align_bytes=64, offset=SLOT_BYTES)[:, 0:1]
+        for r in range(4):
+            nc.scalar.dma_start(xs[:].bitcast(I32)[r:P:32, :], x_scales[0].bitcast(I32)[r:16:4, :])
+        zero = keep.tile([P, 1], F32, name="zero")[:]
         nc.vector.memset(zero, 0.0)
         bias0 = keep.tile([P, 1], F32, name="bias0")
         nc.scalar.activation(bias0[:], zero, GELU, bias=zero)
         ident = keep.tile([P, P], F32, name="ident")
         make_identity(nc, ident[:])
 
-        nc.sync.dma_start(xw[:], x_words[0].rearrange("p t d -> p (t d)").bitcast(I32))
         nc.sync.dma_start(offs_sb[:], offs)
         nc.sync.dma_start(offs2_sb[:], offs2)
+        nc.sync.dma_start(xw[:], x_words[0].rearrange("p t d -> p (t d)").bitcast(I32))
 
         raw = {}
 
-        def slot(m):
-            return (m % SLOTS) * SLOT_BYTES
+        def on_matrix(m):
+            return (m % ROOMS) * ROOM_BYTES + MARGIN_BYTES
+
+        def on_margin(m):
+            return on_matrix(m) + (MATRIX_BYTES if m < ROOMS else -MARGIN_BYTES)
 
         def load(m):
-            source = (w1, wp)[m % 2][m // 2] if m < 2 * E else w2[m - 2 * E]
-            lead = 0 if m < SLOTS else PAD_BYTES
-            tile = arena.tile([P, (RAW_BYTES + PAD_BYTES) // 4], F32, name="raw%d" % m, align_bytes=64, offset=slot(m) + PAD_BYTES - lead)
+            source = (w1, wp)[m % 2][m // 2] if m < FIRST else w2[m - FIRST]
+            lead = 0 if m < ROOMS else MARGIN_BYTES
+            tile = arena.tile([P, (MATRIX_BYTES + MARGIN_BYTES) // 4], F32, name="raw%d" % m, align_bytes=64, offset=on_matrix(m) - lead)
             raw[m] = tile[:, lead // 4 : lead // 4 + 4 * H].rearrange("p (j c) -> p j c", j=4)
             nc.sync.dma_start(raw[m], source.rearrange("(p j) c -> p j c", j=4))
 
-        for m in range(SLOTS):
+        for m in range(ROOMS):
             load(m)
-            if m == 0:
-                for r in range(4):
-                    nc.sync.dma_start(xs[:].bitcast(I32)[r:P:32, :], x_scales[0].bitcast(I32)[r:16:4, :])
 
-        def placed(shape, dtype, tag, name, at, bufs):
-            if at is None:
-                return ring.tile(shape, dtype, name=tag, align_bytes=64, bufs=bufs)
-            return arena.tile(shape, dtype, name=name, align_bytes=64, offset=at)
-
-        gathered = {}
-        for which in range(2):
-            gathered[which] = (keep.tile([P, S], U32, name="words%d" % which, align_bytes=64), keep.tile([P, S], U8, name="bytes%d" % which, align_bytes=64))
-        for sort, table in enumerate((xw[:].bitcast(U32), xs[:])):
+        gathered = [
+            (keep.tile([P, S], U32, name="words%d" % which, align_bytes=64), keep.tile([P, S], U8, name="bytes%d" % which, align_bytes=64))
+            for which in range(2)
+        ]
+        for sort, table in ((1, xs[:]), (0, xw[:].bitcast(U32))):
             for first in range(0, S, 2 * C):
                 for which, lst in enumerate((offs_sb, offs2_sb)):
                     nc.vector.tensor_copy(gathered[which][sort][:, first : first + 2 * C], table.indirect(lst[:, first // 16 : (first + 2 * C) // 16]))
@@ -97,36 +101,39 @@ def tile_moe_duo_gelu_kernel(
         h_codes = {}
         h_scales = {}
 
-        def round_first(m):
+        def round_matrix(m):
             grouped[m] = ring.tile([P, 4 * H], BF16, name="grouped", align_bytes=64, bufs=6)
-            src = raw[m].rearrange("p j (m t) -> p m j t", t=4)
-            dst = grouped[m][:].rearrange("p (t m j) -> p m j t", t=4, j=4)
-            hands = 0 if m < 6 or m == 9 else (2 if m % 2 else 4)
-            if hands > 0:
-                nc.vector.tensor_copy(dst[:, :, :, :hands], src[:, :, :, :hands])
-            if hands < 4:
-                nc.scalar.copy(dst[:, :, :, hands:], src[:, :, :, hands:])
+            src = raw[m].rearrange("p j (c t) -> p c j t", t=HANDS)
+            dst = grouped[m][:].rearrange("p (t c j) -> p c j t", t=HANDS, j=4)
+            on_vector = 0 if m < SCALAR_ALONE else (HANDS // 2 if m % 2 else HANDS)
+            if on_vector > 0:
+                nc.vector.tensor_copy(dst[:, :, :, :on_vector], src[:, :, :, :on_vector])
+            if on_vector < HANDS:
+                nc.scalar.copy(dst[:, :, :, on_vector:], src[:, :, :, on_vector:])
 
-        def load_ahead(m):
-            if SLOTS <= m < 3 * E:
-                load(m)
-            if m == 3 * E - 1:
+        def load_after(m):
+            if ROOMS <= m + ROOMS - 2 < MATRICES:
+                load(m + ROOMS - 2)
+            if m + ROOMS - 2 == MATRICES - 1:
                 nc.sync.dma_start(pos1_sb[:], pos1)
                 nc.sync.dma_start(pos2_sb[:], pos2)
                 for r in range(2):
                     nc.sync.dma_start(gate_sb[r][:], gate[r])
 
-        def quantise_first(m, at):
+        def quantise_matrix(m):
             codes = ring.tile([P, H], U32, name="codes", align_bytes=64, bufs=6)
-            scales = placed([P, H], U8, "scales", "scales%d" % m, at, 5)
-            cuts = {2 * E - 1: (0, 2 * P, H), 3 * E - 1: (0, P, 2 * P, H)}.get(m, (0, H))
+            if SCALAR_ALONE <= m < FIRST - 1 and m % 2:
+                scales = arena.tile([P, H], U8, name="scales%d" % m, align_bytes=64, offset=on_margin(m + 1))
+            else:
+                scales = ring.tile([P, H], U8, name="scales", align_bytes=64, bufs=5)
+            cuts = {FIRST - 1: (0, 2 * P, H), MATRICES - 1: (0, P, 2 * P, H)}.get(m, (0, H))
             for c0, c1 in zip(cuts, cuts[1:]):
                 nc.vector.quantize_mx(codes[:, c0:c1].bitcast(FP8X4), scales[:, c0:c1], grouped[m][:, 4 * c0 : 4 * c1])
             quantised[m] = (codes, scales)
 
-        def first_layer(e, at):
-            hidden[e] = placed([P, C, 4], BF16, "hidden", "hidden%d" % e, at, 2)
-            banks = [psum.tile([P, 4, P], F32, name="bank_a%d_%d" % (e, half), offset=((2 * e + half) % 3) * BANK) for half in range(C // P)]
+        def first_layer(e, offset):
+            hidden[e] = arena.tile([P, C, HANDS], BF16, name="hidden%d" % e, align_bytes=64, offset=offset)
+            banks = [psum.tile([P, HANDS, P], F32, name="bank_a%d_%d" % (e, half), offset=((2 * e + half) % 3) * BANK) for half in range(C // P)]
             for hands in ([(0, 1), (2, 3)] if e == E - 1 else [(0, 1, 2, 3)]):
                 for half in range(C // P):
                     here = slice(e * C + half * P, e * C + (half + 1) * P)
@@ -134,119 +141,108 @@ def tile_moe_duo_gelu_kernel(
                         cols = slice(t * P, (t + 1) * P)
                         for which in range(2):
                             codes, scales = quantised[2 * e + which]
-                            nc.tensor.matmul_mx(banks[half][:, t, :], lhsT=codes[:, cols].bitcast(FP8X4), lhsT_scale=scales[:, cols],
-                                                rhs=gathered[which][0][:, here].bitcast(FP8X4), rhs_scale=gathered[which][1][:, here],
-                                                start=(which == 0), stop=(which == 1))
-                    if hands[-1] == 3:
-                        nc.scalar.activation(hidden[e][:, half * P : (half + 1) * P, :], banks[half][:].rearrange("p t n -> p n t"), GELU, bias=bias0[:])
+                            nc.tensor.matmul_mx(
+                                banks[half][:, t, :], lhsT=codes[:, cols].bitcast(FP8X4), lhsT_scale=scales[:, cols],
+                                rhs=gathered[which][0][:, here].bitcast(FP8X4), rhs_scale=gathered[which][1][:, here],
+                                start=(which == 0), stop=(which == 1),
+                            )
+                    if hands[-1] == HANDS - 1:
+                        nc.scalar.activation(hidden[e][:, half * P : (half + 1) * P, :], banks[half][:].rearrange("p t u -> p u t"), GELU, bias=bias0[:])
 
-        def quantise_hidden(e, at):
+        def quantise_hidden(e, m):
             h_codes[e] = keep.tile([P, C], U32, name="h_codes%d" % e, align_bytes=64)
-            h_scales[e] = placed([P, C], U8, "h_scales", "h_scales%d" % e, at, 3)
-            nc.vector.quantize_mx(h_codes[e][:].bitcast(FP8X4), h_scales[e][:], hidden[e][:].rearrange("p n t -> p (n t)"))
+            h_scales[e] = arena.tile([P, C], U8, name="h_scales%d" % e, align_bytes=64, offset=on_margin(m) + H + e % 2 * C)
+            nc.vector.quantize_mx(h_codes[e][:].bitcast(FP8X4), h_scales[e][:], hidden[e][:].rearrange("p u t -> p (u t)"))
 
-        def behind(m, at):
-            if m >= 3 * E:
-                return None
-            return slot(m) + at + (PAD_BYTES + RAW_BYTES if m < SLOTS else 0)
-
-        y = [keep.tile([P, S], F32, name="y%d" % t) for t in range(4)]
+        y = [keep.tile([P, S], F32, name="y%d" % t) for t in range(HANDS)]
 
         def second_layer(e):
-            codes, scales = quantised[2 * E + e]
-            mine = slice(e * C, (e + 1) * C)
-            for t in range(4):
-                bank = psum.tile([P, C], F32, name="bank_y%d_%d" % (e, t), offset=(3 + (4 * e + t) % 5) * BANK)
+            codes, scales = quantised[FIRST + e]
+            for t in range(HANDS):
+                bank = psum.tile([P, C], F32, name="bank_y%d_%d" % (e, t), offset=(3 + (HANDS * e + t) % 5) * BANK)
                 cols = slice(t * P, (t + 1) * P)
-                nc.tensor.matmul_mx(bank[:], lhsT=codes[:, cols].bitcast(FP8X4), lhsT_scale=scales[:, cols],
-                                    rhs=h_codes[e][:].bitcast(FP8X4), rhs_scale=h_scales[e][:], start=True, stop=True)
-                nc.scalar.copy(y[t][:, mine], bank[:])
+                nc.tensor.matmul_mx(
+                    bank[:], lhsT=codes[:, cols].bitcast(FP8X4), lhsT_scale=scales[:, cols],
+                    rhs=h_codes[e][:].bitcast(FP8X4), rhs_scale=h_scales[e][:], start=True, stop=True,
+                )
+                nc.scalar.copy(y[t][:, e * C : (e + 1) * C], bank[:])
 
         for m in range(SCALAR_ALONE):
-            round_first(m)
-            load_ahead(m + SLOTS - 2)
+            round_matrix(m)
+            load_after(m)
         for m in range(SCALAR_ALONE - 1):
-            quantise_first(m, None)
-        for m in range(SCALAR_ALONE, 3 * E + 1):
-            if m < 3 * E:
-                round_first(m)
-            for k in range(SCALAR_ALONE - 1, 3 * E):
-                if m == k + 1:
-                    quantise_first(k, behind(m, 0) if k % 2 == 1 and k < 11 else None)
-            if m == SCALAR_ALONE:
-                first_layer(0, slot(m - 1) + PAD_BYTES)
-                first_layer(1, slot(m - 1) + PAD_BYTES + 2048)
-            for e in range(2, E):
-                if m == 2 * e + 3:
-                    first_layer(e, slot(m) + PAD_BYTES)
+            quantise_matrix(m)
+        for m in range(SCALAR_ALONE, MATRICES + 1):
+            if m < MATRICES:
+                round_matrix(m)
+            quantise_matrix(m - 1)
             for e in range(E):
-                if m == 2 * e + 6:
-                    quantise_hidden(e, behind(m, 512))
-            load_ahead(m + SLOTS - 2)
-            if m > 2 * E:
-                second_layer(m - 1 - 2 * E)
+                if m == SCALAR_ALONE and 2 * e + GELU_LAG < m:
+                    first_layer(e, on_matrix(m - 1) + e * C * HANDS * 2)
+                if 2 * e + GELU_LAG == m:
+                    first_layer(e, on_matrix(m))
+            for e in range(E):
+                if max(2 * e + HIDDEN_LAG, SCALAR_ALONE + 1) == m:
+                    quantise_hidden(e, m)
+            load_after(m)
+            if m > FIRST:
+                second_layer(m - 1 - FIRST)
 
-        out_rows = out_0.rearrange("(p t) n -> p t n", t=4)
+        out_rows = out_0.rearrange("(p t) n -> p t n", t=HANDS)
         out_words = out_1[0].rearrange("p n d -> p (n d)").bitcast(I32)
         o_scales = keep.tile([P, T], U8, name="o_scales", align_bytes=64)
-        summed = keep.tile([P, 4, T], F32, name="summed")
-        prods = {}
+        summed = keep.tile([P, HANDS, T], F32, name="summed")
 
         def fetch(t, start, width, parts):
-            prods[(t, start)] = ring.tile([P, 2, width], F32, name="prods%d" % width, bufs=2)
+            prods = ring.tile([P, 2, width], F32, name="prods%d" % width, bufs=2)
             for r, lst in enumerate((pos1_sb, pos2_sb)):
                 step = width // parts if r == 1 else width
                 for c0 in range(0, width, step):
                     cols = slice(start + c0, start + c0 + step)
-                    nc.vector.tensor_tensor(prods[(t, start)][:, r, c0 : c0 + step], y[t][:].indirect(lst[:, cols.start // 16 : cols.stop // 16]), gate_sb[r][:, cols], MULT)
+                    nc.vector.tensor_tensor(prods[:, r, c0 : c0 + step], y[t][:].indirect(lst[:, cols.start // 16 : cols.stop // 16]), gate_sb[r][:, cols], MULT)
+            return prods
 
-        def add_by_turning(t, count):
-            there = [psum.tile([P, P], F32, name="there%d_%d" % (t, b), offset=b * BANK) for b in range(count)]
+        def add_by_turning(t, prods):
+            there = [psum.tile([P, P], F32, name="there%d_%d" % (t, b), offset=b * BANK) for b in range(T // P)]
             for r in range(2):
-                for b in range(count):
-                    nc.tensor.matmul(there[b][:], prods[(t, 0)][:, r, b * P : (b + 1) * P], ident[:], start=(r == 0), stop=(r == 1), is_transpose=True)
-            for first in range(0, count, 2):
-                back = psum.tile([P, 2, P], F32, name="back%d_%d" % (t, first), offset=(6 + first // 2 % 2) * BANK)
+                for b in range(T // P):
+                    nc.tensor.matmul(there[b][:], prods[:, r, b * P : (b + 1) * P], ident[:], start=(r == 0), stop=(r == 1), is_transpose=True)
+            for first in range(0, T // P, 2):
+                back = psum.tile([P, 2, P], F32, name="back%d_%d" % (t, first), offset=(T // P + first // 2 % 2) * BANK)
                 for b in range(2):
-                    turned = ring.tile([P, P], F32, name="turned", bufs=4)
+                    turned = ring.tile([P, P], F32, name="turned")
                     nc.scalar.copy(turned[:], there[first + b][:])
                     nc.tensor.transpose(back[:, b, :], turned[:], ident[:])
                 nc.scalar.copy(summed[:, t, first * P : (first + 2) * P], back[:].rearrange("p b n -> p (b n)"))
 
-        def add(t, first, start, width):
-            cols = slice(start - first, start - first + width)
-            nc.vector.tensor_tensor(summed[:, t, start : start + width], prods[(t, first)][:, 0, cols], prods[(t, first)][:, 1, cols], ADD)
-
-        def hand_on(start, width, parts):
-            rounded = keep.tile([P, width, 4], BF16, name="rounded%d" % start, align_bytes=64)
-            o_codes = keep.tile([P, width], U32, name="o_codes%d" % start, align_bytes=64)
-            step = width // parts
-            for c0 in range(0, width, step):
+        def hand_on(start, parts):
+            rounded = keep.tile([P, CHUNK, HANDS], BF16, name="rounded%d" % start, align_bytes=64)
+            o_codes = keep.tile([P, CHUNK], U32, name="o_codes%d" % start, align_bytes=64)
+            step = CHUNK // parts
+            for c0 in range(0, CHUNK, step):
                 src = summed[:, :, start + c0 : start + c0 + step].rearrange("p t (c i) -> p c t i", i=4)
                 dst = rounded[:, c0 : c0 + step, :].rearrange("p (c i) t -> p c t i", i=4)
-                if start + width == T:
+                if start + CHUNK == T:
                     nc.vector.tensor_copy(dst, src)
                 else:
                     nc.scalar.copy(dst, src)
-            for c0 in range(0, width, step):
+            for c0 in range(0, CHUNK, step):
                 nc.vector.quantize_mx(o_codes[:, c0 : c0 + step].bitcast(FP8X4), o_scales[:, start + c0 : start + c0 + step], rounded[:, c0 : c0 + step, :].rearrange("p n t -> p (n t)"))
-            nc.sync.dma_start(out_words[:, start : start + width], o_codes[:].bitcast(I32))
+            nc.sync.dma_start(out_words[:, start : start + CHUNK], o_codes[:].bitcast(I32))
 
-        for t in range(WHOLE):
-            fetch(t, 0, T, 1)
-            turned_blocks = 6
-            add_by_turning(t, turned_blocks)
-            if turned_blocks * P < T:
-                add(t, 0, turned_blocks * P, T - turned_blocks * P)
-            if t < WHOLE - 1:
+        last = HANDS - 1
+        for t in range(last):
+            add_by_turning(t, fetch(t, 0, T, 1))
+            if t < last - 1:
                 nc.sync.dma_start(out_rows[:, t, :], summed[:, t, :])
-        for start, width in CHUNKS:
-            parts = 2 if start + width == T else 1
-            fetch(WHOLE, start, width, parts)
-            for c0 in range(start, start + width, width // parts):
-                add(WHOLE, start, c0, width // parts)
-            nc.sync.dma_start(out_rows[:, WHOLE - 1 :, start : start + width], summed[:, WHOLE - 1 :, start : start + width])
-            hand_on(start, width, parts)
+        for start in range(0, T, CHUNK):
+            parts = 2 if start + CHUNK == T else 1
+            prods = fetch(last, start, CHUNK, parts)
+            for c0 in range(0, CHUNK, CHUNK // parts):
+                c1 = c0 + CHUNK // parts
+                nc.vector.tensor_tensor(summed[:, last, start + c0 : start + c1], prods[:, 0, c0:c1], prods[:, 1, c0:c1], ADD)
+            nc.sync.dma_start(out_rows[:, last - 1 :, start : start + CHUNK], summed[:, last - 1 :, start : start + CHUNK])
+            hand_on(start, parts)
         for r in range(4):
-            eng = nc.scalar if r % 2 else nc.sync
-            eng.dma_start(out_2[0].bitcast(I32)[r:16:4, :], o_scales[:].bitcast(I32)[r:P:32, :])
+            queue = nc.scalar if r % 2 else nc.sync
+            queue.dma_start(out_2[0].bitcast(I32)[r:16:4, :], o_scales[:].bitcast(I32)[r:P:32, :])

@@ -106,7 +106,10 @@ def tile_moe_duo_gelu_kernel(
             src = raw[m].rearrange("p j (c t) -> p c j t", t=HANDS)
             dst = grouped[m][:].rearrange("p (t c j) -> p c j t", t=HANDS, j=4)
             on_vector = 0 if m < SCALAR_ALONE else (HANDS // 2 if m % 2 else HANDS)
-            if on_vector > 0:
+            if m == MATRICES - 2:
+                for t in range(0, HANDS, 2):
+                    nc.vector.tensor_copy(dst[:, :, :, t : t + 2], src[:, :, :, t : t + 2])
+            elif on_vector > 0:
                 nc.vector.tensor_copy(dst[:, :, :, :on_vector], src[:, :, :, :on_vector])
             if on_vector < HANDS:
                 nc.scalar.copy(dst[:, :, :, on_vector:], src[:, :, :, on_vector:])
@@ -126,7 +129,7 @@ def tile_moe_duo_gelu_kernel(
                 scales = arena.tile([P, H], U8, name="scales%d" % m, align_bytes=64, offset=on_margin(m + 1))
             else:
                 scales = ring.tile([P, H], U8, name="scales", align_bytes=64, bufs=5)
-            cuts = {FIRST - 1: (0, 2 * P, H), MATRICES - 1: (0, P, 2 * P, H)}.get(m, (0, H))
+            cuts = {FIRST - 1: (0, 2 * P, H), MATRICES - 2: (0, 2 * P, H), MATRICES - 1: (0, P, 2 * P, H)}.get(m, (0, H))
             for c0, c1 in zip(cuts, cuts[1:]):
                 nc.vector.quantize_mx(codes[:, c0:c1].bitcast(FP8X4), scales[:, c0:c1], grouped[m][:, 4 * c0 : 4 * c1])
             quantised[m] = (codes, scales)
@@ -156,25 +159,45 @@ def tile_moe_duo_gelu_kernel(
 
         y = [keep.tile([P, S], F32, name="y%d" % t) for t in range(HANDS)]
 
+        def product(e, t, codes, scales):
+            bank = psum.tile([P, C], F32, name="bank_y%d_%d" % (e, t), offset=(3 + (HANDS * e + t) % 5) * BANK)
+            nc.tensor.matmul_mx(
+                bank[:], lhsT=codes.bitcast(FP8X4), lhsT_scale=scales,
+                rhs=h_codes[e][:].bitcast(FP8X4), rhs_scale=h_scales[e][:], start=True, stop=True,
+            )
+            nc.scalar.copy(y[t][:, e * C : (e + 1) * C], bank[:])
+
         def second_layer(e):
             codes, scales = quantised[FIRST + e]
             for t in range(HANDS):
-                bank = psum.tile([P, C], F32, name="bank_y%d_%d" % (e, t), offset=(3 + (HANDS * e + t) % 5) * BANK)
-                cols = slice(t * P, (t + 1) * P)
-                nc.tensor.matmul_mx(
-                    bank[:], lhsT=codes[:, cols].bitcast(FP8X4), lhsT_scale=scales[:, cols],
-                    rhs=h_codes[e][:].bitcast(FP8X4), rhs_scale=h_scales[e][:], start=True, stop=True,
-                )
-                nc.scalar.copy(y[t][:, e * C : (e + 1) * C], bank[:])
+                product(e, t, codes[:, t * P : (t + 1) * P], scales[:, t * P : (t + 1) * P])
 
         for m in range(SCALAR_ALONE):
             round_matrix(m)
             load_after(m)
         for m in range(SCALAR_ALONE - 1):
             quantise_matrix(m)
-        for m in range(SCALAR_ALONE, MATRICES + 1):
-            if m < MATRICES:
-                round_matrix(m)
+        def last_two_experts():
+            m, e = MATRICES - 1, E - 1
+            round_matrix(m)
+            quantise_matrix(m - 1)
+            codes, scales = quantised[m - 1]
+            product(e - 1, 0, codes[:, :P], scales[:, :P])
+            quantise_matrix(m)
+            codes, scales = quantised[m]
+            product(e, 0, codes[:, :P], scales[:, :P])
+            for t in range(1, HANDS):
+                bank = psum.tile([P, 2, C], F32, name="bank_pair%d" % t, offset=(t - 1) * BANK)
+                for u in range(2):
+                    codes, scales = quantised[m - 1 + u]
+                    nc.tensor.matmul_mx(
+                        bank[:, u, :], lhsT=codes[:, t * P : (t + 1) * P].bitcast(FP8X4), lhsT_scale=scales[:, t * P : (t + 1) * P],
+                        rhs=h_codes[e - 1 + u][:].bitcast(FP8X4), rhs_scale=h_scales[e - 1 + u][:], start=True, stop=True,
+                    )
+                nc.scalar.copy(y[t][:, (e - 1) * C :], bank[:].rearrange("p u c -> p (u c)"))
+
+        for m in range(SCALAR_ALONE, MATRICES - 1):
+            round_matrix(m)
             quantise_matrix(m - 1)
             for e in range(E):
                 if m == SCALAR_ALONE and 2 * e + GELU_LAG < m:
@@ -182,67 +205,69 @@ def tile_moe_duo_gelu_kernel(
                 if 2 * e + GELU_LAG == m:
                     first_layer(e, on_matrix(m))
             for e in range(E):
-                if max(2 * e + HIDDEN_LAG, SCALAR_ALONE + 1) == m:
+                if min(max(2 * e + HIDDEN_LAG, SCALAR_ALONE + 1), MATRICES - 4) == m:
                     quantise_hidden(e, m)
             load_after(m)
             if m > FIRST:
                 second_layer(m - 1 - FIRST)
+        last_two_experts()
 
         out_rows = out_0.rearrange("(p t) n -> p t n", t=HANDS)
         out_words = out_1[0].rearrange("p n d -> p (n d)").bitcast(I32)
         o_scales = keep.tile([P, T], U8, name="o_scales", align_bytes=64)
         summed = keep.tile([P, HANDS, T], F32, name="summed")
 
-        def fetch(t, start, width, parts):
-            prods = ring.tile([P, 2, width], F32, name="prods%d" % width, bufs=2)
+        def fetch(t, start, width):
+            prods = arena.tile([P, 2, width], F32, name="prods%d_%d" % (t, start), offset=on_matrix(ROOMS - 2 + t) + 2 * start * 4)
+            cols = slice(start, start + width)
             for r, lst in enumerate((pos1_sb, pos2_sb)):
-                step = width // parts if r == 1 else width
-                for c0 in range(0, width, step):
-                    cols = slice(start + c0, start + c0 + step)
-                    nc.vector.tensor_tensor(prods[:, r, c0 : c0 + step], y[t][:].indirect(lst[:, cols.start // 16 : cols.stop // 16]), gate_sb[r][:, cols], MULT)
+                nc.vector.tensor_tensor(prods[:, r, :], y[t][:].indirect(lst[:, cols.start // 16 : cols.stop // 16]), gate_sb[r][:, cols], MULT)
             return prods
 
-        def add_by_turning(t, prods):
-            there = [psum.tile([P, P], F32, name="there%d_%d" % (t, b), offset=b * BANK) for b in range(T // P)]
+        def add_by_turning(t, start, width):
+            prods = fetch(t, start, width)
+            blocks = width // P
+            there = [psum.tile([P, P], F32, name="there%d_%d" % (t, b), offset=b * BANK) for b in range(blocks)]
             for r in range(2):
-                for b in range(T // P):
+                for b in range(blocks):
                     nc.tensor.matmul(there[b][:], prods[:, r, b * P : (b + 1) * P], ident[:], start=(r == 0), stop=(r == 1), is_transpose=True)
-            for first in range(0, T // P, 2):
-                back = psum.tile([P, 2, P], F32, name="back%d_%d" % (t, first), offset=(T // P + first // 2 % 2) * BANK)
-                for b in range(2):
+            for first in range(0, blocks, 2):
+                count = min(2, blocks - first)
+                back = psum.tile([P, count, P], F32, name="back%d_%d" % (t, first), offset=(T // P + first // 2 % 2) * BANK)
+                for b in range(count):
                     turned = ring.tile([P, P], F32, name="turned")
                     nc.scalar.copy(turned[:], there[first + b][:])
                     nc.tensor.transpose(back[:, b, :], turned[:], ident[:])
-                nc.scalar.copy(summed[:, t, first * P : (first + 2) * P], back[:].rearrange("p b n -> p (b n)"))
+                nc.scalar.copy(summed[:, t, start + first * P : start + (first + count) * P], back[:].rearrange("p b n -> p (b n)"))
 
-        def hand_on(start, parts):
-            rounded = keep.tile([P, CHUNK, HANDS], BF16, name="rounded%d" % start, align_bytes=64)
-            o_codes = keep.tile([P, CHUNK], U32, name="o_codes%d" % start, align_bytes=64)
-            step = CHUNK // parts
-            for c0 in range(0, CHUNK, step):
-                src = summed[:, :, start + c0 : start + c0 + step].rearrange("p t (c i) -> p c t i", i=4)
-                dst = rounded[:, c0 : c0 + step, :].rearrange("p (c i) t -> p c t i", i=4)
-                if start + CHUNK == T:
-                    nc.vector.tensor_copy(dst, src)
-                else:
-                    nc.scalar.copy(dst, src)
-            for c0 in range(0, CHUNK, step):
-                nc.vector.quantize_mx(o_codes[:, c0 : c0 + step].bitcast(FP8X4), o_scales[:, start + c0 : start + c0 + step], rounded[:, c0 : c0 + step, :].rearrange("p n t -> p (n t)"))
-            nc.sync.dma_start(out_words[:, start : start + CHUNK], o_codes[:].bitcast(I32))
+        def add_on_vector(hands, start, width):
+            prods = [fetch(t, start, width) for t in hands]
+            for t, both in zip(hands, prods):
+                nc.vector.tensor_tensor(summed[:, t, start : start + width], both[:, 0, :], both[:, 1, :], ADD)
 
-        last = HANDS - 1
-        for t in range(last):
-            add_by_turning(t, fetch(t, 0, T, 1))
-            if t < last - 1:
-                nc.sync.dma_start(out_rows[:, t, :], summed[:, t, :])
-        for start in range(0, T, CHUNK):
-            parts = 2 if start + CHUNK == T else 1
-            prods = fetch(last, start, CHUNK, parts)
-            for c0 in range(0, CHUNK, CHUNK // parts):
-                c1 = c0 + CHUNK // parts
-                nc.vector.tensor_tensor(summed[:, last, start + c0 : start + c1], prods[:, 0, c0:c1], prods[:, 1, c0:c1], ADD)
-            nc.sync.dma_start(out_rows[:, last - 1 :, start : start + CHUNK], summed[:, last - 1 :, start : start + CHUNK])
-            hand_on(start, parts)
+        def hand_on(start, pieces, copy):
+            total = sum(width for width, offset in pieces)
+            nc.sync.dma_start(out_rows[:, 1:, start : start + total], summed[:, 1:, start : start + total])
+            o_codes = keep.tile([P, total], U32, name="o_codes%d" % start, align_bytes=64)
+            at = start
+            for width, offset in pieces:
+                rounded = arena.tile([P, width, HANDS], BF16, name="rounded%d" % at, align_bytes=64, offset=on_matrix(ROOMS + 2) + offset * 8)
+                src = summed[:, :, at : at + width].rearrange("p t (c i) -> p c t i", i=4)
+                copy(rounded[:].rearrange("p (c i) t -> p c t i", i=4), src)
+                nc.vector.quantize_mx(o_codes[:, at - start : at - start + width].bitcast(FP8X4), o_scales[:, at : at + width], rounded[:].rearrange("p n t -> p (n t)"))
+                at += width
+            nc.sync.dma_start(out_words[:, start:at], o_codes[:].bitcast(I32))
+
+        add_by_turning(0, 0, T)
+        nc.sync.dma_start(out_rows[:, 0, :], summed[:, 0, :])
+        add_by_turning(2, 0, 3 * P)
+        add_by_turning(1, 0, T)
+        add_on_vector((3,), 0, 3 * P)
+        hand_on(0, ((P, 0), (2 * P, P)), nc.scalar.copy)
+        add_on_vector((2, 3), 3 * P, 2 * P)
+        hand_on(3 * P, ((2 * P, 3 * P),), nc.scalar.copy)
+        add_on_vector((2, 3), 5 * P, P)
+        hand_on(5 * P, ((P, P),), nc.vector.tensor_copy)
         for r in range(4):
             queue = nc.scalar if r % 2 else nc.sync
             queue.dma_start(out_2[0].bitcast(I32)[r:16:4, :], o_scales[:].bitcast(I32)[r:P:32, :])

@@ -33,7 +33,9 @@ ROOM_BYTES = MATRIX_BYTES + 2 * MARGIN_BYTES
 SCALAR_ALONE = 7
 GELU_LAG = 3
 HIDDEN_LAG = 6
-CHUNK = 256
+HIDDEN_LAST = MATRICES - 4
+CHUNKS = ((0, 3 * P), (3 * P, 2 * P), (5 * P, P))
+TURNED = 5 * P
 
 
 def tile_moe_duo_gelu_kernel(
@@ -172,11 +174,6 @@ def tile_moe_duo_gelu_kernel(
             for t in range(HANDS):
                 product(e, t, codes[:, t * P : (t + 1) * P], scales[:, t * P : (t + 1) * P])
 
-        for m in range(SCALAR_ALONE):
-            round_matrix(m)
-            load_after(m)
-        for m in range(SCALAR_ALONE - 1):
-            quantise_matrix(m)
         def last_two_experts():
             m, e = MATRICES - 1, E - 1
             round_matrix(m)
@@ -196,6 +193,11 @@ def tile_moe_duo_gelu_kernel(
                     )
                 nc.scalar.copy(y[t][:, (e - 1) * C :], bank[:].rearrange("p u c -> p (u c)"))
 
+        for m in range(SCALAR_ALONE):
+            round_matrix(m)
+            load_after(m)
+        for m in range(SCALAR_ALONE - 1):
+            quantise_matrix(m)
         for m in range(SCALAR_ALONE, MATRICES - 1):
             round_matrix(m)
             quantise_matrix(m - 1)
@@ -205,7 +207,7 @@ def tile_moe_duo_gelu_kernel(
                 if 2 * e + GELU_LAG == m:
                     first_layer(e, on_matrix(m))
             for e in range(E):
-                if min(max(2 * e + HIDDEN_LAG, SCALAR_ALONE + 1), MATRICES - 4) == m:
+                if min(max(2 * e + HIDDEN_LAG, SCALAR_ALONE + 1), HIDDEN_LAST) == m:
                     quantise_hidden(e, m)
             load_after(m)
             if m > FIRST:
@@ -224,8 +226,8 @@ def tile_moe_duo_gelu_kernel(
                 nc.vector.tensor_tensor(prods[:, r, :], y[t][:].indirect(lst[:, cols.start // 16 : cols.stop // 16]), gate_sb[r][:, cols], MULT)
             return prods
 
-        def add_by_turning(t, start, width):
-            prods = fetch(t, start, width)
+        def add_by_turning(t, width):
+            prods = fetch(t, 0, width)
             blocks = width // P
             there = [psum.tile([P, P], F32, name="there%d_%d" % (t, b), offset=b * BANK) for b in range(blocks)]
             for r in range(2):
@@ -238,36 +240,37 @@ def tile_moe_duo_gelu_kernel(
                     turned = ring.tile([P, P], F32, name="turned")
                     nc.scalar.copy(turned[:], there[first + b][:])
                     nc.tensor.transpose(back[:, b, :], turned[:], ident[:])
-                nc.scalar.copy(summed[:, t, start + first * P : start + (first + count) * P], back[:].rearrange("p b n -> p (b n)"))
+                nc.scalar.copy(summed[:, t, first * P : (first + count) * P], back[:].rearrange("p b n -> p (b n)"))
 
         def add_on_vector(hands, start, width):
             prods = [fetch(t, start, width) for t in hands]
             for t, both in zip(hands, prods):
                 nc.vector.tensor_tensor(summed[:, t, start : start + width], both[:, 0, :], both[:, 1, :], ADD)
 
-        def hand_on(start, pieces, copy):
-            total = sum(width for width, offset in pieces)
-            nc.sync.dma_start(out_rows[:, 1:, start : start + total], summed[:, 1:, start : start + total])
-            o_codes = keep.tile([P, total], U32, name="o_codes%d" % start, align_bytes=64)
-            at = start
-            for width, offset in pieces:
-                rounded = arena.tile([P, width, HANDS], BF16, name="rounded%d" % at, align_bytes=64, offset=on_matrix(ROOMS + 2) + offset * 8)
-                src = summed[:, :, at : at + width].rearrange("p t (c i) -> p c t i", i=4)
-                copy(rounded[:].rearrange("p (c i) t -> p c t i", i=4), src)
-                nc.vector.quantize_mx(o_codes[:, at - start : at - start + width].bitcast(FP8X4), o_scales[:, at : at + width], rounded[:].rearrange("p n t -> p (n t)"))
-                at += width
-            nc.sync.dma_start(out_words[:, start:at], o_codes[:].bitcast(I32))
+        def hand_on(start, width):
+            nc.sync.dma_start(out_rows[:, 1:, start : start + width], summed[:, 1:, start : start + width])
+            o_codes = keep.tile([P, width], U32, name="o_codes%d" % start, align_bytes=64)
+            cuts = (start, start + P, start + width) if width == 3 * P else (start, start + width)
+            last = start + width == T
+            for c0, c1 in zip(cuts, cuts[1:]):
+                place = P if last else c0
+                rounded = arena.tile([P, c1 - c0, HANDS], BF16, name="rounded%d" % c0, align_bytes=64, offset=on_matrix(FIRST) + place * HANDS * 2)
+                src = summed[:, :, c0:c1].rearrange("p t (c i) -> p c t i", i=4)
+                dst = rounded[:].rearrange("p (c i) t -> p c t i", i=4)
+                if last:
+                    nc.vector.tensor_copy(dst, src)
+                else:
+                    nc.scalar.copy(dst, src)
+                nc.vector.quantize_mx(o_codes[:, c0 - start : c1 - start].bitcast(FP8X4), o_scales[:, c0:c1], rounded[:].rearrange("p n t -> p (n t)"))
+            nc.sync.dma_start(out_words[:, start : start + width], o_codes[:].bitcast(I32))
 
-        add_by_turning(0, 0, T)
+        add_by_turning(0, T)
         nc.sync.dma_start(out_rows[:, 0, :], summed[:, 0, :])
-        add_by_turning(2, 0, 3 * P)
-        add_by_turning(1, 0, T)
-        add_on_vector((3,), 0, 3 * P)
-        hand_on(0, ((P, 0), (2 * P, P)), nc.scalar.copy)
-        add_on_vector((2, 3), 3 * P, 2 * P)
-        hand_on(3 * P, ((2 * P, 3 * P),), nc.scalar.copy)
-        add_on_vector((2, 3), 5 * P, P)
-        hand_on(5 * P, ((P, P),), nc.vector.tensor_copy)
+        add_by_turning(2, TURNED)
+        add_by_turning(1, T)
+        for start, width in CHUNKS:
+            add_on_vector((3,) if start < TURNED else (2, 3), start, width)
+            hand_on(start, width)
         for r in range(4):
             queue = nc.scalar if r % 2 else nc.sync
             queue.dma_start(out_2[0].bitcast(I32)[r:16:4, :], o_scales[:].bitcast(I32)[r:P:32, :])

@@ -21,6 +21,7 @@ ADD = mybir.AluOpType.add
 GELU = mybir.ActivationFunctionType.Gelu_apprx_tanh
 
 HANDS = 4
+WINDOW = 2048
 FIRST = 2 * E
 MATRICES = 3 * E
 BANK = 2048
@@ -53,11 +54,13 @@ def tile_moe_duo_gelu_kernel(
         offs2_sb = lists.tile([P, S // 16], U16, name="offs2_sb")
         pos1_sb = lists.tile([P, T // 16], U16, name="pos1_sb")
         pos2_sb = lists.tile([P, T // 16], U16, name="pos2_sb")
-        xw = keep.tile([P, T], I32, name="xw", align_bytes=64)
-        xs = keep.tile([P, T], U8, name="xs", align_bytes=64)
-        nc.vector.memset(xs[:].bitcast(I32), 0)
+        xw = keep.tile([P, WINDOW], I32, name="xw", align_bytes=64)
+        xs = keep.tile([P, WINDOW], U8, name="xs", align_bytes=64)
+        nc.gpsimd.memset(xs[:, :T].bitcast(I32), 0)
+        nc.vector.memset(xs[:, T:].bitcast(I32), 0)
+        nc.vector.memset(xw[:, T:], 0)
         for r in range(4):
-            nc.scalar.dma_start(xs[:].bitcast(I32)[r:P:32, :], x_scales[0].bitcast(I32)[r:16:4, :])
+            nc.scalar.dma_start(xs[:, :T].bitcast(I32)[r:P:32, :], x_scales[0].bitcast(I32)[r:16:4, :])
         zero = keep.tile([P, 1], F32, name="zero")[:]
         nc.vector.memset(zero, 0.0)
         bias0 = keep.tile([P, 1], F32, name="bias0")
@@ -67,7 +70,7 @@ def tile_moe_duo_gelu_kernel(
 
         nc.sync.dma_start(offs_sb[:], offs)
         nc.sync.dma_start(offs2_sb[:], offs2)
-        nc.sync.dma_start(xw[:], x_words[0].rearrange("p t d -> p (t d)").bitcast(I32))
+        nc.sync.dma_start(xw[:, :T], x_words[0].rearrange("p t d -> p (t d)").bitcast(I32))
 
         raw = {}
 
@@ -92,9 +95,8 @@ def tile_moe_duo_gelu_kernel(
             for which in range(2)
         ]
         for sort, table in ((1, xs[:]), (0, xw[:].bitcast(U32))):
-            for first in range(0, S, 2 * C):
-                for which, lst in enumerate((offs_sb, offs2_sb)):
-                    nc.vector.tensor_copy(gathered[which][sort][:, first : first + 2 * C], table.indirect(lst[:, first // 16 : (first + 2 * C) // 16]))
+            for which, lst in enumerate((offs_sb, offs2_sb)):
+                nc.vector.tensor_copy(gathered[which][sort][:], table.indirect(lst[:]))
 
         gate_sb = [keep.tile([P, T], F32, name="gate%d" % r) for r in range(2)]
         grouped = {}

@@ -19,6 +19,7 @@ FP8X4 = mybir.dt.float8_e4m3fn_x4
 MULT = mybir.AluOpType.mult
 ADD = mybir.AluOpType.add
 GELU = mybir.ActivationFunctionType.Gelu_apprx_tanh
+COPY = mybir.ActivationFunctionType.Copy
 
 HANDS = 4
 WINDOW = 2048
@@ -35,8 +36,9 @@ SCALAR_ALONE = 7
 GELU_LAG = 3
 HIDDEN_LAG = 6
 HIDDEN_LAST = MATRICES - 4
-CHUNKS = ((0, 3 * P), (3 * P, 2 * P), (5 * P, P))
-TURNED = 5 * P
+CHUNKS = ((0, 2 * P), (2 * P, 2 * P), (4 * P, P))
+BLOCKS = 5
+SHARED = BLOCKS * P
 
 
 def tile_moe_duo_gelu_kernel(
@@ -90,6 +92,14 @@ def tile_moe_duo_gelu_kernel(
         for m in range(ROOMS):
             load(m)
 
+        gate1_rows = keep.tile([P, P], F32, name="gate1_rows")
+        nc.gpsimd.memset(gate1_rows[:], 0.0)
+        nc.sync.dma_start(gate1_rows[:BLOCKS, :], gate[0, 0:1, :SHARED].rearrange("o (b p) -> (o b) p", p=P))
+        gate1_turned = psum.tile([P, P], F32, name="gate1_turned", offset=7 * BANK)
+        nc.tensor.transpose(gate1_turned[:], gate1_rows[:], ident[:])
+        gate1 = keep.tile([P, BLOCKS], F32, name="gate1")
+        nc.scalar.copy(gate1[:], gate1_turned[:, :BLOCKS])
+
         gathered = [
             (keep.tile([P, S], U32, name="words%d" % which, align_bytes=64), keep.tile([P, S], U8, name="bytes%d" % which, align_bytes=64))
             for which in range(2)
@@ -98,7 +108,8 @@ def tile_moe_duo_gelu_kernel(
             for which, lst in enumerate((offs_sb, offs2_sb)):
                 nc.vector.tensor_copy(gathered[which][sort][:], table.indirect(lst[:]))
 
-        gate_sb = [keep.tile([P, T], F32, name="gate%d" % r) for r in range(2)]
+        gate2 = keep.tile([P, T], F32, name="gate2")
+        gate1_last = keep.tile([P, T - SHARED], F32, name="gate1_last")
         grouped = {}
         quantised = {}
         hidden = {}
@@ -122,10 +133,10 @@ def tile_moe_duo_gelu_kernel(
             if ROOMS <= m + ROOMS - 2 < MATRICES:
                 load(m + ROOMS - 2)
             if m + ROOMS - 2 == MATRICES - 1:
-                nc.sync.dma_start(pos1_sb[:], pos1)
                 nc.sync.dma_start(pos2_sb[:], pos2)
-                for r in range(2):
-                    nc.sync.dma_start(gate_sb[r][:], gate[r])
+                nc.sync.dma_start(gate2[:], gate[1])
+                nc.sync.dma_start(pos1_sb[:], pos1)
+                nc.sync.dma_start(gate1_last[:], gate[0, :, SHARED:])
 
         def quantise_matrix(m):
             codes = ring.tile([P, H], U32, name="codes", align_bytes=64, bufs=6)
@@ -221,58 +232,44 @@ def tile_moe_duo_gelu_kernel(
         o_scales = keep.tile([P, T], U8, name="o_scales", align_bytes=64)
         summed = keep.tile([P, HANDS, T], F32, name="summed")
 
-        def fetch(t, start, width):
-            prods = arena.tile([P, 2, width], F32, name="prods%d_%d" % (t, start), offset=on_matrix(ROOMS - 2 + t) + 2 * start * 4)
+        second = keep.tile([P, HANDS, T], F32, name="second")
+        for t in range(HANDS):
+            nc.vector.tensor_tensor(second[:, t, :], y[t][:].indirect(pos2_sb[:]), gate2[:], MULT)
+        first_last = keep.tile([P, HANDS, T - SHARED], F32, name="first_last")
+        for t in range(HANDS):
+            nc.vector.tensor_tensor(first_last[:, t, :], y[t][:].indirect(pos1_sb[:, SHARED // 16 :]), gate1_last[:], MULT)
+        nc.vector.tensor_tensor(summed[:, :, SHARED:], first_last[:], second[:, :, SHARED:], ADD)
+
+        def hand_on(start, width, round_copy):
             cols = slice(start, start + width)
-            for r, lst in enumerate((pos1_sb, pos2_sb)):
-                nc.vector.tensor_tensor(prods[:, r, :], y[t][:].indirect(lst[:, cols.start // 16 : cols.stop // 16]), gate_sb[r][:, cols], MULT)
-            return prods
-
-        def add_by_turning(t, width):
-            prods = fetch(t, 0, width)
-            blocks = width // P
-            there = [psum.tile([P, P], F32, name="there%d_%d" % (t, b), offset=b * BANK) for b in range(blocks)]
-            for r in range(2):
-                for b in range(blocks):
-                    nc.tensor.matmul(there[b][:], prods[:, r, b * P : (b + 1) * P], ident[:], start=(r == 0), stop=(r == 1), is_transpose=True)
-            for first in range(0, blocks, 2):
-                count = min(2, blocks - first)
-                back = psum.tile([P, count, P], F32, name="back%d_%d" % (t, first), offset=(T // P + first // 2 % 2) * BANK)
-                for b in range(count):
-                    turned = ring.tile([P, P], F32, name="turned")
-                    nc.scalar.copy(turned[:], there[first + b][:])
-                    nc.tensor.transpose(back[:, b, :], turned[:], ident[:])
-                nc.scalar.copy(summed[:, t, first * P : (first + count) * P], back[:].rearrange("p b n -> p (b n)"))
-
-        def add_on_vector(hands, start, width):
-            prods = [fetch(t, start, width) for t in hands]
-            for t, both in zip(hands, prods):
-                nc.vector.tensor_tensor(summed[:, t, start : start + width], both[:, 0, :], both[:, 1, :], ADD)
-
-        def hand_on(start, width):
-            nc.sync.dma_start(out_rows[:, 1:, start : start + width], summed[:, 1:, start : start + width])
+            nc.sync.dma_start(out_rows[:, :, cols], summed[:, :, cols])
+            rounded = arena.tile([P, width, HANDS], BF16, name="rounded%d" % start, align_bytes=64, offset=on_matrix(FIRST) + start * HANDS * 2)
+            round_copy(rounded[:].rearrange("p (c i) t -> p c t i", i=4), summed[:, :, cols].rearrange("p t (c i) -> p c t i", i=4))
             o_codes = keep.tile([P, width], U32, name="o_codes%d" % start, align_bytes=64)
-            cuts = (start, start + P, start + width) if width == 3 * P else (start, start + width)
-            last = start + width == T
-            for c0, c1 in zip(cuts, cuts[1:]):
-                place = P if last else c0
-                rounded = arena.tile([P, c1 - c0, HANDS], BF16, name="rounded%d" % c0, align_bytes=64, offset=on_matrix(FIRST) + place * HANDS * 2)
-                src = summed[:, :, c0:c1].rearrange("p t (c i) -> p c t i", i=4)
-                dst = rounded[:].rearrange("p (c i) t -> p c t i", i=4)
-                if last:
-                    nc.vector.tensor_copy(dst, src)
-                else:
-                    nc.scalar.copy(dst, src)
-                nc.vector.quantize_mx(o_codes[:, c0 - start : c1 - start].bitcast(FP8X4), o_scales[:, c0:c1], rounded[:].rearrange("p n t -> p (n t)"))
-            nc.sync.dma_start(out_words[:, start : start + width], o_codes[:].bitcast(I32))
+            nc.vector.quantize_mx(o_codes[:].bitcast(FP8X4), o_scales[:, cols], rounded[:].rearrange("p n t -> p (n t)"))
+            nc.sync.dma_start(out_words[:, cols], o_codes[:].bitcast(I32))
 
-        add_by_turning(0, T)
-        nc.sync.dma_start(out_rows[:, 0, :], summed[:, 0, :])
-        add_by_turning(2, TURNED)
-        add_by_turning(1, T)
-        for start, width in CHUNKS:
-            add_on_vector((3,) if start < TURNED else (2, 3), start, width)
-            hand_on(start, width)
+        for chunk, (start, width) in enumerate(CHUNKS):
+            first = arena.tile([P, HANDS, width], F32, name="first%d" % start, offset=on_matrix(8 + chunk))
+            for t in range(HANDS):
+                nc.scalar.activation(first[:, t, :], y[t][:].indirect(pos1_sb[:, start // 16 : (start + width) // 16]), COPY)
+            blocks = range(start // P, (start + width) // P)
+            there = {}
+            for b in blocks:
+                there[b] = psum.tile([P, HANDS, P], F32, name="there%d" % b, offset=b % 4 * BANK)
+            for t in range(HANDS):
+                for b in blocks:
+                    nc.tensor.transpose(there[b][:, t, :], first[:, t, b * P - start : (b + 1) * P - start], ident[:])
+            for b in blocks:
+                gated = arena.tile([P, HANDS, P], F32, name="gated%d" % b, offset=on_matrix(8 + chunk) + (2 + b % 2) * HANDS * P * 4)
+                nc.scalar.activation(gated[:], there[b][:], COPY, scale=gate1[:, b : b + 1])
+                back = psum.tile([P, HANDS, P], F32, name="back%d" % b, offset=(4 + b % 4) * BANK)
+                for t in range(HANDS):
+                    nc.tensor.transpose(back[:, t, :], gated[:, t, :], ident[:])
+                cols = slice(b * P, (b + 1) * P)
+                nc.vector.tensor_tensor(summed[:, :, cols], back[:], second[:, :, cols], ADD)
+            hand_on(start, width, nc.scalar.copy if chunk == 1 else nc.vector.tensor_copy)
+        hand_on(SHARED, T - SHARED, nc.scalar.copy)
         for r in range(4):
             queue = nc.scalar if r % 2 else nc.sync
             queue.dma_start(out_2[0].bitcast(I32)[r:16:4, :], o_scales[:].bitcast(I32)[r:P:32, :])

@@ -230,46 +230,77 @@ def tile_moe_duo_gelu_kernel(
         out_rows = out_0.rearrange("(p t) n -> p t n", t=HANDS)
         out_words = out_1[0].rearrange("p n d -> p (n d)").bitcast(I32)
         o_scales = keep.tile([P, T], U8, name="o_scales", align_bytes=64)
-        summed = keep.tile([P, HANDS, T], F32, name="summed")
 
         second = keep.tile([P, HANDS, T], F32, name="second")
         for t in range(HANDS):
             nc.vector.tensor_tensor(second[:, t, :], y[t][:].indirect(pos2_sb[:]), gate2[:], MULT)
-        first_last = keep.tile([P, HANDS, T - SHARED], F32, name="first_last")
-        for t in range(HANDS):
-            nc.vector.tensor_tensor(first_last[:, t, :], y[t][:].indirect(pos1_sb[:, SHARED // 16 :]), gate1_last[:], MULT)
-        nc.vector.tensor_tensor(summed[:, :, SHARED:], first_last[:], second[:, :, SHARED:], ADD)
 
-        def hand_on(start, width, round_copy):
-            cols = slice(start, start + width)
-            nc.sync.dma_start(out_rows[:, :, cols], summed[:, :, cols])
-            rounded = arena.tile([P, width, HANDS], BF16, name="rounded%d" % start, align_bytes=64, offset=on_matrix(FIRST) + start * HANDS * 2)
-            round_copy(rounded[:].rearrange("p (c i) t -> p c t i", i=4), summed[:, :, cols].rearrange("p t (c i) -> p c t i", i=4))
-            o_codes = keep.tile([P, width], U32, name="o_codes%d" % start, align_bytes=64)
-            nc.vector.quantize_mx(o_codes[:].bitcast(FP8X4), o_scales[:, cols], rounded[:].rearrange("p n t -> p (n t)"))
-            nc.sync.dma_start(out_words[:, cols], o_codes[:].bitcast(I32))
+        summed = {}
+        rounded = {}
+        there = {}
 
-        for chunk, (start, width) in enumerate(CHUNKS):
-            first = arena.tile([P, HANDS, width], F32, name="first%d" % start, offset=on_matrix(8 + chunk))
+        def on_gated(b):
+            return on_matrix(8 + b // 2) + (2 + b % 2) * HANDS * P * 4
+
+        def fetch_and_turn(start, width):
+            first = arena.tile([P, HANDS, width], F32, name="first%d" % start, offset=on_matrix(8 + start // (2 * P)))
             for t in range(HANDS):
                 nc.scalar.activation(first[:, t, :], y[t][:].indirect(pos1_sb[:, start // 16 : (start + width) // 16]), COPY)
             blocks = range(start // P, (start + width) // P)
-            there = {}
             for b in blocks:
                 there[b] = psum.tile([P, HANDS, P], F32, name="there%d" % b, offset=b % 4 * BANK)
             for t in range(HANDS):
                 for b in blocks:
                     nc.tensor.transpose(there[b][:, t, :], first[:, t, b * P - start : (b + 1) * P - start], ident[:])
-            for b in blocks:
-                gated = arena.tile([P, HANDS, P], F32, name="gated%d" % b, offset=on_matrix(8 + chunk) + (2 + b % 2) * HANDS * P * 4)
-                nc.scalar.activation(gated[:], there[b][:], COPY, scale=gate1[:, b : b + 1])
-                back = psum.tile([P, HANDS, P], F32, name="back%d" % b, offset=(4 + b % 4) * BANK)
-                for t in range(HANDS):
-                    nc.tensor.transpose(back[:, t, :], gated[:, t, :], ident[:])
-                cols = slice(b * P, (b + 1) * P)
-                nc.vector.tensor_tensor(summed[:, :, cols], back[:], second[:, :, cols], ADD)
-            hand_on(start, width, nc.scalar.copy if chunk == 1 else nc.vector.tensor_copy)
-        hand_on(SHARED, T - SHARED, nc.scalar.copy)
+            summed[start] = keep.tile([P, HANDS, width], F32, name="summed%d" % start)
+
+        def gate_and_add(start, b):
+            gated = arena.tile([P, HANDS, P], F32, name="gated%d" % b, offset=on_gated(b))
+            nc.scalar.activation(gated[:], there[b][:], COPY, scale=gate1[:, b : b + 1])
+            back = psum.tile([P, HANDS, P], F32, name="back%d" % b, offset=(4 + b % 4) * BANK)
+            for t in range(HANDS):
+                nc.tensor.transpose(back[:, t, :], gated[:, t, :], ident[:])
+            nc.vector.tensor_tensor(summed[start][:, :, b * P - start : (b + 1) * P - start], back[:], second[:, :, b * P : (b + 1) * P], ADD)
+
+        def store_sum(start, width):
+            nc.sync.dma_start(out_rows[:, :, start : start + width], summed[start][:])
+
+        def round_sum(tile, sums, copy_on_engine):
+            copy_on_engine(tile.rearrange("p (c i) t -> p c t i", i=4), sums.rearrange("p t (c i) -> p c t i", i=4))
+
+        def quantise_sum(start):
+            o_codes = keep.tile([P, 2 * P], U32, name="o_codes%d" % start, align_bytes=64)
+            nc.vector.quantize_mx(o_codes[:].bitcast(FP8X4), o_scales[:, start : start + 2 * P], rounded[start][:].rearrange("p n t -> p (n t)"))
+            nc.sync.dma_start(out_words[:, start : start + 2 * P], o_codes[:].bitcast(I32))
+
+        early, middle, late = CHUNKS
+        alone = (SHARED, T - SHARED)
+        fetch_and_turn(*early)
+        gate_and_add(early[0], 0)
+        gate_and_add(early[0], 1)
+        store_sum(*early)
+        first_last = arena.tile([P, HANDS, T - SHARED], F32, name="first_last", offset=on_gated(1))
+        for t in range(HANDS):
+            nc.vector.tensor_tensor(first_last[:, t, :], y[t][:].indirect(pos1_sb[:, SHARED // 16 :]), gate1_last[:], MULT)
+        summed[SHARED] = keep.tile([P, HANDS, T - SHARED], F32, name="summed_alone")
+        nc.vector.tensor_tensor(summed[SHARED][:], first_last[:], second[:, :, SHARED:], ADD)
+        store_sum(*alone)
+        fetch_and_turn(*middle)
+        fetch_and_turn(*late)
+        gate_and_add(middle[0], 2)
+        gate_and_add(middle[0], 3)
+        store_sum(*middle)
+        gate_and_add(late[0], 4)
+        store_sum(*late)
+        for start, offset in ((early[0], on_gated(2)), (middle[0], on_gated(4)), (late[0], on_gated(3))):
+            rounded[start] = arena.tile([P, 2 * P, HANDS], BF16, name="rounded%d" % start, align_bytes=64, offset=offset)
+        round_sum(rounded[early[0]][:], summed[early[0]][:], nc.scalar.copy)
+        round_sum(rounded[late[0]][:, P:, :], summed[SHARED][:], nc.scalar.copy)
+        round_sum(rounded[middle[0]][:, :P, :], summed[middle[0]][:, :, :P], nc.scalar.copy)
+        round_sum(rounded[middle[0]][:, P:, :], summed[middle[0]][:, :, P:], nc.vector.tensor_copy)
+        round_sum(rounded[late[0]][:, :P, :], summed[late[0]][:], nc.vector.tensor_copy)
+        for start, width in CHUNKS:
+            quantise_sum(start)
         for r in range(4):
             queue = nc.scalar if r % 2 else nc.sync
             queue.dma_start(out_2[0].bitcast(I32)[r:16:4, :], o_scales[:].bitcast(I32)[r:P:32, :])

@@ -235,72 +235,76 @@ def tile_moe_duo_gelu_kernel(
         for t in range(HANDS):
             nc.vector.tensor_tensor(second[:, t, :], y[t][:].indirect(pos2_sb[:]), gate2[:], MULT)
 
-        summed = {}
-        rounded = {}
+        block_bytes = HANDS * P * 4
         there = {}
+        summed = {}
 
-        def on_gated(b):
-            return on_matrix(8 + b // 2) + (2 + b % 2) * HANDS * P * 4
+        def on_gated(b, side=0):
+            return (3 * b + 1) * block_bytes + side * (block_bytes - 64)
 
-        def fetch_and_turn(start, width):
-            first = arena.tile([P, HANDS, width], F32, name="first%d" % start, offset=on_matrix(8 + start // (2 * P)))
-            for t in range(HANDS):
-                nc.scalar.activation(first[:, t, :], y[t][:].indirect(pos1_sb[:, start // 16 : (start + width) // 16]), COPY)
-            blocks = range(start // P, (start + width) // P)
-            for b in blocks:
-                there[b] = psum.tile([P, HANDS, P], F32, name="there%d" % b, offset=b % 4 * BANK)
-            for t in range(HANDS):
-                for b in blocks:
-                    nc.tensor.transpose(there[b][:, t, :], first[:, t, b * P - start : (b + 1) * P - start], ident[:])
-            summed[start] = keep.tile([P, HANDS, width], F32, name="summed%d" % start)
+        def fetch(tile, t, blocks):
+            nc.scalar.activation(tile, y[t][:].indirect(pos1_sb[:, blocks[0] * P // 16 : (blocks[-1] + 1) * P // 16]), COPY)
+            for i, b in enumerate(blocks):
+                if t == 0:
+                    there[b] = psum.tile([P, HANDS, P], F32, name="there%d" % b, offset=b % 4 * BANK)
+                nc.tensor.transpose(there[b][:, t, :], tile[:, i * P : (i + 1) * P], ident[:])
 
-        def gate_and_add(start, b):
+        def gate_and_add(b, sums):
             gated = arena.tile([P, HANDS, P], F32, name="gated%d" % b, offset=on_gated(b))
             nc.scalar.activation(gated[:], there[b][:], COPY, scale=gate1[:, b : b + 1])
             back = psum.tile([P, HANDS, P], F32, name="back%d" % b, offset=(4 + b % 4) * BANK)
             for t in range(HANDS):
                 nc.tensor.transpose(back[:, t, :], gated[:, t, :], ident[:])
-            nc.vector.tensor_tensor(summed[start][:, :, b * P - start : (b + 1) * P - start], back[:], second[:, :, b * P : (b + 1) * P], ADD)
-
-        def store_sum(start, width):
-            nc.sync.dma_start(out_rows[:, :, start : start + width], summed[start][:])
+            nc.vector.tensor_tensor(sums, back[:], second[:, :, b * P : (b + 1) * P], ADD)
 
         def round_sum(tile, sums, copy_on_engine):
             copy_on_engine(tile.rearrange("p (c i) t -> p c t i", i=4), sums.rearrange("p t (c i) -> p c t i", i=4))
 
-        def quantise_sum(start):
-            o_codes = keep.tile([P, 2 * P], U32, name="o_codes%d" % start, align_bytes=64)
-            nc.vector.quantize_mx(o_codes[:].bitcast(FP8X4), o_scales[:, start : start + 2 * P], rounded[start][:].rearrange("p n t -> p (n t)"))
-            nc.sync.dma_start(out_words[:, start : start + 2 * P], o_codes[:].bitcast(I32))
+        def quantise_sum(codes, pair):
+            nc.vector.quantize_mx(codes.bitcast(FP8X4), o_scales[:, pair * 2 * P : (pair + 1) * 2 * P], rounded[pair][:].rearrange("p n t -> p (n t)"))
 
-        early, middle, late = CHUNKS
-        alone = (SHARED, T - SHARED)
-        fetch_and_turn(*early)
-        gate_and_add(early[0], 0)
-        gate_and_add(early[0], 1)
-        store_sum(*early)
-        first_last = arena.tile([P, HANDS, T - SHARED], F32, name="first_last", offset=on_gated(1))
+        first01 = arena.tile([P, HANDS, 2 * P], F32, name="first01", offset=on_matrix(8))
+        for t in range(HANDS):
+            fetch(first01[:, t, :], t, (0, 1))
+        summed01 = keep.tile([P, HANDS, 2 * P], F32, name="summed01")
+        for b in range(2):
+            gate_and_add(b, summed01[:, :, b * P : (b + 1) * P])
+        nc.sync.dma_start(out_rows[:, :, : 2 * P], summed01[:])
+
+        for b in range(2, T // P):
+            summed[b] = keep.tile([P, HANDS, P], F32, name="summed%d" % b)
+        first_last = arena.tile([P, HANDS, P], F32, name="first_last", offset=on_gated(1, 1))
         for t in range(HANDS):
             nc.vector.tensor_tensor(first_last[:, t, :], y[t][:].indirect(pos1_sb[:, SHARED // 16 :]), gate1_last[:], MULT)
-        summed[SHARED] = keep.tile([P, HANDS, T - SHARED], F32, name="summed_alone")
-        nc.vector.tensor_tensor(summed[SHARED][:], first_last[:], second[:, :, SHARED:], ADD)
-        store_sum(*alone)
-        fetch_and_turn(*middle)
-        fetch_and_turn(*late)
-        gate_and_add(middle[0], 2)
-        gate_and_add(middle[0], 3)
-        store_sum(*middle)
-        gate_and_add(late[0], 4)
-        store_sum(*late)
-        for start, offset in ((early[0], on_gated(2)), (middle[0], on_gated(4)), (late[0], on_gated(3))):
-            rounded[start] = arena.tile([P, 2 * P, HANDS], BF16, name="rounded%d" % start, align_bytes=64, offset=offset)
-        round_sum(rounded[early[0]][:], summed[early[0]][:], nc.scalar.copy)
-        round_sum(rounded[late[0]][:, P:, :], summed[SHARED][:], nc.scalar.copy)
-        round_sum(rounded[middle[0]][:, :P, :], summed[middle[0]][:, :, :P], nc.scalar.copy)
-        round_sum(rounded[middle[0]][:, P:, :], summed[middle[0]][:, :, P:], nc.vector.tensor_copy)
-        round_sum(rounded[late[0]][:, :P, :], summed[late[0]][:], nc.vector.tensor_copy)
-        for start, width in CHUNKS:
-            quantise_sum(start)
+        nc.vector.tensor_tensor(summed[5][:], first_last[:], second[:, :, SHARED:], ADD)
+        nc.sync.dma_start(out_rows[:, :, SHARED:], summed[5][:])
+
+        for t in range(HANDS):
+            tile = arena.tile([P, 2 * P], F32, name="first23_%d" % t, offset=on_matrix(8 if t >= 2 else 9) + t * 2 * P * 4)
+            fetch(tile[:], t, (2, 3))
+        for t in range(HANDS - 1):
+            tile = arena.tile([P, P], F32, name="first4_%d" % t, offset=on_gated(1) + t * P * 4)
+            fetch(tile[:], t, (4,))
+        rounded = [arena.tile([P, 2 * P, HANDS], BF16, name="rounded%d" % pair, align_bytes=64, offset=offset) for pair, offset in enumerate((on_gated(2), on_gated(3, -1), on_gated(3, 1)))]
+        gate_and_add(2, summed[2][:])
+        nc.sync.dma_start(out_rows[:, :, 2 * P : 3 * P], summed[2][:])
+        round_sum(rounded[0][:], summed01[:], nc.vector.tensor_copy)
+        tile = arena.tile([P, P], F32, name="first4_3", offset=on_matrix(8) + 6 * P * 4)
+        fetch(tile[:], HANDS - 1, (4,))
+        for b in (3, 4):
+            gate_and_add(b, summed[b][:])
+            nc.sync.dma_start(out_rows[:, :, b * P : (b + 1) * P], summed[b][:])
+
+        for b in (5, 2, 3):
+            round_sum(rounded[b // 2][:, b % 2 * P : (b % 2 + 1) * P, :], summed[b][:], nc.scalar.copy)
+        codes03 = arena.tile([P, 4 * P], U32, name="codes03", align_bytes=64, offset=on_gated(4))
+        codes45 = keep.tile([P, 2 * P], U32, name="codes45", align_bytes=64)
+        quantise_sum(codes03[:, : 2 * P], 0)
+        round_sum(rounded[2][:, :P, :], summed[4][:], nc.vector.tensor_copy)
+        quantise_sum(codes03[:, 2 * P :], 1)
+        nc.sync.dma_start(out_words[:, : 4 * P], codes03[:].bitcast(I32))
+        quantise_sum(codes45[:], 2)
+        nc.sync.dma_start(out_words[:, 4 * P :], codes45[:].bitcast(I32))
         for r in range(4):
             queue = nc.scalar if r % 2 else nc.sync
             queue.dma_start(out_2[0].bitcast(I32)[r:16:4, :], o_scales[:].bitcast(I32)[r:P:32, :])

@@ -116,15 +116,26 @@ def tile_moe_duo_gelu_kernel(
         h_codes = {}
         h_scales = {}
 
+        def round_and_quantise_by_halves(m):
+            src = raw[m].rearrange("p j (c t) -> p c j t", t=HANDS)
+            halves = [arena.tile([P, 2 * H], BF16, name="half%d" % u, align_bytes=64, offset=on_matrix(9) + 4 * H + u * (4 * H - 64)) for u in range(2)]
+            codes = ring.tile([P, H], U32, name="codes", align_bytes=64, bufs=6)
+            scales = ring.tile([P, H], U8, name="scales", align_bytes=64, bufs=5)
+            nc.vector.tensor_copy(halves[0][:].rearrange("p (t c j) -> p c j t", t=2, j=4), src[:, :, :, :2])
+            nc.vector.quantize_mx(codes[:, : 2 * P].bitcast(FP8X4), scales[:, : 2 * P], halves[0][:])
+            nc.vector.tensor_copy(halves[1][:].rearrange("p (t c j) -> p c j t", t=2, j=4), src[:, :, :, 2:])
+            grouped[m] = halves[1]
+            quantised[m] = (codes, scales)
+
         def round_matrix(m):
+            if m == MATRICES - 2:
+                round_and_quantise_by_halves(m)
+                return
             grouped[m] = ring.tile([P, 4 * H], BF16, name="grouped", align_bytes=64, bufs=6)
             src = raw[m].rearrange("p j (c t) -> p c j t", t=HANDS)
             dst = grouped[m][:].rearrange("p (t c j) -> p c j t", t=HANDS, j=4)
             on_vector = 0 if m < SCALAR_ALONE else (HANDS // 2 if m % 2 else HANDS)
-            if m == MATRICES - 2:
-                for t in range(0, HANDS, 2):
-                    nc.vector.tensor_copy(dst[:, :, :, t : t + 2], src[:, :, :, t : t + 2])
-            elif on_vector > 0:
+            if on_vector > 0:
                 nc.vector.tensor_copy(dst[:, :, :, :on_vector], src[:, :, :, :on_vector])
             if on_vector < HANDS:
                 nc.scalar.copy(dst[:, :, :, on_vector:], src[:, :, :, on_vector:])
@@ -144,7 +155,7 @@ def tile_moe_duo_gelu_kernel(
                 scales = arena.tile([P, H], U8, name="scales%d" % m, align_bytes=64, offset=on_margin(m + 1))
             else:
                 scales = ring.tile([P, H], U8, name="scales", align_bytes=64, bufs=5)
-            cuts = {FIRST - 1: (0, 2 * P, H), MATRICES - 2: (0, 2 * P, H), MATRICES - 1: (0, P, 2 * P, H)}.get(m, (0, H))
+            cuts = {FIRST - 1: (0, 2 * P, H), MATRICES - 1: (0, P, 2 * P, H)}.get(m, (0, H))
             for c0, c1 in zip(cuts, cuts[1:]):
                 nc.vector.quantize_mx(codes[:, c0:c1].bitcast(FP8X4), scales[:, c0:c1], grouped[m][:, 4 * c0 : 4 * c1])
             quantised[m] = (codes, scales)
@@ -189,10 +200,11 @@ def tile_moe_duo_gelu_kernel(
 
         def last_two_experts():
             m, e = MATRICES - 1, E - 1
-            round_matrix(m)
-            quantise_matrix(m - 1)
             codes, scales = quantised[m - 1]
             product(e - 1, 0, codes[:, :P], scales[:, :P])
+            round_matrix(m)
+            late_scales = arena.tile([P, 2 * P], U8, name="late_scales", align_bytes=64, offset=on_margin(m))
+            nc.vector.quantize_mx(codes[:, 2 * P :].bitcast(FP8X4), late_scales[:], grouped[m - 1][:])
             quantise_matrix(m)
             codes, scales = quantised[m]
             product(e, 0, codes[:, :P], scales[:, :P])
@@ -200,8 +212,9 @@ def tile_moe_duo_gelu_kernel(
                 bank = psum.tile([P, 2, C], F32, name="bank_pair%d" % t, offset=(t - 1) * BANK)
                 for u in range(2):
                     codes, scales = quantised[m - 1 + u]
+                    scales = late_scales[:, (t - 2) * P : (t - 1) * P] if u == 0 and t >= 2 else scales[:, t * P : (t + 1) * P]
                     nc.tensor.matmul_mx(
-                        bank[:, u, :], lhsT=codes[:, t * P : (t + 1) * P].bitcast(FP8X4), lhsT_scale=scales[:, t * P : (t + 1) * P],
+                        bank[:, u, :], lhsT=codes[:, t * P : (t + 1) * P].bitcast(FP8X4), lhsT_scale=scales,
                         rhs=h_codes[e - 1 + u][:].bitcast(FP8X4), rhs_scale=h_scales[e - 1 + u][:], start=True, stop=True,
                     )
                 nc.scalar.copy(y[t][:, (e - 1) * C :], bank[:].rearrange("p u c -> p (u c)"))
@@ -212,8 +225,12 @@ def tile_moe_duo_gelu_kernel(
         for m in range(SCALAR_ALONE - 1):
             quantise_matrix(m)
         for m in range(SCALAR_ALONE, MATRICES - 1):
-            round_matrix(m)
-            quantise_matrix(m - 1)
+            if m == MATRICES - 2:
+                quantise_matrix(m - 1)
+                round_matrix(m)
+            else:
+                round_matrix(m)
+                quantise_matrix(m - 1)
             for e in range(E):
                 if m == SCALAR_ALONE and 2 * e + GELU_LAG < m:
                     first_layer(e, on_matrix(m - 1) + e * C * HANDS * 2)
@@ -260,8 +277,8 @@ def tile_moe_duo_gelu_kernel(
         def round_sum(tile, sums, copy_on_engine):
             copy_on_engine(tile.rearrange("p (c i) t -> p c t i", i=4), sums.rearrange("p t (c i) -> p c t i", i=4))
 
-        def quantise_sum(codes, pair):
-            nc.vector.quantize_mx(codes.bitcast(FP8X4), o_scales[:, pair * 2 * P : (pair + 1) * 2 * P], rounded[pair][:].rearrange("p n t -> p (n t)"))
+        def quantise_sum(codes, tile, start, width):
+            nc.vector.quantize_mx(codes.bitcast(FP8X4), o_scales[:, start : start + width], tile[:].rearrange("p n t -> p (n t)"))
 
         first01 = arena.tile([P, HANDS, 2 * P], F32, name="first01", offset=on_matrix(8))
         for t in range(HANDS):
@@ -276,7 +293,8 @@ def tile_moe_duo_gelu_kernel(
         first_last = arena.tile([P, HANDS, P], F32, name="first_last", offset=on_gated(1, 1))
         for t in range(HANDS):
             nc.vector.tensor_tensor(first_last[:, t, :], y[t][:].indirect(pos1_sb[:, SHARED // 16 :]), gate1_last[:], MULT)
-        nc.vector.tensor_tensor(summed[5][:], first_last[:], second[:, :, SHARED:], ADD)
+        for t in range(0, HANDS, 2):
+            nc.vector.tensor_tensor(summed[5][:, t : t + 2, :], first_last[:, t : t + 2, :], second[:, t : t + 2, SHARED:], ADD)
         nc.sync.dma_start(out_rows[:, :, SHARED:], summed[5][:])
 
         for t in range(HANDS):
@@ -285,25 +303,30 @@ def tile_moe_duo_gelu_kernel(
         for t in range(HANDS - 1):
             tile = arena.tile([P, P], F32, name="first4_%d" % t, offset=on_gated(1) + t * P * 4)
             fetch(tile[:], t, (4,))
-        rounded = [arena.tile([P, 2 * P, HANDS], BF16, name="rounded%d" % pair, align_bytes=64, offset=offset) for pair, offset in enumerate((on_gated(2), on_gated(3, -1), on_gated(3, 1)))]
-        gate_and_add(2, summed[2][:])
-        nc.sync.dma_start(out_rows[:, :, 2 * P : 3 * P], summed[2][:])
-        round_sum(rounded[0][:], summed01[:], nc.vector.tensor_copy)
-        tile = arena.tile([P, P], F32, name="first4_3", offset=on_matrix(8) + 6 * P * 4)
-        fetch(tile[:], HANDS - 1, (4,))
-        for b in (3, 4):
+        rounded0 = arena.tile([P, P, HANDS], BF16, name="rounded0", align_bytes=64, offset=on_gated(2))
+        rounded1 = arena.tile([P, P, HANDS], BF16, name="rounded1", align_bytes=64, offset=on_gated(3) + block_bytes // 4)
+        rounded23 = arena.tile([P, 2 * P, HANDS], BF16, name="rounded23", align_bytes=64, offset=on_gated(3, -1))
+        rounded45 = arena.tile([P, 2 * P, HANDS], BF16, name="rounded45", align_bytes=64, offset=on_gated(3, 1))
+        for b in range(2, BLOCKS):
             gate_and_add(b, summed[b][:])
             nc.sync.dma_start(out_rows[:, :, b * P : (b + 1) * P], summed[b][:])
+            if b == 2:
+                tile = arena.tile([P, P], F32, name="first4_3", offset=on_matrix(8) + 6 * P * 4)
+                fetch(tile[:], HANDS - 1, (4,))
+            if b < 4:
+                round_sum((rounded0, rounded1)[b - 2][:], summed01[:, :, (b - 2) * P : (b - 1) * P], nc.vector.tensor_copy)
 
-        for b in (5, 2, 3):
-            round_sum(rounded[b // 2][:, b % 2 * P : (b % 2 + 1) * P, :], summed[b][:], nc.scalar.copy)
+        round_sum(rounded45[:, P:, :], summed[5][:], nc.scalar.copy)
+        for b in (2, 3):
+            round_sum(rounded23[:, (b - 2) * P : (b - 1) * P, :], summed[b][:], nc.scalar.copy)
         codes03 = arena.tile([P, 4 * P], U32, name="codes03", align_bytes=64, offset=on_gated(4))
         codes45 = keep.tile([P, 2 * P], U32, name="codes45", align_bytes=64)
-        quantise_sum(codes03[:, : 2 * P], 0)
-        round_sum(rounded[2][:, :P, :], summed[4][:], nc.vector.tensor_copy)
-        quantise_sum(codes03[:, 2 * P :], 1)
+        quantise_sum(codes03[:, :P], rounded0, 0, P)
+        round_sum(rounded45[:, :P, :], summed[4][:], nc.vector.tensor_copy)
+        quantise_sum(codes03[:, P : 2 * P], rounded1, P, P)
+        quantise_sum(codes03[:, 2 * P :], rounded23, 2 * P, 2 * P)
         nc.sync.dma_start(out_words[:, : 4 * P], codes03[:].bitcast(I32))
-        quantise_sum(codes45[:], 2)
+        quantise_sum(codes45[:], rounded45, 4 * P, 2 * P)
         nc.sync.dma_start(out_words[:, 4 * P :], codes45[:].bitcast(I32))
         for r in range(4):
             queue = nc.scalar if r % 2 else nc.sync

@@ -71,7 +71,6 @@ def tile_moe_duo_gelu_kernel(
         make_identity(nc, ident[:])
 
         nc.sync.dma_start(offs_sb[:], offs)
-        nc.sync.dma_start(offs2_sb[:], offs2)
         nc.sync.dma_start(xw[:, :T], x_words[0].rearrange("p t d -> p (t d)").bitcast(I32))
 
         raw = {}
@@ -91,6 +90,8 @@ def tile_moe_duo_gelu_kernel(
 
         for m in range(ROOMS):
             load(m)
+            if m == 1:
+                nc.sync.dma_start(offs2_sb[:], offs2)
 
         gate1_rows = keep.tile([P, P], F32, name="gate1_rows")
         nc.gpsimd.memset(gate1_rows[:], 0.0)
@@ -104,8 +105,8 @@ def tile_moe_duo_gelu_kernel(
             (keep.tile([P, S], U32, name="words%d" % which, align_bytes=64), keep.tile([P, S], U8, name="bytes%d" % which, align_bytes=64))
             for which in range(2)
         ]
-        for sort, table in ((1, xs[:]), (0, xw[:].bitcast(U32))):
-            for which, lst in enumerate((offs_sb, offs2_sb)):
+        for which, lst in enumerate((offs_sb, offs2_sb)):
+            for sort, table in ((1, xs[:]), (0, xw[:].bitcast(U32))):
                 nc.vector.tensor_copy(gathered[which][sort][:], table.indirect(lst[:]))
 
         gate2 = keep.tile([P, T], F32, name="gate2")

@@ -36,9 +36,10 @@ SCALAR_ALONE = 7
 GELU_LAG = 3
 HIDDEN_LAG = 6
 HIDDEN_LAST = MATRICES - 4
-CHUNKS = ((0, 2 * P), (2 * P, 2 * P), (4 * P, P))
-BLOCKS = 5
-SHARED = BLOCKS * P
+CHUNK = 2 * P
+BLOCKS = T // P
+OWN = 1
+UNITS = ((0, 0), (1, 0), (2, 0), (0, 1), (2, 1))
 
 
 def tile_moe_duo_gelu_kernel(
@@ -95,7 +96,7 @@ def tile_moe_duo_gelu_kernel(
 
         gate1_rows = keep.tile([P, P], F32, name="gate1_rows")
         nc.gpsimd.memset(gate1_rows[:], 0.0)
-        nc.sync.dma_start(gate1_rows[:BLOCKS, :], gate[0, 0:1, :SHARED].rearrange("o (b p) -> (o b) p", p=P))
+        nc.sync.dma_start(gate1_rows[:BLOCKS, :], gate[0, 0:1, :].rearrange("o (b p) -> (o b) p", p=P))
         gate1_turned = psum.tile([P, P], F32, name="gate1_turned", offset=7 * BANK)
         nc.tensor.transpose(gate1_turned[:], gate1_rows[:], ident[:])
         gate1 = keep.tile([P, BLOCKS], F32, name="gate1")
@@ -110,7 +111,7 @@ def tile_moe_duo_gelu_kernel(
                 nc.vector.tensor_copy(gathered[which][sort][:], table.indirect(lst[:]))
 
         gate2 = keep.tile([P, T], F32, name="gate2")
-        gate1_last = keep.tile([P, T - SHARED], F32, name="gate1_last")
+        gate1_own = keep.tile([P, CHUNK], F32, name="gate1_own")
         grouped = {}
         quantised = {}
         hidden = {}
@@ -148,7 +149,7 @@ def tile_moe_duo_gelu_kernel(
                 nc.sync.dma_start(pos2_sb[:], pos2)
                 nc.sync.dma_start(gate2[:], gate[1])
                 nc.sync.dma_start(pos1_sb[:], pos1)
-                nc.sync.dma_start(gate1_last[:], gate[0, :, SHARED:])
+                nc.sync.dma_start(gate1_own[:], gate[0, :, OWN * CHUNK : (OWN + 1) * CHUNK])
 
         def quantise_matrix(m):
             codes = ring.tile([P, H], U32, name="codes", align_bytes=64, bufs=6)
@@ -253,82 +254,76 @@ def tile_moe_duo_gelu_kernel(
         for t in range(HANDS):
             nc.vector.tensor_tensor(second[:, t, :], y[t][:].indirect(pos2_sb[:]), gate2[:], MULT)
 
-        block_bytes = HANDS * P * 4
+        unit_bytes = 2 * CHUNK * 4
+        summed = [keep.tile([P, HANDS, CHUNK], F32, name="summed%d" % c) for c in range(T // CHUNK)]
         there = {}
-        summed = {}
 
-        def on_gated(b, side=0):
-            return (3 * b + 1) * block_bytes + side * (block_bytes - 64)
+        def on_gated(i, side=0):
+            return (3 * i + 1) * unit_bytes + side * (unit_bytes - 64)
 
-        def fetch(tile, t, blocks):
-            nc.scalar.activation(tile, y[t][:].indirect(pos1_sb[:, blocks[0] * P // 16 : (blocks[-1] + 1) * P // 16]), COPY)
-            for i, b in enumerate(blocks):
-                if t == 0:
-                    there[b] = psum.tile([P, HANDS, P], F32, name="there%d" % b, offset=b % 4 * BANK)
-                nc.tensor.transpose(there[b][:, t, :], tile[:, i * P : (i + 1) * P], ident[:])
+        def fetch(i, k):
+            c, pair = UNITS[i]
+            n = 2 * i + k
+            tile = arena.tile([P, CHUNK], F32, name="first%d" % n, offset=on_matrix(8 + n // 8) + n % 8 * CHUNK * 4)
+            nc.scalar.activation(tile[:], y[2 * pair + k][:].indirect(pos1_sb[:, c * CHUNK // 16 : (c + 1) * CHUNK // 16]), COPY)
+            if k == 0:
+                there[i] = psum.tile([P, 2, 2, P], F32, name="there%d" % i, offset=(3 + i if i < 3 else i - 2) * BANK)
+            for block in range(2):
+                nc.tensor.transpose(there[i][:, block, k, :], tile[:, block * P : (block + 1) * P], ident[:])
 
-        def gate_and_add(b, sums):
-            gated = arena.tile([P, HANDS, P], F32, name="gated%d" % b, offset=on_gated(b))
-            nc.scalar.activation(gated[:], there[b][:], COPY, scale=gate1[:, b : b + 1])
-            back = psum.tile([P, HANDS, P], F32, name="back%d" % b, offset=(4 + b % 4) * BANK)
-            for t in range(HANDS):
-                nc.tensor.transpose(back[:, t, :], gated[:, t, :], ident[:])
-            nc.vector.tensor_tensor(sums, back[:], second[:, :, b * P : (b + 1) * P], ADD)
+        def store(c, pair):
+            nc.sync.dma_start(out_rows[:, 2 * pair : 2 * pair + 2, c * CHUNK : (c + 1) * CHUNK], summed[c][:, 2 * pair : 2 * pair + 2, :])
 
-        def round_sum(tile, sums, copy_on_engine):
-            copy_on_engine(tile.rearrange("p (c i) t -> p c t i", i=4), sums.rearrange("p t (c i) -> p c t i", i=4))
+        def gate_and_add(i):
+            c, pair = UNITS[i]
+            hands = slice(2 * pair, 2 * pair + 2)
+            gated = arena.tile([P, 2, 2, P], F32, name="gated%d" % i, offset=on_gated(i))
+            back = psum.tile([P, 2, CHUNK], F32, name="back%d" % i, offset=((6 + i) % 8 if i < 3 else i) * BANK)
+            for block in range(2):
+                nc.scalar.activation(gated[:, block], there[i][:, block], COPY, scale=gate1[:, 2 * c + block : 2 * c + block + 1])
+                for k in range(2):
+                    nc.tensor.transpose(back[:, k, block * P : (block + 1) * P], gated[:, block, k, :], ident[:])
+            nc.vector.tensor_tensor(summed[c][:, hands, :], back[:], second[:, hands, c * CHUNK : (c + 1) * CHUNK], ADD)
+            store(c, pair)
 
-        def quantise_sum(codes, tile, start, width):
-            nc.vector.quantize_mx(codes.bitcast(FP8X4), o_scales[:, start : start + width], tile[:].rearrange("p n t -> p (n t)"))
+        def round_sum(c, offset, copy_on_engine):
+            tile = arena.tile([P, CHUNK, HANDS], BF16, name="rounded%d" % c, align_bytes=64, offset=offset)
+            copy_on_engine(tile[:].rearrange("p (c i) t -> p c t i", i=4), summed[c][:].rearrange("p t (c i) -> p c t i", i=4))
+            return tile
 
-        first01 = arena.tile([P, HANDS, 2 * P], F32, name="first01", offset=on_matrix(8))
-        for t in range(HANDS):
-            fetch(first01[:, t, :], t, (0, 1))
-        summed01 = keep.tile([P, HANDS, 2 * P], F32, name="summed01")
-        for b in range(2):
-            gate_and_add(b, summed01[:, :, b * P : (b + 1) * P])
-        nc.sync.dma_start(out_rows[:, :, : 2 * P], summed01[:])
+        def quantise_sum(codes, c, tile):
+            nc.vector.quantize_mx(codes.bitcast(FP8X4), o_scales[:, c * CHUNK : (c + 1) * CHUNK], tile[:].rearrange("p n t -> p (n t)"))
 
-        for b in range(2, T // P):
-            summed[b] = keep.tile([P, HANDS, P], F32, name="summed%d" % b)
-        first_last = arena.tile([P, HANDS, P], F32, name="first_last", offset=on_gated(1, 1))
-        for t in range(HANDS):
-            nc.vector.tensor_tensor(first_last[:, t, :], y[t][:].indirect(pos1_sb[:, SHARED // 16 :]), gate1_last[:], MULT)
-        for t in range(0, HANDS, 2):
-            nc.vector.tensor_tensor(summed[5][:, t : t + 2, :], first_last[:, t : t + 2, :], second[:, t : t + 2, SHARED:], ADD)
-        nc.sync.dma_start(out_rows[:, :, SHARED:], summed[5][:])
+        for k in range(2):
+            for i in range(3):
+                fetch(i, k)
+        for i in range(3):
+            gate_and_add(i)
 
-        for t in range(HANDS):
-            tile = arena.tile([P, 2 * P], F32, name="first23_%d" % t, offset=on_matrix(8 if t >= 2 else 9) + t * 2 * P * 4)
-            fetch(tile[:], t, (2, 3))
-        for t in range(HANDS - 1):
-            tile = arena.tile([P, P], F32, name="first4_%d" % t, offset=on_gated(1) + t * P * 4)
-            fetch(tile[:], t, (4,))
-        rounded0 = arena.tile([P, P, HANDS], BF16, name="rounded0", align_bytes=64, offset=on_gated(2))
-        rounded1 = arena.tile([P, P, HANDS], BF16, name="rounded1", align_bytes=64, offset=on_gated(3) + block_bytes // 4)
-        rounded23 = arena.tile([P, 2 * P, HANDS], BF16, name="rounded23", align_bytes=64, offset=on_gated(3, -1))
-        rounded45 = arena.tile([P, 2 * P, HANDS], BF16, name="rounded45", align_bytes=64, offset=on_gated(3, 1))
-        for b in range(2, BLOCKS):
-            gate_and_add(b, summed[b][:])
-            nc.sync.dma_start(out_rows[:, :, b * P : (b + 1) * P], summed[b][:])
-            if b == 2:
-                tile = arena.tile([P, P], F32, name="first4_3", offset=on_matrix(8) + 6 * P * 4)
-                fetch(tile[:], HANDS - 1, (4,))
-            if b < 4:
-                round_sum((rounded0, rounded1)[b - 2][:], summed01[:, :, (b - 2) * P : (b - 1) * P], nc.vector.tensor_copy)
+        own = slice(OWN * CHUNK, (OWN + 1) * CHUNK)
+        first_own = arena.tile([P, 2, CHUNK], F32, name="first_own", offset=on_gated(1, 1))
+        for k in range(2):
+            nc.vector.tensor_tensor(first_own[:, k, :], y[2 + k][:].indirect(pos1_sb[:, own.start // 16 : own.stop // 16]), gate1_own[:], MULT)
+        for k in range(2):
+            nc.vector.tensor_tensor(summed[OWN][:, 2 + k, :], first_own[:, k, :], second[:, 2 + k, own], ADD)
+        store(OWN, 1)
 
-        round_sum(rounded45[:, P:, :], summed[5][:], nc.scalar.copy)
-        for b in (2, 3):
-            round_sum(rounded23[:, (b - 2) * P : (b - 1) * P, :], summed[b][:], nc.scalar.copy)
-        codes03 = arena.tile([P, 4 * P], U32, name="codes03", align_bytes=64, offset=on_gated(4))
-        codes45 = keep.tile([P, 2 * P], U32, name="codes45", align_bytes=64)
-        quantise_sum(codes03[:, :P], rounded0, 0, P)
-        round_sum(rounded45[:, :P, :], summed[4][:], nc.vector.tensor_copy)
-        quantise_sum(codes03[:, P : 2 * P], rounded1, P, P)
-        quantise_sum(codes03[:, 2 * P :], rounded23, 2 * P, 2 * P)
-        nc.sync.dma_start(out_words[:, : 4 * P], codes03[:].bitcast(I32))
-        quantise_sum(codes45[:], rounded45, 4 * P, 2 * P)
-        nc.sync.dma_start(out_words[:, 4 * P :], codes45[:].bitcast(I32))
+        for i in range(3, len(UNITS)):
+            for k in range(2):
+                fetch(i, k)
+        for i in range(3, len(UNITS)):
+            gate_and_add(i)
+
+        rounded1 = round_sum(1, on_gated(3, -1), nc.scalar.copy)
+        rounded0 = round_sum(0, on_gated(3, 1), nc.scalar.copy)
+        rounded2 = round_sum(2, on_matrix(8), nc.vector.tensor_copy)
+        codes12 = arena.tile([P, 2 * CHUNK], U32, name="codes12", align_bytes=64, offset=on_gated(4))
+        codes0 = keep.tile([P, CHUNK], U32, name="codes0", align_bytes=64)
+        quantise_sum(codes12[:, :CHUNK], 1, rounded1)
+        quantise_sum(codes12[:, CHUNK:], 2, rounded2)
+        nc.sync.dma_start(out_words[:, CHUNK:], codes12[:].bitcast(I32))
+        quantise_sum(codes0[:], 0, rounded0)
+        nc.sync.dma_start(out_words[:, :CHUNK], codes0[:].bitcast(I32))
         for r in range(4):
             queue = nc.scalar if r % 2 else nc.sync
             queue.dma_start(out_2[0].bitcast(I32)[r:16:4, :], o_scales[:].bitcast(I32)[r:P:32, :])

@@ -263,8 +263,8 @@ def tile_moe_duo_gelu_kernel(
 
         def fetch(i, k):
             c, pair = UNITS[i]
-            n = 2 * i + k
-            tile = arena.tile([P, CHUNK], F32, name="first%d" % n, offset=on_matrix(8 + n // 8) + n % 8 * CHUNK * 4)
+            place = (3 * k + i) * CHUNK * 4 if pair == 0 else (2 + (2 * i + k - 5) % 4) * CHUNK * 4 + 64
+            tile = arena.tile([P, CHUNK], F32, name="first%d_%d" % (i, k), offset=on_matrix(8) + place)
             nc.scalar.activation(tile[:], y[2 * pair + k][:].indirect(pos1_sb[:, c * CHUNK // 16 : (c + 1) * CHUNK // 16]), COPY)
             if k == 0:
                 there[i] = psum.tile([P, 2, 2, P], F32, name="there%d" % i, offset=(3 + i if i < 3 else i - 2) * BANK)
@@ -286,9 +286,12 @@ def tile_moe_duo_gelu_kernel(
             nc.vector.tensor_tensor(summed[c][:, hands, :], back[:], second[:, hands, c * CHUNK : (c + 1) * CHUNK], ADD)
             store(c, pair)
 
-        def round_sum(c, offset, copy_on_engine):
+        def round_sum(c, offset, copies):
             tile = arena.tile([P, CHUNK, HANDS], BF16, name="rounded%d" % c, align_bytes=64, offset=offset)
-            copy_on_engine(tile[:].rearrange("p (c i) t -> p c t i", i=4), summed[c][:].rearrange("p t (c i) -> p c t i", i=4))
+            share = CHUNK // len(copies)
+            for n, copy_on_engine in enumerate(copies):
+                tokens = slice(n * share, (n + 1) * share)
+                copy_on_engine(tile[:, tokens, :].rearrange("p (c i) t -> p c t i", i=4), summed[c][:, :, tokens].rearrange("p t (c i) -> p c t i", i=4))
             return tile
 
         def quantise_sum(codes, c, tile):
@@ -314,16 +317,16 @@ def tile_moe_duo_gelu_kernel(
         for i in range(3, len(UNITS)):
             gate_and_add(i)
 
-        rounded1 = round_sum(1, on_gated(3, -1), nc.scalar.copy)
-        rounded0 = round_sum(0, on_gated(3, 1), nc.scalar.copy)
-        rounded2 = round_sum(2, on_matrix(8), nc.vector.tensor_copy)
-        codes12 = arena.tile([P, 2 * CHUNK], U32, name="codes12", align_bytes=64, offset=on_gated(4))
-        codes0 = keep.tile([P, CHUNK], U32, name="codes0", align_bytes=64)
-        quantise_sum(codes12[:, :CHUNK], 1, rounded1)
-        quantise_sum(codes12[:, CHUNK:], 2, rounded2)
-        nc.sync.dma_start(out_words[:, CHUNK:], codes12[:].bitcast(I32))
-        quantise_sum(codes0[:], 0, rounded0)
-        nc.sync.dma_start(out_words[:, :CHUNK], codes0[:].bitcast(I32))
+        rounded1 = round_sum(1, on_gated(3, -1), [nc.scalar.copy])
+        rounded0 = round_sum(0, on_gated(3, 1), [nc.vector.tensor_copy, nc.scalar.copy])
+        rounded2 = round_sum(2, on_matrix(8), [nc.vector.tensor_copy, nc.scalar.copy])
+        codes01 = arena.tile([P, 2 * CHUNK], U32, name="codes01", align_bytes=64, offset=on_gated(4))
+        codes2 = keep.tile([P, CHUNK], U32, name="codes2", align_bytes=64)
+        quantise_sum(codes01[:, CHUNK:], 1, rounded1)
+        quantise_sum(codes01[:, :CHUNK], 0, rounded0)
+        nc.sync.dma_start(out_words[:, : 2 * CHUNK], codes01[:].bitcast(I32))
+        quantise_sum(codes2[:], 2, rounded2)
+        nc.sync.dma_start(out_words[:, 2 * CHUNK :], codes2[:].bitcast(I32))
         for r in range(4):
             queue = nc.scalar if r % 2 else nc.sync
             queue.dma_start(out_2[0].bitcast(I32)[r:16:4, :], o_scales[:].bitcast(I32)[r:P:32, :])

@@ -255,7 +255,7 @@ def tile_moe_duo_gelu_kernel(
             nc.vector.tensor_tensor(second[:, t, :], y[t][:].indirect(pos2_sb[:]), gate2[:], MULT)
 
         unit_bytes = 2 * CHUNK * 4
-        summed = [keep.tile([P, HANDS, CHUNK], F32, name="summed%d" % c) for c in range(T // CHUNK)]
+        summed = keep.tile([P, HANDS, T], F32, name="summed")
         there = {}
 
         def on_gated(i, side=0):
@@ -271,27 +271,32 @@ def tile_moe_duo_gelu_kernel(
             for block in range(2):
                 nc.tensor.transpose(there[i][:, block, k, :], tile[:, block * P : (block + 1) * P], ident[:])
 
-        def store(c, pair):
-            nc.sync.dma_start(out_rows[:, 2 * pair : 2 * pair + 2, c * CHUNK : (c + 1) * CHUNK], summed[c][:, 2 * pair : 2 * pair + 2, :])
+        def store(pair, first_chunk, last_chunk):
+            part = (slice(None), slice(2 * pair, 2 * pair + 2), slice(first_chunk * CHUNK, (last_chunk + 1) * CHUNK))
+            nc.sync.dma_start(out_rows[part], summed[part])
 
         def gate_and_add(i):
             c, pair = UNITS[i]
             hands = slice(2 * pair, 2 * pair + 2)
             gated = arena.tile([P, 2, 2, P], F32, name="gated%d" % i, offset=on_gated(i))
-            back = psum.tile([P, 2, CHUNK], F32, name="back%d" % i, offset=((6 + i) % 8 if i < 3 else i) * BANK)
-            for block in range(2):
-                nc.scalar.activation(gated[:, block], there[i][:, block], COPY, scale=gate1[:, 2 * c + block : 2 * c + block + 1])
-                for k in range(2):
-                    nc.tensor.transpose(back[:, k, block * P : (block + 1) * P], gated[:, block, k, :], ident[:])
-            nc.vector.tensor_tensor(summed[c][:, hands, :], back[:], second[:, hands, c * CHUNK : (c + 1) * CHUNK], ADD)
-            store(c, pair)
+            parts = ((0, 1),) if pair == 0 else ((0,), (1,))
+            for blocks in parts:
+                start, width = blocks[0] * P, len(blocks) * P
+                back = psum.tile([P, 2, width], F32, name="back%d_%d" % (i, start), offset=((6 + i) % 8 if pair == 0 else i + 2 * blocks[0]) * BANK)
+                for block in blocks:
+                    nc.scalar.activation(gated[:, block], there[i][:, block], COPY, scale=gate1[:, 2 * c + block : 2 * c + block + 1])
+                    for k in range(2):
+                        nc.tensor.transpose(back[:, k, block * P - start : (block + 1) * P - start], gated[:, block, k, :], ident[:])
+                tokens = slice(c * CHUNK + start, c * CHUNK + start + width)
+                nc.vector.tensor_tensor(summed[:, hands, tokens], back[:], second[:, hands, tokens], ADD)
+            if i >= 2:
+                store(pair, 0 if pair == 0 else c, c)
 
-        def round_sum(c, offset, copies):
+        def round_sum(c, offset, on_vector):
             tile = arena.tile([P, CHUNK, HANDS], BF16, name="rounded%d" % c, align_bytes=64, offset=offset)
-            share = CHUNK // len(copies)
-            for n, copy_on_engine in enumerate(copies):
-                tokens = slice(n * share, (n + 1) * share)
-                copy_on_engine(tile[:, tokens, :].rearrange("p (c i) t -> p c t i", i=4), summed[c][:, :, tokens].rearrange("p t (c i) -> p c t i", i=4))
+            for tokens, copy_on_engine in ((slice(0, on_vector), nc.vector.tensor_copy), (slice(on_vector, CHUNK), nc.scalar.copy)):
+                if tokens.stop > tokens.start:
+                    copy_on_engine(tile[:, tokens, :].rearrange("p (c i) t -> p c t i", i=4), summed[:, :, c * CHUNK + tokens.start : c * CHUNK + tokens.stop].rearrange("p t (c i) -> p c t i", i=4))
             return tile
 
         def quantise_sum(codes, c, tile):
@@ -304,12 +309,12 @@ def tile_moe_duo_gelu_kernel(
             gate_and_add(i)
 
         own = slice(OWN * CHUNK, (OWN + 1) * CHUNK)
-        first_own = arena.tile([P, 2, CHUNK], F32, name="first_own", offset=on_gated(1, 1))
+        first_own = arena.tile([P, 2, CHUNK], F32, name="first_own", offset=on_gated(2, 1))
         for k in range(2):
             nc.vector.tensor_tensor(first_own[:, k, :], y[2 + k][:].indirect(pos1_sb[:, own.start // 16 : own.stop // 16]), gate1_own[:], MULT)
         for k in range(2):
-            nc.vector.tensor_tensor(summed[OWN][:, 2 + k, :], first_own[:, k, :], second[:, 2 + k, own], ADD)
-        store(OWN, 1)
+            nc.vector.tensor_tensor(summed[:, 2 + k, own], first_own[:, k, :], second[:, 2 + k, own], ADD)
+        store(1, OWN, OWN)
 
         for i in range(3, len(UNITS)):
             for k in range(2):
@@ -317,16 +322,14 @@ def tile_moe_duo_gelu_kernel(
         for i in range(3, len(UNITS)):
             gate_and_add(i)
 
-        rounded1 = round_sum(1, on_gated(3, -1), [nc.scalar.copy])
-        rounded0 = round_sum(0, on_gated(3, 1), [nc.vector.tensor_copy, nc.scalar.copy])
-        rounded2 = round_sum(2, on_matrix(8), [nc.vector.tensor_copy, nc.scalar.copy])
-        codes01 = arena.tile([P, 2 * CHUNK], U32, name="codes01", align_bytes=64, offset=on_gated(4))
+        rounded1 = round_sum(1, on_gated(3, -1), 0)
+        rounded0 = round_sum(0, on_gated(3, 1), CHUNK // 2)
+        rounded2 = round_sum(2, on_matrix(8), 3 * CHUNK // 4)
+        codes = arena.tile([P, 2 * CHUNK], U32, name="codes01", align_bytes=64, offset=on_gated(4))
         codes2 = keep.tile([P, CHUNK], U32, name="codes2", align_bytes=64)
-        quantise_sum(codes01[:, CHUNK:], 1, rounded1)
-        quantise_sum(codes01[:, :CHUNK], 0, rounded0)
-        nc.sync.dma_start(out_words[:, : 2 * CHUNK], codes01[:].bitcast(I32))
-        quantise_sum(codes2[:], 2, rounded2)
-        nc.sync.dma_start(out_words[:, 2 * CHUNK :], codes2[:].bitcast(I32))
+        for c, words, tile in ((1, codes[:, CHUNK:], rounded1), (0, codes[:, :CHUNK], rounded0), (2, codes2[:], rounded2)):
+            quantise_sum(words, c, tile)
+            nc.sync.dma_start(out_words[:, c * CHUNK : (c + 1) * CHUNK], words.bitcast(I32))
         for r in range(4):
             queue = nc.scalar if r % 2 else nc.sync
             queue.dma_start(out_2[0].bitcast(I32)[r:16:4, :], o_scales[:].bitcast(I32)[r:P:32, :])

@@ -157,7 +157,7 @@ def tile_moe_duo_gelu_kernel(
                 scales = arena.tile([P, H], U8, name="scales%d" % m, align_bytes=64, offset=on_margin(m + 1))
             else:
                 scales = ring.tile([P, H], U8, name="scales", align_bytes=64, bufs=5)
-            cuts = {FIRST - 1: (0, 2 * P, H), MATRICES - 1: (0, P, 2 * P, H)}.get(m, (0, H))
+            cuts = {FIRST - 1: (0, 2 * P, H)}.get(m, (0, H))
             for c0, c1 in zip(cuts, cuts[1:]):
                 nc.vector.quantize_mx(codes[:, c0:c1].bitcast(FP8X4), scales[:, c0:c1], grouped[m][:, 4 * c0 : 4 * c1])
             quantised[m] = (codes, scales)
@@ -203,18 +203,31 @@ def tile_moe_duo_gelu_kernel(
         def last_two_experts():
             m, e = MATRICES - 1, E - 1
             codes, scales = quantised[m - 1]
-            product(e - 1, 0, codes[:, :P], scales[:, :P])
-            round_matrix(m)
-            late_scales = arena.tile([P, 2 * P], U8, name="late_scales", align_bytes=64, offset=on_margin(m))
-            nc.vector.quantize_mx(codes[:, 2 * P :].bitcast(FP8X4), late_scales[:], grouped[m - 1][:])
-            quantise_matrix(m)
-            codes, scales = quantised[m]
-            product(e, 0, codes[:, :P], scales[:, :P])
-            for t in range(1, HANDS):
+            for t in range(2):
+                product(e - 1, t, codes[:, t * P : (t + 1) * P], scales[:, t * P : (t + 1) * P])
+            late_codes = codes[:, 2 * P :]
+            src = raw[m].rearrange("p j (c t) -> p c j t", t=HANDS)
+            codes = ring.tile([P, H], U32, name="codes", align_bytes=64, bufs=6)
+            scales = ring.tile([P, H], U8, name="scales", align_bytes=64, bufs=5)
+            quantised[m] = (codes, scales)
+            front = arena.tile([P, 2 * H], BF16, name="front", align_bytes=64, offset=on_matrix(9))
+            rear = arena.tile([P, 2 * H], BF16, name="rear", align_bytes=64, offset=on_matrix(9) + 12 * H)
+            nc.vector.tensor_copy(front[:].rearrange("p (t c j) -> p c j t", t=2, j=4), src[:, :, :, :2])
+            dst = rear[:].rearrange("p (t c j) -> p c j t", t=2, j=4)
+            nc.vector.tensor_copy(dst[:, : P // 4], src[:, : P // 4, :, 2:])
+            nc.scalar.copy(dst[:, P // 4 :], src[:, P // 4 :, :, 2:])
+            for t in range(2):
+                nc.vector.quantize_mx(codes[:, t * P : (t + 1) * P].bitcast(FP8X4), scales[:, t * P : (t + 1) * P], front[:, t * H : (t + 1) * H])
+            late_scales = arena.tile([P, 2 * P], U8, name="late_scales", align_bytes=64, offset=on_matrix(9))
+            nc.vector.quantize_mx(late_codes.bitcast(FP8X4), late_scales[:], grouped[m - 1][:])
+            nc.vector.quantize_mx(codes[:, 2 * P :].bitcast(FP8X4), scales[:, 2 * P :], rear[:])
+            for t in range(2):
+                product(e, t, codes[:, t * P : (t + 1) * P], scales[:, t * P : (t + 1) * P])
+            for t in range(2, HANDS):
                 bank = psum.tile([P, 2, C], F32, name="bank_pair%d" % t, offset=(t - 1) * BANK)
                 for u in range(2):
                     codes, scales = quantised[m - 1 + u]
-                    scales = late_scales[:, (t - 2) * P : (t - 1) * P] if u == 0 and t >= 2 else scales[:, t * P : (t + 1) * P]
+                    scales = late_scales[:, (t - 2) * P : (t - 1) * P] if u == 0 else scales[:, t * P : (t + 1) * P]
                     nc.tensor.matmul_mx(
                         bank[:, u, :], lhsT=codes[:, t * P : (t + 1) * P].bitcast(FP8X4), lhsT_scale=scales,
                         rhs=h_codes[e - 1 + u][:].bitcast(FP8X4), rhs_scale=h_scales[e - 1 + u][:], start=True, stop=True,

from contextlib import ExitStack

import concourse.mybir as mybir
from concourse.masks import make_identity

K, T, E, C, H, N = 512, 768, 6, 256, 512, 512
S = E * C
P = 128
FLOPS = 2 * S * (2 * K * H + H * N)
BYTES = 3 * E * K * H * 4 + K * T + K * T // 32 + 2 * T * 4 + 2 * (S + T) * 16 + N * T * 5 + N * T // 32

F32 = mybir.dt.float32
BF16 = mybir.dt.bfloat16
I32 = mybir.dt.int32
U32 = mybir.dt.uint32
U16 = mybir.dt.uint16
U8 = mybir.dt.uint8
FP8X4 = mybir.dt.float8_e4m3fn_x4
MULT = mybir.AluOpType.mult
ADD = mybir.AluOpType.add
GELU = mybir.ActivationFunctionType.Gelu_apprx_tanh
COPY = mybir.ActivationFunctionType.Copy

HANDS = 4
WINDOW = 2048
FIRST = 2 * E
MATRICES = 3 * E
BANK = 2048

ROOMS = 10
MATRIX_BYTES = 4 * H * 4
MARGIN_BYTES = 1024
ROOM_BYTES = MATRIX_BYTES + 2 * MARGIN_BYTES

SCALAR_ALONE = 7
GELU_LAG = 3
HIDDEN_LAG = 6
HIDDEN_LAST = MATRICES - 4
CHUNK = 2 * P
BLOCKS = T // P
OWN = 1
UNITS = ((0, 0), (1, 0), (2, 0), (0, 1), (2, 1))


def tile_moe_duo_gelu_kernel(
    tc, x_words, x_scales, w1, wp, w2, gate, offs, pos1, pos2, offs2, out_0, out_1, out_2
):
    nc = tc.nc
    with ExitStack() as ctx:
        lists = ctx.enter_context(tc.tile_pool(name="lists", bufs=1))
        keep = ctx.enter_context(tc.tile_pool(name="keep", bufs=1))
        arena = ctx.enter_context(tc.tile_pool(name="arena", bufs=1))
        ring = ctx.enter_context(tc.tile_pool(name="ring", bufs=4))
        psum = ctx.enter_context(tc.psum_pool(name="psum", bufs=1))

        offs_sb = lists.tile([P, S // 16], U16, name="offs_sb")
        offs2_sb = lists.tile([P, S // 16], U16, name="offs2_sb")
        pos1_sb = lists.tile([P, T // 16], U16, name="pos1_sb")
        pos2_sb = lists.tile([P, T // 16], U16, name="pos2_sb")
        xw = keep.tile([P, WINDOW], I32, name="xw", align_bytes=64)
        xs = keep.tile([P, WINDOW], U8, name="xs", align_bytes=64)
        nc.gpsimd.memset(xs[:, :T].bitcast(I32), 0)
        nc.vector.memset(xs[:, T:].bitcast(I32), 0)
        nc.vector.memset(xw[:, T:], 0)
        for r in range(4):
            nc.scalar.dma_start(xs[:, :T].bitcast(I32)[r:P:32, :], x_scales[0].bitcast(I32)[r:16:4, :])
        zero = keep.tile([P, 1], F32, name="zero")[:]
        nc.vector.memset(zero, 0.0)
        bias0 = keep.tile([P, 1], F32, name="bias0")
        nc.scalar.activation(bias0[:], zero, GELU, bias=zero)
        ident = keep.tile([P, P], F32, name="ident")
        make_identity(nc, ident[:])

        nc.sync.dma_start(offs_sb[:], offs)
        nc.sync.dma_start(xw[:, :T], x_words[0].rearrange("p t d -> p (t d)").bitcast(I32))

        raw = {}

        def on_matrix(m):
            return (m % ROOMS) * ROOM_BYTES + MARGIN_BYTES

        def on_margin(m):
            return on_matrix(m) + (MATRIX_BYTES if m < ROOMS else -MARGIN_BYTES)

        def load(m):
            source = (w1, wp)[m % 2][m // 2] if m < FIRST else w2[m - FIRST]
            lead = 0 if m < ROOMS else MARGIN_BYTES
            tile = arena.tile([P, (MATRIX_BYTES + MARGIN_BYTES) // 4], F32, name="raw%d" % m, align_bytes=64, offset=on_matrix(m) - lead)
            raw[m] = tile[:, lead // 4 : lead // 4 + 4 * H].rearrange("p (j c) -> p j c", j=4)
            nc.sync.dma_start(raw[m], source.rearrange("(p j) c -> p j c", j=4))

        for m in range(ROOMS):
            load(m)
            if m == 1:
                nc.sync.dma_start(offs2_sb[:], offs2)

        gate1_rows = keep.tile([P, P], F32, name="gate1_rows")
        nc.gpsimd.memset(gate1_rows[:], 0.0)
        nc.sync.dma_start(gate1_rows[:BLOCKS, :], gate[0, 0:1, :].rearrange("o (b p) -> (o b) p", p=P))
        gate1_turned = psum.tile([P, P], F32, name="gate1_turned", offset=7 * BANK)
        nc.tensor.transpose(gate1_turned[:], gate1_rows[:], ident[:])
        gate1 = keep.tile([P, BLOCKS], F32, name="gate1")
        nc.scalar.copy(gate1[:], gate1_turned[:, :BLOCKS])

        gathered = [
            (keep.tile([P, S], U32, name="words%d" % which, align_bytes=64), keep.tile([P, S], U8, name="bytes%d" % which, align_bytes=64))
            for which in range(2)
        ]
        for which, lst in enumerate((offs_sb, offs2_sb)):
            for sort, table in ((1, xs[:]), (0, xw[:].bitcast(U32))):
                nc.vector.tensor_copy(gathered[which][sort][:], table.indirect(lst[:]))

        gate2 = keep.tile([P, T], F32, name="gate2")
        gate1_own = keep.tile([P, CHUNK], F32, name="gate1_own")
        grouped = {}
        quantised = {}
        hidden = {}
        h_codes = {}
        h_scales = {}

        def round_and_quantise_by_halves(m):
            src = raw[m].rearrange("p j (c t) -> p c j t", t=HANDS)
            halves = [arena.tile([P, 2 * H], BF16, name="half%d" % u, align_bytes=64, offset=on_matrix(9) + 4 * H + u * (4 * H - 64)) for u in range(2)]
            codes = ring.tile([P, H], U32, name="codes", align_bytes=64, bufs=6)
            scales = ring.tile([P, H], U8, name="scales", align_bytes=64, bufs=5)
            nc.vector.tensor_copy(halves[0][:].rearrange("p (t c j) -> p c j t", t=2, j=4), src[:, :, :, :2])
            nc.vector.quantize_mx(codes[:, : 2 * P].bitcast(FP8X4), scales[:, : 2 * P], halves[0][:])
            nc.vector.tensor_copy(halves[1][:].rearrange("p (t c j) -> p c j t", t=2, j=4), src[:, :, :, 2:])
            grouped[m] = halves[1]
            quantised[m] = (codes, scales)

        def round_matrix(m):
            if m == MATRICES - 2:
                round_and_quantise_by_halves(m)
                return
            grouped[m] = ring.tile([P, 4 * H], BF16, name="grouped", align_bytes=64, bufs=6)
            src = raw[m].rearrange("p j (c t) -> p c j t", t=HANDS)
            dst = grouped[m][:].rearrange("p (t c j) -> p c j t", t=HANDS, j=4)
            on_vector = 0 if m < SCALAR_ALONE else (HANDS // 2 if m % 2 else HANDS)
            if on_vector > 0:
                nc.vector.tensor_copy(dst[:, :, :, :on_vector], src[:, :, :, :on_vector])
            if on_vector < HANDS:
                nc.scalar.copy(dst[:, :, :, on_vector:], src[:, :, :, on_vector:])

        def load_after(m):
            if ROOMS <= m + ROOMS - 2 < MATRICES:
                load(m + ROOMS - 2)
            if m + ROOMS - 2 == MATRICES - 1:
                nc.sync.dma_start(pos2_sb[:], pos2)
                nc.sync.dma_start(gate2[:], gate[1])
                nc.sync.dma_start(pos1_sb[:], pos1)
                nc.sync.dma_start(gate1_own[:], gate[0, :, OWN * CHUNK : (OWN + 1) * CHUNK])

        def quantise_matrix(m):
            codes = ring.tile([P, H], U32, name="codes", align_bytes=64, bufs=6)
            if SCALAR_ALONE <= m < FIRST - 1 and m % 2:
                scales = arena.tile([P, H], U8, name="scales%d" % m, align_bytes=64, offset=on_margin(m + 1))
            else:
                scales = ring.tile([P, H], U8, name="scales", align_bytes=64, bufs=5)
            cuts = {FIRST - 1: (0, 2 * P, H)}.get(m, (0, H))
            for c0, c1 in zip(cuts, cuts[1:]):
                nc.vector.quantize_mx(codes[:, c0:c1].bitcast(FP8X4), scales[:, c0:c1], grouped[m][:, 4 * c0 : 4 * c1])
            quantised[m] = (codes, scales)

        def first_layer(e, offset):
            hidden[e] = arena.tile([P, C, HANDS], BF16, name="hidden%d" % e, align_bytes=64, offset=offset)
            banks = [psum.tile([P, HANDS, P], F32, name="bank_a%d_%d" % (e, half), offset=((2 * e + half) % 3) * BANK) for half in range(C // P)]
            for hands in ([(0, 1), (2, 3)] if e == E - 1 else [(0, 1, 2, 3)]):
                for half in range(C // P):
                    here = slice(e * C + half * P, e * C + (half + 1) * P)
                    for t in hands:
                        cols = slice(t * P, (t + 1) * P)
                        for which in range(2):
                            codes, scales = quantised[2 * e + which]
                            nc.tensor.matmul_mx(
                                banks[half][:, t, :], lhsT=codes[:, cols].bitcast(FP8X4), lhsT_scale=scales[:, cols],
                                rhs=gathered[which][0][:, here].bitcast(FP8X4), rhs_scale=gathered[which][1][:, here],
                                start=(which == 0), stop=(which == 1),
                            )
                    if hands[-1] == HANDS - 1:
                        nc.scalar.activation(hidden[e][:, half * P : (half + 1) * P, :], banks[half][:].rearrange("p t u -> p u t"), GELU, bias=bias0[:])

        def quantise_hidden(e, m):
            h_codes[e] = keep.tile([P, C], U32, name="h_codes%d" % e, align_bytes=64)
            h_scales[e] = arena.tile([P, C], U8, name="h_scales%d" % e, align_bytes=64, offset=on_margin(m) + H + e % 2 * C)
            nc.vector.quantize_mx(h_codes[e][:].bitcast(FP8X4), h_scales[e][:], hidden[e][:].rearrange("p u t -> p (u t)"))

        y = [keep.tile([P, S], F32, name="y%d" % t) for t in range(HANDS)]

        def product(e, t, codes, scales):
            bank = psum.tile([P, C], F32, name="bank_y%d_%d" % (e, t), offset=(3 + (HANDS * e + t) % 5) * BANK)
            nc.tensor.matmul_mx(
                bank[:], lhsT=codes.bitcast(FP8X4), lhsT_scale=scales,
                rhs=h_codes[e][:].bitcast(FP8X4), rhs_scale=h_scales[e][:], start=True, stop=True,
            )
            nc.scalar.copy(y[t][:, e * C : (e + 1) * C], bank[:])

        def second_layer(e):
            codes, scales = quantised[FIRST + e]
            for t in range(HANDS):
                product(e, t, codes[:, t * P : (t + 1) * P], scales[:, t * P : (t + 1) * P])

        def last_two_experts():
            m, e = MATRICES - 1, E - 1
            codes, scales = quantised[m - 1]
            for t in range(2):
                product(e - 1, t, codes[:, t * P : (t + 1) * P], scales[:, t * P : (t + 1) * P])
            late_codes = codes[:, 2 * P :]
            src = raw[m].rearrange("p j (c t) -> p c j t", t=HANDS)
            codes = ring.tile([P, H], U32, name="codes", align_bytes=64, bufs=6)
            scales = ring.tile([P, H], U8, name="scales", align_bytes=64, bufs=5)
            quantised[m] = (codes, scales)
            front = arena.tile([P, 2 * H], BF16, name="front", align_bytes=64, offset=on_matrix(9))
            rear = arena.tile([P, 2 * H], BF16, name="rear", align_bytes=64, offset=on_matrix(9) + 12 * H)
            nc.vector.tensor_copy(front[:].rearrange("p (t c j) -> p c j t", t=2, j=4), src[:, :, :, :2])
            dst = rear[:].rearrange("p (t c j) -> p c j t", t=2, j=4)
            nc.vector.tensor_copy(dst[:, : P // 4], src[:, : P // 4, :, 2:])
            nc.scalar.copy(dst[:, P // 4 :], src[:, P // 4 :, :, 2:])
            for t in range(2):
                nc.vector.quantize_mx(codes[:, t * P : (t + 1) * P].bitcast(FP8X4), scales[:, t * P : (t + 1) * P], front[:, t * H : (t + 1) * H])
            late_scales = arena.tile([P, 2 * P], U8, name="late_scales", align_bytes=64, offset=on_matrix(9))
            nc.vector.quantize_mx(late_codes.bitcast(FP8X4), late_scales[:], grouped[m - 1][:])
            nc.vector.quantize_mx(codes[:, 2 * P :].bitcast(FP8X4), scales[:, 2 * P :], rear[:])
            for t in range(2):
                product(e, t, codes[:, t * P : (t + 1) * P], scales[:, t * P : (t + 1) * P])
            for t in range(2, HANDS):
                bank = psum.tile([P, 2, C], F32, name="bank_pair%d" % t, offset=(t - 1) * BANK)
                for u in range(2):
                    codes, scales = quantised[m - 1 + u]
                    scales = late_scales[:, (t - 2) * P : (t - 1) * P] if u == 0 else scales[:, t * P : (t + 1) * P]
                    nc.tensor.matmul_mx(
                        bank[:, u, :], lhsT=codes[:, t * P : (t + 1) * P].bitcast(FP8X4), lhsT_scale=scales,
                        rhs=h_codes[e - 1 + u][:].bitcast(FP8X4), rhs_scale=h_scales[e - 1 + u][:], start=True, stop=True,
                    )
                nc.scalar.copy(y[t][:, (e - 1) * C :], bank[:].rearrange("p u c -> p (u c)"))

        for m in range(SCALAR_ALONE):
            round_matrix(m)
            load_after(m)
        for m in range(SCALAR_ALONE - 1):
            quantise_matrix(m)
        for m in range(SCALAR_ALONE, MATRICES - 1):
            if m == MATRICES - 2:
                quantise_matrix(m - 1)
                round_matrix(m)
            else:
                round_matrix(m)
                quantise_matrix(m - 1)
            for e in range(E):
                if m == SCALAR_ALONE and 2 * e + GELU_LAG < m:
                    first_layer(e, on_matrix(m - 1) + e * C * HANDS * 2)
                if 2 * e + GELU_LAG == m:
                    first_layer(e, on_matrix(m))
            for e in range(E):
                if min(max(2 * e + HIDDEN_LAG, SCALAR_ALONE + 1), HIDDEN_LAST) == m:
                    quantise_hidden(e, m)
            load_after(m)
            if m > FIRST:
                second_layer(m - 1 - FIRST)
        last_two_experts()

        out_rows = out_0.rearrange("(p t) n -> p t n", t=HANDS)
        out_words = out_1[0].rearrange("p n d -> p (n d)").bitcast(I32)
        o_scales = keep.tile([P, T], U8, name="o_scales", align_bytes=64)

        second = keep.tile([P, HANDS, T], F32, name="second")
        for t in range(HANDS):
            nc.vector.tensor_tensor(second[:, t, :], y[t][:].indirect(pos2_sb[:]), gate2[:], MULT)

        unit_bytes = 2 * CHUNK * 4
        summed = keep.tile([P, HANDS, T], F32, name="summed")
        there = {}

        def on_gated(i, side=0):
            return (3 * i + 1) * unit_bytes + side * (unit_bytes - 64)

        def fetch(i, k):
            c, pair = UNITS[i]
            place = (3 * k + i) * CHUNK * 4 if pair == 0 else (2 + (2 * i + k - 5) % 4) * CHUNK * 4 + 64
            tile = arena.tile([P, CHUNK], F32, name="first%d_%d" % (i, k), offset=on_matrix(8) + place)
            nc.scalar.activation(tile[:], y[2 * pair + k][:].indirect(pos1_sb[:, c * CHUNK // 16 : (c + 1) * CHUNK // 16]), COPY)
            if k == 0:
                there[i] = psum.tile([P, 2, 2, P], F32, name="there%d" % i, offset=(3 + i if i < 3 else i - 2) * BANK)
            for block in range(2):
                nc.tensor.transpose(there[i][:, block, k, :], tile[:, block * P : (block + 1) * P], ident[:])

        def store(pair, first_chunk, last_chunk):
            part = (slice(None), slice(2 * pair, 2 * pair + 2), slice(first_chunk * CHUNK, (last_chunk + 1) * CHUNK))
            nc.sync.dma_start(out_rows[part], summed[part])

        def gate_and_add(i):
            c, pair = UNITS[i]
            hands = slice(2 * pair, 2 * pair + 2)
            gated = arena.tile([P, 2, 2, P], F32, name="gated%d" % i, offset=on_gated(i))
            parts = ((0, 1),) if pair == 0 else ((0,), (1,))
            for blocks in parts:
                start, width = blocks[0] * P, len(blocks) * P
                back = psum.tile([P, 2, width], F32, name="back%d_%d" % (i, start), offset=((6 + i) % 8 if pair == 0 else i + 2 * blocks[0]) * BANK)
                for block in blocks:
                    nc.scalar.activation(gated[:, block], there[i][:, block], COPY, scale=gate1[:, 2 * c + block : 2 * c + block + 1])
                    for k in range(2):
                        nc.tensor.transpose(back[:, k, block * P - start : (block + 1) * P - start], gated[:, block, k, :], ident[:])
                tokens = slice(c * CHUNK + start, c * CHUNK + start + width)
                nc.vector.tensor_tensor(summed[:, hands, tokens], back[:], second[:, hands, tokens], ADD)
            if i >= 2:
                store(pair, 0 if pair == 0 else c, c)

        def round_sum(c, offset, on_vector):
            tile = arena.tile([P, CHUNK, HANDS], BF16, name="rounded%d" % c, align_bytes=64, offset=offset)
            for tokens, copy_on_engine in ((slice(0, on_vector), nc.vector.tensor_copy), (slice(on_vector, CHUNK), nc.scalar.copy)):
                if tokens.stop > tokens.start:
                    copy_on_engine(tile[:, tokens, :].rearrange("p (c i) t -> p c t i", i=4), summed[:, :, c * CHUNK + tokens.start : c * CHUNK + tokens.stop].rearrange("p t (c i) -> p c t i", i=4))
            return tile

        def quantise_sum(codes, c, tile):
            nc.vector.quantize_mx(codes.bitcast(FP8X4), o_scales[:, c * CHUNK : (c + 1) * CHUNK], tile[:].rearrange("p n t -> p (n t)"))

        for k in range(2):
            for i in range(3):
                fetch(i, k)
        for i in range(3):
            gate_and_add(i)

        own = slice(OWN * CHUNK, (OWN + 1) * CHUNK)
        first_own = arena.tile([P, 2, CHUNK], F32, name="first_own", offset=on_gated(2, 1))
        for k in range(2):
            nc.vector.tensor_tensor(first_own[:, k, :], y[2 + k][:].indirect(pos1_sb[:, own.start // 16 : own.stop // 16]), gate1_own[:], MULT)
        for k in range(2):
            nc.vector.tensor_tensor(summed[:, 2 + k, own], first_own[:, k, :], second[:, 2 + k, own], ADD)
        store(1, OWN, OWN)

        for i in range(3, len(UNITS)):
            for k in range(2):
                fetch(i, k)
        for i in range(3, len(UNITS)):
            gate_and_add(i)

        rounded1 = round_sum(1, on_gated(3, -1), 0)
        rounded0 = round_sum(0, on_gated(3, 1), CHUNK // 2)
        rounded2 = round_sum(2, on_matrix(8), 3 * CHUNK // 4)
        codes = arena.tile([P, 2 * CHUNK], U32, name="codes01", align_bytes=64, offset=on_gated(4))
        codes2 = keep.tile([P, CHUNK], U32, name="codes2", align_bytes=64)
        for c, words, tile in ((1, codes[:, CHUNK:], rounded1), (0, codes[:, :CHUNK], rounded0), (2, codes2[:], rounded2)):
            quantise_sum(words, c, tile)
            nc.sync.dma_start(out_words[:, c * CHUNK : (c + 1) * CHUNK], words.bitcast(I32))
        for r in range(4):
            queue = nc.scalar if r % 2 else nc.sync
            queue.dma_start(out_2[0].bitcast(I32)[r:16:4, :], o_scales[:].bitcast(I32)[r:P:32, :])
